import numpy as np
import ml_dtypes


def mxq(x, axis, fmt="e4m3"):
    dtype, down = {"e4m3": (ml_dtypes.float8_e4m3fn, 7), "e5m2": (ml_dtypes.float8_e5m2, 14)}[fmt]
    v = np.moveaxis(np.asarray(x, np.float32).astype(ml_dtypes.bfloat16).astype(np.float64), axis, -1)
    blocks = v.reshape(v.shape[:-1] + (-1, 32))
    amax = np.abs(blocks).max(-1, keepdims=True)
    byte = np.maximum(np.where(amax > 0, np.frexp(amax)[1] - 1 + 127, 0) - down, 1)
    scale = np.exp2(byte - 127.0)
    codes = (blocks / scale).astype(np.float32).astype(dtype).astype(np.float64)
    return np.moveaxis((codes * scale).reshape(v.shape), -1, axis)


WIDE = False


def mx_kscale(k):
    if not WIDE:
        return np.ones(k)
    levels = np.array([10, -10, 5, -5, 0])
    if k % 512:
        return np.exp2(np.random.permutation(np.resize(levels, k // 32))).repeat(32)
    a = np.empty((k // 512, 16))
    for p in range(k // 512):
        a[p, :8] = np.random.permutation(np.resize(levels, 8))
        for g in range(8):
            far = levels[np.abs(levels - a[p, g]) >= 10]
            a[p, g + 8] = far[np.random.randint(len(far))]
    return np.exp2(a.ravel()).repeat(32)


def f64(x):
    return np.asarray(x).astype(np.float64)


def striped(idx):
    return np.tile(idx.reshape(-1, 16).T, (8, 1)).astype(np.uint16)


def unstriped(offs):
    return offs[:16].T.reshape(-1).astype(np.int64)


E2M1 = np.array([0.0, 0.5, 1.0, 1.5, 2.0, 3.0, 4.0, 6.0, -0.0, -0.5, -1.0, -1.5, -2.0, -3.0, -4.0, -6.0])


def pack_weight(w, fmt):
    k, n = w.shape
    w = f64(np.asarray(w, np.float32).astype(ml_dtypes.bfloat16)).reshape(k // 32, 32, n)
    amax = np.abs(w).max(1)
    if fmt == "e4m3":
        byte = np.frexp(amax)[1] - 1 + 127 - 7
    else:
        mant, ex = np.frexp(amax / 6.0)
        byte = np.where(mant > 0.5, ex, ex - 1) + 127
    byte = np.clip(np.where(amax > 0, byte, 1), 1, 254)
    scaled = (w * np.exp2(127.0 - byte)[:, None, :]).reshape(k, n).astype(np.float32)
    by_word = np.ascontiguousarray(scaled.reshape(k // 512, 128, 4, n).transpose(0, 1, 3, 2))
    if fmt == "e4m3":
        words = by_word.astype(ml_dtypes.float8_e4m3fn).view(np.uint8)
    else:
        c = by_word.astype(ml_dtypes.float4_e2m1fn).view(np.uint8) & 0xF
        words = (c[..., 0::2] | (c[..., 1::2] << 4)).reshape(k // 512, 128, 2 * n)
    return np.ascontiguousarray(words), np.ascontiguousarray(byte.astype(np.uint8).reshape(k // 512, 16, n))


def unpack_weight(words, scales, fmt):
    g, _, n = scales.shape
    words = np.ascontiguousarray(words).reshape(g, 128, n, -1)
    if fmt == "e4m3":
        vals = words.view(ml_dtypes.float8_e4m3fn).astype(np.float64)
    else:
        nib = np.empty((g, 128, n, 4), np.uint8)
        nib[..., 0::2] = words & 0xF
        nib[..., 1::2] = words >> 4
        vals = E2M1[nib]
    vals = vals * np.repeat(np.exp2(scales.astype(np.float64) - 127.0), 8, axis=1)[..., None]
    return vals.transpose(0, 1, 3, 2).reshape(g * 512, n)


def gelu(v):
    return 0.5 * v * (1.0 + np.tanh(np.sqrt(2.0 / np.pi) * (v + 0.044715 * v**3)))


K, T, S, H, N = 1536, 4096, 1024, 512, 384

def setup_inputs():
    n = np.random.standard_normal
    s = mx_kscale(K)[:, None]
    u = mx_kscale(H)[:, None]
    inputs = {}
    inputs["tab_words"], inputs["tab_scales"] = pack_weight(n((K, T)) * s, "e4m3")
    inputs["offs"] = striped(np.random.permutation(T)[:S])
    inputs["wt"] = (n((K, H)) / np.sqrt(K) / s).astype(np.float32)
    inputs["wg_words"], inputs["wg_scales"] = pack_weight(1.5 * n((K, H)) / np.sqrt(K) / s, "e2m1")
    inputs["gt"] = (np.exp(0.3 * n(H)) * u[:, 0]).astype(np.float32)
    inputs["gs"] = (np.exp(0.3 * n(H)) * u[:, 0]).astype(np.float32)
    inputs["wp_words"], inputs["wp_scales"] = pack_weight(1.5 * n((H, N)) / np.sqrt(H) / u, "e4m3")
    inputs["wq"] = (1.5 * n((H, N)) / np.sqrt(H) / u).astype(np.float32)
    return inputs

def reference(tab_words, tab_scales, offs, wt, wg_words, wg_scales, gt, gs, wp_words, wp_scales, wq):
    v = unpack_weight(tab_words, tab_scales, "e4m3")[:, unstriped(offs)]
    wtq = mxq(f64(wt), 0, "e4m3")
    wg = unpack_weight(wg_words, wg_scales, "e2m1")
    wp = unpack_weight(wp_words, wp_scales, "e4m3")
    wqq = mxq(f64(wq), 0, "e4m3")
    a = f64(gt)[:, None] * np.tanh(wtq.T @ v)
    b = f64(gs)[:, None] * (1.0 / (1.0 + np.exp(-(wg.T @ v))))
    value = wp.T @ mxq(a, 0, "e4m3")
    response = wqq.T @ mxq(b, 0, "e4m3")
    return value * response

@@ -1,0 +1,284 @@
+from contextlib import ExitStack
+
+import concourse.mybir as mybir
+
+K, T, S, H, N = 1536, 4096, 1024, 512, 384
+FLOPS = 2 * 2 * K * H * S + 2 * 2 * H * N * S
+
+F32 = mybir.dt.float32
+BF16 = mybir.dt.bfloat16
+I32 = mybir.dt.int32
+U32 = mybir.dt.uint32
+U16 = mybir.dt.uint16
+U8 = mybir.dt.uint8
+FP8X4 = mybir.dt.float8_e4m3fn_x4
+FP4X4 = mybir.dt.float4_e2m1fn_x4
+ACT = mybir.ActivationFunctionType
+MULT = mybir.AluOpType.mult
+
+P = 128
+PACK = 4
+PASSES = K // (P * PACK)
+HALF = 512
+HALVES = S // HALF
+SLOT_TILES = N // P
+SHIFT_ROWS = 112
+
+
+def tile_list_campaign_branch_bids_kernel(
+    tc, tab_words, tab_scales, offs, wt, wg_words, wg_scales, gt, gs, wp_words, wp_scales, wq, out
+):
+    nc = tc.nc
+    with ExitStack() as ctx:
+        keep = ctx.enter_context(tc.tile_pool(name="keep", bufs=1))
+        rooms = ctx.enter_context(tc.tile_pool(name="rooms", bufs=1))
+        psum = ctx.enter_context(tc.psum_pool(name="psum", bufs=8))
+
+        def held(shape, dtype, name, tag=""):
+            return keep.tile(shape, dtype, name=name, tag=tag or name, align_bytes=64)
+
+        def placed(shape, dtype, name, kib):
+            return rooms.tile(shape, dtype, name=name, align_bytes=64, offset=int(kib * 1024))
+
+        offsets = keep.tile([P, S // 16], U16, name="offsets")
+        table = {}
+        table_scales = placed([P, T // 4], I32, "table_scales", 14)
+        wg_raw = placed([P, PASSES, H // 2], I32, "wg_raw", 20)
+        wg_scales_raw = held([P, PASSES, H // 4], I32, "wg_scales_raw", "room_e")
+        wp_plane = held([P, N // 4], I32, "wp_plane")
+        moved = [held([P, S // 4], I32, "moved%d" % a) for a in range(1, PASSES)]
+
+        nc.vector.memset(table_scales[:], 0)
+        nc.vector.memset(wg_scales_raw[:], 0)
+        nc.vector.memset(wp_plane[:], 0)
+        for plane in moved:
+            nc.vector.memset(plane[:], 0)
+
+        def load_table(a, kib):
+            table[a] = placed([P, T], I32, "table%d" % a, kib)
+            nc.sync.dma_start(out=table[a][:], in_=tab_words[a].rearrange("p t i -> p (t i)").bitcast(I32))
+
+        nc.sync.dma_start(offsets[:], offs)
+        nc.sync.dma_start(out=wg_raw[:], in_=wg_words.rearrange("a p c -> p a c").bitcast(I32))
+        load_table(0, 44)
+        for q in range(4):
+            nc.scalar.dma_start(
+                out=wg_scales_raw[32 * q : 32 * q + 4, :, :],
+                in_=wg_scales[:, 4 * q : 4 * q + 4, :].rearrange("a r c -> r a c").bitcast(I32),
+            )
+
+        for q in range(4):
+            nc.gpsimd.dma_start(
+                out=table_scales[32 * q : 32 * q + 4 * PASSES, :],
+                in_=tab_scales[:, 4 * q : 4 * q + 4, :].bitcast(I32),
+            )
+        for q in range(4):
+            nc.scalar.dma_start(
+                out=wp_plane[32 * q : 32 * q + 4, :],
+                in_=wp_scales[0, 4 * q : 4 * q + 4, :].bitcast(I32),
+            )
+
+        wg_codes = held([P, PASSES, 2 * H], U8, "wg_codes")
+        wg_plane = held([P, PASSES, H], U8, "wg_plane")
+        nc.vector.tensor_copy(
+            out=wg_codes[:].bitcast(U16).rearrange("p a (t m) -> p a t m", t=PACK),
+            in_=wg_raw[:].bitcast(U16).rearrange("p a (m t) -> p a t m", t=PACK),
+        )
+        load_table(1, 20)
+        nc.vector.tensor_copy(
+            out=wg_plane[:].rearrange("p a (t m) -> p a t m", t=PACK),
+            in_=wg_scales_raw[:].bitcast(U8).rearrange("p a (m t) -> p a t m", t=PACK),
+        )
+        gains = held([P, 2, 2 * PACK], F32, "gains", "room_e")
+        gs_sb = gains[:, 0, 0:PACK]
+        gt_sb = gains[:, 1, 0:PACK]
+        nc.scalar.dma_start(out=gs_sb, in_=gs.rearrange("(p t) -> p t", t=PACK))
+        nc.scalar.dma_start(out=gt_sb, in_=gt.rearrange("(p t) -> p t", t=PACK))
+
+        picked_scales = held([P, S], U8, "picked_scales")
+        nc.vector.tensor_copy(picked_scales[:], table_scales[:].bitcast(U8).indirect(offsets[:]))
+        for a in range(1, PASSES):
+            nc.scalar.dma_start(
+                out=moved[a - 1][0:SHIFT_ROWS, :],
+                in_=picked_scales[4 * a : 4 * a + SHIFT_ROWS, :].bitcast(I32),
+            )
+        v_planes = [picked_scales[:]] + [plane[:].bitcast(U8) for plane in moved]
+
+        v_codes = {}
+
+        def gather_whole(a, picked):
+            nc.vector.tensor_copy(picked[:], table[a][:].bitcast(U32).indirect(offsets[:]))
+            for h in range(HALVES):
+                v_codes[a, h] = picked[:, h * HALF : (h + 1) * HALF]
+
+        def gather_half(a, h):
+            picked = held([P, HALF], U32, "picked%d_%d" % (a, h))
+            cols = HALF // 16
+            nc.vector.tensor_copy(picked[:], table[a][:].bitcast(U32).indirect(offsets[:, h * cols : (h + 1) * cols]))
+            v_codes[a, h] = picked[:]
+
+        load_table(2, 0)
+        gather_whole(0, placed([P, S], U32, "picked0", 16))
+        gather_whole(1, held([P, S], U32, "picked1"))
+        wt_raw = placed([P, PASSES, PACK, H], F32, "wt_raw", 20)
+        for a in range(PASSES):
+            rows = wt[a * P * PACK : (a + 1) * P * PACK, :]
+            nc.sync.dma_start(out=wt_raw[:, a, :, :], in_=rows.rearrange("(p j) c -> p j c", j=PACK))
+
+        banks = {}
+
+        def first_layer(branch, h, a):
+            for t in range(PACK):
+                if a == 0:
+                    banks[branch, h, t] = psum.tile([P, HALF], F32, name="bank")
+                if branch == "sigmoid":
+                    lhsT = wg_codes[:, a, 2 * P * t : 2 * P * (t + 1)].bitcast(FP4X4)
+                    lhsT_scale = wg_plane[:, a, P * t : P * (t + 1)]
+                else:
+                    lhsT = wt_codes[a][:, P * t : P * (t + 1)].bitcast(FP8X4)
+                    lhsT_scale = wt_plane[a][:, P * t : P * (t + 1)]
+                nc.tensor.matmul_mx(
+                    out=banks[branch, h, t][:],
+                    lhsT=lhsT,
+                    lhsT_scale=lhsT_scale,
+                    rhs=v_codes[a, h].bitcast(FP8X4),
+                    rhs_scale=v_planes[a][:, h * HALF : (h + 1) * HALF],
+                    start=(a == 0),
+                    stop=(a == PASSES - 1),
+                )
+
+        acts = {}
+
+        def activate(branch, h):
+            func = ACT.Sigmoid if branch == "sigmoid" else ACT.Tanh
+            acts[branch, h] = held([P, PACK, HALF], F32, "act_%s%d" % (branch, h))
+            for t in range(PACK):
+                nc.scalar.activation(out=acts[branch, h][:, t, :], in_=banks[branch, h, t][:], func=func)
+
+        hidden = {}
+
+        def apply_gain(branch, h):
+            gain = gs_sb if branch == "sigmoid" else gt_sb
+            hidden[branch, h] = held([P, HALF * PACK], BF16, "hidden_%s%d" % (branch, h))
+            nc.vector.tensor_tensor(
+                out=hidden[branch, h][:].rearrange("p (c i t) -> p c t i", i=2, t=PACK),
+                in0=acts[branch, h][:].rearrange("p t (c i) -> p c t i", i=2),
+                in1=gain.unsqueeze(1).unsqueeze(3).to_broadcast([P, HALF // 2, PACK, 2]),
+                op=MULT,
+            )
+
+        hidden_codes = {}
+        hidden_plane = {}
+
+        def quantise_hidden(branch, h):
+            hidden_codes[branch, h] = held([P, HALF], U32, "hidden_codes_%s%d" % (branch, h))
+            hidden_plane[branch, h] = held([P, HALF], U8, "hidden_plane_%s%d" % (branch, h))
+            nc.vector.quantize_mx(
+                out=hidden_codes[branch, h][:].bitcast(FP8X4),
+                scales=hidden_plane[branch, h][:],
+                in_=hidden[branch, h][:],
+            )
+
+        wt_grouped = [held([P, H * PACK], BF16, "wt_grouped%d" % a) for a in range(PASSES)]
+        wt_codes = [held([P, H], U32, "wt_codes%d" % a) for a in range(PASSES)]
+        wt_plane = [held([P, H], U8, "wt_plane%d" % a) for a in range(PASSES)]
+
+        def round_wt(a, on_vector):
+            dst = wt_grouped[a][:].rearrange("p (t m j) -> p m j t", t=PACK, j=PACK)
+            src = wt_raw[:, a, :, :].rearrange("p j (m t) -> p m j t", t=PACK)
+            if on_vector:
+                nc.vector.tensor_copy(out=dst, in_=src)
+            else:
+                nc.scalar.copy(out=dst, in_=src)
+
+        def quantise_wt(a):
+            nc.vector.quantize_mx(out=wt_codes[a][:].bitcast(FP8X4), scales=wt_plane[a][:], in_=wt_grouped[a][:])
+
+        wq_grouped = held([P, N * PACK], BF16, "wq_grouped")
+        wq_codes = held([P, N], U32, "wq_codes")
+        wq_plane = held([P, N], U8, "wq_plane")
+
+        def second_layer(branch, h):
+            for n in range(SLOT_TILES):
+                cols = slice(P * n, P * (n + 1))
+                banks[branch, h, "slots", n] = psum.tile([P, HALF], F32, name="bank")
+                if branch == "sigmoid":
+                    lhsT, lhsT_scale = wq_codes[:, cols], wq_plane[:, cols]
+                else:
+                    lhsT, lhsT_scale = wp_codes[:, cols], wp_plane[:].bitcast(U8)[:, cols]
+                nc.tensor.matmul_mx(
+                    out=banks[branch, h, "slots", n][:],
+                    lhsT=lhsT.bitcast(FP8X4),
+                    lhsT_scale=lhsT_scale,
+                    rhs=hidden_codes[branch, h][:].bitcast(FP8X4),
+                    rhs_scale=hidden_plane[branch, h][:],
+                    start=True,
+                    stop=True,
+                )
+
+        response = {}
+
+        def keep_response(h):
+            for n in range(SLOT_TILES):
+                response[h, n] = held([P, HALF], F32, "response%d_%d" % (h, n))
+                nc.scalar.copy(out=response[h, n][:], in_=banks["sigmoid", h, "slots", n][:])
+
+        def multiply_and_store(h):
+            for n in range(SLOT_TILES):
+                bids = held([P, HALF], F32, "bids%d_%d" % (h, n))
+                nc.vector.tensor_tensor(
+                    out=bids[:], in0=banks["tanh", h, "slots", n][:], in1=response[h, n][:], op=MULT
+                )
+                nc.sync.dma_start(out=out[P * n : P * (n + 1), h * HALF : (h + 1) * HALF], in_=bids[:])
+
+        for a in range(PASSES - 1):
+            for h in range(HALVES):
+                first_layer("sigmoid", h, a)
+        for h in range(HALVES):
+            gather_half(PASSES - 1, h)
+            first_layer("sigmoid", h, PASSES - 1)
+        wq_raw = placed([P, PACK, N], F32, "wq_raw", 0)
+        nc.sync.dma_start(out=wq_raw[:], in_=wq.rearrange("(p j) c -> p j c", j=PACK))
+        wp_codes = placed([P, N], I32, "wp_codes", 6)
+        nc.sync.dma_start(out=wp_codes[:], in_=wp_words[0].rearrange("p c i -> p (c i)").bitcast(I32))
+        activate("sigmoid", 0)
+        round_wt(0, True)
+        activate("sigmoid", 1)
+        quantise_wt(0)
+        apply_gain("sigmoid", 0)
+        first_layer("tanh", 0, 0)
+        round_wt(1, False)
+        round_wt(2, True)
+        quantise_hidden("sigmoid", 0)
+        quantise_wt(1)
+        quantise_wt(2)
+        first_layer("tanh", 0, 1)
+        first_layer("tanh", 0, 2)
+        nc.scalar.copy(
+            out=wq_grouped[:].rearrange("p (c i j) -> p c j i", i=2, j=PACK),
+            in_=wq_raw[:].rearrange("p j (c i) -> p c j i", i=2),
+        )
+        for a in range(PASSES):
+            first_layer("tanh", 1, a)
+        apply_gain("sigmoid", 1)
+        activate("tanh", 0)
+        for lo, hi in ((0, 256), (256, N)):
+            nc.vector.quantize_mx(
+                out=wq_codes[:, lo:hi].bitcast(FP8X4),
+                scales=wq_plane[:, lo:hi],
+                in_=wq_grouped[:, PACK * lo : PACK * hi],
+            )
+        quantise_hidden("sigmoid", 1)
+        activate("tanh", 1)
+        second_layer("sigmoid", 0)
+        apply_gain("tanh", 0)
+        second_layer("sigmoid", 1)
+        keep_response(0)
+        quantise_hidden("tanh", 0)
+        apply_gain("tanh", 1)
+        second_layer("tanh", 0)
+        keep_response(1)
+        quantise_hidden("tanh", 1)
+        multiply_and_store(0)
+        second_layer("tanh", 1)
+        multiply_and_store(1)

@@ -73,7 +73,7 @@ def tile_list_campaign_branch_bids_kernel(
                 in_=tab_scales[:, 4 * q : 4 * q + 4, :].bitcast(I32),
             )
         for q in range(4):
-            nc.scalar.dma_start(
+            nc.gpsimd.dma_start(
                 out=wp_plane[32 * q : 32 * q + 4, :],
                 in_=wp_scales[0, 4 * q : 4 * q + 4, :].bitcast(I32),
             )
@@ -161,9 +161,9 @@ def tile_list_campaign_branch_bids_kernel(
             gain = gs_sb if branch == "sigmoid" else gt_sb
             hidden[branch, h] = held([P, HALF * PACK], BF16, "hidden_%s%d" % (branch, h))
             nc.vector.tensor_tensor(
-                out=hidden[branch, h][:].rearrange("p (c i t) -> p c t i", i=2, t=PACK),
-                in0=acts[branch, h][:].rearrange("p t (c i) -> p c t i", i=2),
-                in1=gain.unsqueeze(1).unsqueeze(3).to_broadcast([P, HALF // 2, PACK, 2]),
+                out=hidden[branch, h][:].rearrange("p (c i t) -> p c t i", i=4, t=PACK),
+                in0=acts[branch, h][:].rearrange("p t (c i) -> p c t i", i=4),
+                in1=gain.unsqueeze(1).unsqueeze(3).to_broadcast([P, HALF // 4, PACK, 4]),
                 op=MULT,
             )
 
@@ -184,12 +184,13 @@ def tile_list_campaign_branch_bids_kernel(
         wt_plane = [held([P, H], U8, "wt_plane%d" % a) for a in range(PASSES)]
 
         def round_wt(a, on_vector):
-            dst = wt_grouped[a][:].rearrange("p (t m j) -> p m j t", t=PACK, j=PACK)
-            src = wt_raw[:, a, :, :].rearrange("p j (m t) -> p m j t", t=PACK)
+            dst = wt_grouped[a][:].rearrange("p (u e m j) -> p u m j e", u=2, e=2, j=PACK)
+            src = wt_raw[:, a, :, :].rearrange("p j (m u e) -> p u m j e", u=2, e=2)
             if on_vector:
                 nc.vector.tensor_copy(out=dst, in_=src)
             else:
-                nc.scalar.copy(out=dst, in_=src)
+                for u in range(2):
+                    nc.scalar.copy(out=dst[:, u, :, :, :], in_=src[:, u, :, :, :])
 
         def quantise_wt(a):
             nc.vector.quantize_mx(out=wt_codes[a][:].bitcast(FP8X4), scales=wt_plane[a][:], in_=wt_grouped[a][:])
@@ -245,21 +246,22 @@ def tile_list_campaign_branch_bids_kernel(
         round_wt(0, True)
         activate("sigmoid", 1)
         quantise_wt(0)
-        apply_gain("sigmoid", 0)
+        round_wt(1, True)
         first_layer("tanh", 0, 0)
-        round_wt(1, False)
-        round_wt(2, True)
-        quantise_hidden("sigmoid", 0)
+        first_layer("tanh", 1, 0)
         quantise_wt(1)
-        quantise_wt(2)
+        round_wt(2, False)
         first_layer("tanh", 0, 1)
+        first_layer("tanh", 1, 1)
+        apply_gain("sigmoid", 0)
+        quantise_wt(2)
         first_layer("tanh", 0, 2)
+        first_layer("tanh", 1, 2)
+        quantise_hidden("sigmoid", 0)
         nc.scalar.copy(
-            out=wq_grouped[:].rearrange("p (c i j) -> p c j i", i=2, j=PACK),
-            in_=wq_raw[:].rearrange("p j (c i) -> p c j i", i=2),
+            out=wq_grouped[:].rearrange("p (c i j) -> p c j i", i=4, j=PACK),
+            in_=wq_raw[:].rearrange("p j (c i) -> p c j i", i=4),
         )
-        for a in range(PASSES):
-            first_layer("tanh", 1, a)
         apply_gain("sigmoid", 1)
         activate("tanh", 0)
         for lo, hi in ((0, 256), (256, N)):

@@ -42,41 +42,59 @@ def tile_list_campaign_branch_bids_kernel(
 
         offsets = keep.tile([P, S // 16], U16, name="offsets")
         table = {}
-        table_scales = placed([P, T // 4], I32, "table_scales", 14)
-        wg_raw = placed([P, PASSES, H // 2], I32, "wg_raw", 20)
-        wg_scales_raw = held([P, PASSES, H // 4], I32, "wg_scales_raw", "room_e")
-        wp_plane = held([P, N // 4], I32, "wp_plane")
-        moved = [held([P, S // 4], I32, "moved%d" % a) for a in range(1, PASSES)]
+        table_scales = placed([P, T // 4], I32, "table_scales", 15)
+        wg_raw = held([P, PASSES, H // 2], I32, "wg_raw")
+        wg_scales_raw = held([P, PASSES, H // 4], I32, "wg_scales_raw")
+        v_plane_words = held([P, PASSES, S // 4], I32, "v_plane_words")
 
-        nc.vector.memset(table_scales[:], 0)
         nc.vector.memset(wg_scales_raw[:], 0)
-        nc.vector.memset(wp_plane[:], 0)
-        for plane in moved:
-            nc.vector.memset(plane[:], 0)
+        for lo, hi in ((0, 16), (32, 64), (64, 96)):
+            nc.vector.memset(table_scales[lo:hi, :], 0)
+        nc.vector.memset(v_plane_words[:], 0)
 
         def load_table(a, kib):
             table[a] = placed([P, T], I32, "table%d" % a, kib)
             nc.sync.dma_start(out=table[a][:], in_=tab_words[a].rearrange("p t i -> p (t i)").bitcast(I32))
 
         nc.sync.dma_start(offsets[:], offs)
+        scale_rows = tab_scales.rearrange("a q t -> (a q) t").bitcast(I32)
+        nc.sync.dma_start(out=table_scales[16:32, :], in_=scale_rows[0:16, :])
+        nc.sync.dma_start(out=table_scales[96:128, :], in_=scale_rows[16:48, :])
+        first_row = (16, 96, 112)
         nc.sync.dma_start(out=wg_raw[:], in_=wg_words.rearrange("a p c -> p a c").bitcast(I32))
-        load_table(0, 44)
+        load_table(0, 58)
         for q in range(4):
-            nc.scalar.dma_start(
+            nc.sync.dma_start(
                 out=wg_scales_raw[32 * q : 32 * q + 4, :, :],
                 in_=wg_scales[:, 4 * q : 4 * q + 4, :].rearrange("a r c -> r a c").bitcast(I32),
             )
 
-        for q in range(4):
-            nc.gpsimd.dma_start(
-                out=table_scales[32 * q : 32 * q + 4 * PASSES, :],
-                in_=tab_scales[:, 4 * q : 4 * q + 4, :].bitcast(I32),
+        picked_scales = held([P, S], U8, "picked_scales")
+        nc.vector.tensor_copy(picked_scales[:], table_scales[:].bitcast(U8).indirect(offsets[:]))
+
+        def move_scale_rows(a, q):
+            row = first_row[a] + 4 * q
+            nc.sync.dma_start(
+                out=v_plane_words[32 * q : 32 * q + 4, a, :],
+                in_=picked_scales[row : row + 4, :].bitcast(I32),
             )
+
+        move_scale_rows(0, 0)
+        move_scale_rows(0, 1)
+        load_table(1, 0)
+        move_scale_rows(0, 2)
+        move_scale_rows(0, 3)
         for q in range(4):
-            nc.gpsimd.dma_start(
-                out=wp_plane[32 * q : 32 * q + 4, :],
-                in_=wp_scales[0, 4 * q : 4 * q + 4, :].bitcast(I32),
-            )
+            move_scale_rows(1, q)
+        load_table(2, 18)
+        for q in range(4):
+            move_scale_rows(2, q)
+        gains = placed([P, 2, 2 * PACK], F32, "gains", 16)
+        gs_sb = gains[:, 0, 0:PACK]
+        gt_sb = gains[:, 1, 0:PACK]
+        nc.sync.dma_start(out=gs_sb, in_=gs.rearrange("(p t) -> p t", t=PACK))
+        nc.sync.dma_start(out=gt_sb, in_=gt.rearrange("(p t) -> p t", t=PACK))
+        v_planes = [v_plane_words[:, a, :].bitcast(U8) for a in range(PASSES)]
 
         wg_codes = held([P, PASSES, 2 * H], U8, "wg_codes")
         wg_plane = held([P, PASSES, H], U8, "wg_plane")
@@ -84,29 +102,15 @@ def tile_list_campaign_branch_bids_kernel(
             out=wg_codes[:].bitcast(U16).rearrange("p a (t m) -> p a t m", t=PACK),
             in_=wg_raw[:].bitcast(U16).rearrange("p a (m t) -> p a t m", t=PACK),
         )
-        load_table(1, 20)
         nc.vector.tensor_copy(
             out=wg_plane[:].rearrange("p a (t m) -> p a t m", t=PACK),
             in_=wg_scales_raw[:].bitcast(U8).rearrange("p a (m t) -> p a t m", t=PACK),
         )
-        gains = held([P, 2, 2 * PACK], F32, "gains", "room_e")
-        gs_sb = gains[:, 0, 0:PACK]
-        gt_sb = gains[:, 1, 0:PACK]
-        nc.scalar.dma_start(out=gs_sb, in_=gs.rearrange("(p t) -> p t", t=PACK))
-        nc.scalar.dma_start(out=gt_sb, in_=gt.rearrange("(p t) -> p t", t=PACK))
-
-        picked_scales = held([P, S], U8, "picked_scales")
-        nc.vector.tensor_copy(picked_scales[:], table_scales[:].bitcast(U8).indirect(offsets[:]))
-        for a in range(1, PASSES):
-            nc.scalar.dma_start(
-                out=moved[a - 1][0:SHIFT_ROWS, :],
-                in_=picked_scales[4 * a : 4 * a + SHIFT_ROWS, :].bitcast(I32),
-            )
-        v_planes = [picked_scales[:]] + [plane[:].bitcast(U8) for plane in moved]
 
         v_codes = {}
 
-        def gather_whole(a, picked):
+        def gather_whole(a):
+            picked = held([P, S], U32, "picked%d" % a)
             nc.vector.tensor_copy(picked[:], table[a][:].bitcast(U32).indirect(offsets[:]))
             for h in range(HALVES):
                 v_codes[a, h] = picked[:, h * HALF : (h + 1) * HALF]
@@ -117,13 +121,23 @@ def tile_list_campaign_branch_bids_kernel(
             nc.vector.tensor_copy(picked[:], table[a][:].bitcast(U32).indirect(offsets[:, h * cols : (h + 1) * cols]))
             v_codes[a, h] = picked[:]
 
-        load_table(2, 0)
-        gather_whole(0, placed([P, S], U32, "picked0", 16))
-        gather_whole(1, held([P, S], U32, "picked1"))
-        wt_raw = placed([P, PASSES, PACK, H], F32, "wt_raw", 20)
+        gather_whole(0)
+        wt_raw = placed([P, PASSES, PACK, H], F32, "wt_raw", 35)
         for a in range(PASSES):
             rows = wt[a * P * PACK : (a + 1) * P * PACK, :]
             nc.sync.dma_start(out=wt_raw[:, a, :, :], in_=rows.rearrange("(p j) c -> p j c", j=PACK))
+        wq_raw = placed([P, PACK, N], F32, "wq_raw", 60)
+        nc.sync.dma_start(out=wq_raw[:], in_=wq.rearrange("(p j) c -> p j c", j=PACK))
+        wp_codes = placed([P, N], I32, "wp_codes", 66)
+        nc.sync.dma_start(out=wp_codes[:], in_=wp_words[0].rearrange("p c i -> p (c i)").bitcast(I32))
+        wp_plane = placed([P, N // 4], I32, "wp_plane", 68)
+        nc.vector.memset(wp_plane[:], 0)
+        for q in range(4):
+            nc.sync.dma_start(
+                out=wp_plane[32 * q : 32 * q + 4, :],
+                in_=wp_scales[0, 4 * q : 4 * q + 4, :].bitcast(I32),
+            )
+        gather_whole(1)
 
         banks = {}
 
@@ -161,9 +175,9 @@ def tile_list_campaign_branch_bids_kernel(
             gain = gs_sb if branch == "sigmoid" else gt_sb
             hidden[branch, h] = held([P, HALF * PACK], BF16, "hidden_%s%d" % (branch, h))
             nc.vector.tensor_tensor(
-                out=hidden[branch, h][:].rearrange("p (c i t) -> p c t i", i=4, t=PACK),
-                in0=acts[branch, h][:].rearrange("p t (c i) -> p c t i", i=4),
-                in1=gain.unsqueeze(1).unsqueeze(3).to_broadcast([P, HALF // 4, PACK, 4]),
+                out=hidden[branch, h][:].rearrange("p (c i t) -> p c t i", i=2, t=PACK),
+                in0=acts[branch, h][:].rearrange("p t (c i) -> p c t i", i=2),
+                in1=gain.unsqueeze(1).unsqueeze(3).to_broadcast([P, HALF // 2, PACK, 2]),
                 op=MULT,
             )
 
@@ -184,13 +198,12 @@ def tile_list_campaign_branch_bids_kernel(
         wt_plane = [held([P, H], U8, "wt_plane%d" % a) for a in range(PASSES)]
 
         def round_wt(a, on_vector):
-            dst = wt_grouped[a][:].rearrange("p (u e m j) -> p u m j e", u=2, e=2, j=PACK)
-            src = wt_raw[:, a, :, :].rearrange("p j (m u e) -> p u m j e", u=2, e=2)
+            dst = wt_grouped[a][:].rearrange("p (t m j) -> p m t j", t=PACK, j=PACK)
+            src = wt_raw[:, a, :, :].rearrange("p j (m t) -> p m t j", t=PACK)
             if on_vector:
                 nc.vector.tensor_copy(out=dst, in_=src)
             else:
-                for u in range(2):
-                    nc.scalar.copy(out=dst[:, u, :, :, :], in_=src[:, u, :, :, :])
+                nc.scalar.copy(out=dst, in_=src)
 
         def quantise_wt(a):
             nc.vector.quantize_mx(out=wt_codes[a][:].bitcast(FP8X4), scales=wt_plane[a][:], in_=wt_grouped[a][:])
@@ -238,10 +251,6 @@ def tile_list_campaign_branch_bids_kernel(
         for h in range(HALVES):
             gather_half(PASSES - 1, h)
             first_layer("sigmoid", h, PASSES - 1)
-        wq_raw = placed([P, PACK, N], F32, "wq_raw", 0)
-        nc.sync.dma_start(out=wq_raw[:], in_=wq.rearrange("(p j) c -> p j c", j=PACK))
-        wp_codes = placed([P, N], I32, "wp_codes", 6)
-        nc.sync.dma_start(out=wp_codes[:], in_=wp_words[0].rearrange("p c i -> p (c i)").bitcast(I32))
         activate("sigmoid", 0)
         round_wt(0, True)
         activate("sigmoid", 1)
@@ -259,8 +268,8 @@ def tile_list_campaign_branch_bids_kernel(
         first_layer("tanh", 1, 2)
         quantise_hidden("sigmoid", 0)
         nc.scalar.copy(
-            out=wq_grouped[:].rearrange("p (c i j) -> p c j i", i=4, j=PACK),
-            in_=wq_raw[:].rearrange("p j (c i) -> p c j i", i=4),
+            out=wq_grouped[:].rearrange("p (c i j) -> p c j i", i=2, j=PACK),
+            in_=wq_raw[:].rearrange("p j (c i) -> p c j i", i=2),
         )
         apply_gain("sigmoid", 1)
         activate("tanh", 0)

@@ -22,7 +22,8 @@ PASSES = K // (P * PACK)
 HALF = 512
 HALVES = S // HALF
 SLOT_TILES = N // P
-SHIFT_ROWS = 112
+UNIT = 128
+UNITS = S // UNIT
 
 
 def tile_list_campaign_branch_bids_kernel(
@@ -141,10 +142,11 @@ def tile_list_campaign_branch_bids_kernel(
 
         banks = {}
 
-        def first_layer(branch, h, a):
+        def first_layer(branch, u, a):
+            if a == 0:
+                banks[branch, u] = psum.tile([P, PACK, UNIT], F32, name="bank")
+            h, lo = divmod(u * UNIT, HALF)
             for t in range(PACK):
-                if a == 0:
-                    banks[branch, h, t] = psum.tile([P, HALF], F32, name="bank")
                 if branch == "sigmoid":
                     lhsT = wg_codes[:, a, 2 * P * t : 2 * P * (t + 1)].bitcast(FP4X4)
                     lhsT_scale = wg_plane[:, a, P * t : P * (t + 1)]
@@ -152,58 +154,64 @@ def tile_list_campaign_branch_bids_kernel(
                     lhsT = wt_codes[a][:, P * t : P * (t + 1)].bitcast(FP8X4)
                     lhsT_scale = wt_plane[a][:, P * t : P * (t + 1)]
                 nc.tensor.matmul_mx(
-                    out=banks[branch, h, t][:],
+                    out=banks[branch, u][:, t, :],
                     lhsT=lhsT,
                     lhsT_scale=lhsT_scale,
-                    rhs=v_codes[a, h].bitcast(FP8X4),
-                    rhs_scale=v_planes[a][:, h * HALF : (h + 1) * HALF],
-                    start=(a == 0),
-                    stop=(a == PASSES - 1),
+                    rhs=v_codes[a, h][:, lo : lo + UNIT].bitcast(FP8X4),
+                    rhs_scale=v_planes[a][:, u * UNIT : (u + 1) * UNIT],
+                    start=(a == 0 and t == 0),
+                    stop=(a == PASSES - 1 and t == PACK - 1),
                 )
 
         acts = {}
-
-        def activate(branch, h):
-            func = ACT.Sigmoid if branch == "sigmoid" else ACT.Tanh
-            acts[branch, h] = held([P, PACK, HALF], F32, "act_%s%d" % (branch, h))
-            for t in range(PACK):
-                nc.scalar.activation(out=acts[branch, h][:, t, :], in_=banks[branch, h, t][:], func=func)
-
         hidden = {}
+        hidden_codes = {}
+        hidden_plane = {}
+        for branch in ("sigmoid", "tanh"):
+            for h in range(HALVES):
+                hidden_codes[branch, h] = held([P, HALF], U32, "hidden_codes_%s%d" % (branch, h))
+                hidden_plane[branch, h] = held([P, HALF], U8, "hidden_plane_%s%d" % (branch, h))
+            for d in range(UNITS // 2):
+                acts[branch, d] = held([P, 2 * UNIT * PACK], F32, "act_%s%d" % (branch, d))
+                hidden[branch, d] = held([P, 2 * UNIT * PACK], BF16, "hidden_%s%d" % (branch, d))
 
-        def apply_gain(branch, h):
+        def activate(branch, u):
+            func = ACT.Sigmoid if branch == "sigmoid" else ACT.Tanh
+            lo = (u % 2) * UNIT * PACK
+            nc.scalar.activation(
+                out=acts[branch, u // 2][:, lo : lo + UNIT * PACK].rearrange("p (c t) -> p c t", t=PACK),
+                in_=banks[branch, u][:].rearrange("p t c -> p c t"),
+                func=func,
+            )
+
+        def apply_gain(branch, u, count):
             gain = gs_sb if branch == "sigmoid" else gt_sb
-            hidden[branch, h] = held([P, HALF * PACK], BF16, "hidden_%s%d" % (branch, h))
+            lo = (u % 2) * UNIT * PACK
+            cols = slice(lo, lo + count * UNIT * PACK)
             nc.vector.tensor_tensor(
-                out=hidden[branch, h][:].rearrange("p (c i t) -> p c t i", i=2, t=PACK),
-                in0=acts[branch, h][:].rearrange("p t (c i) -> p c t i", i=2),
-                in1=gain.unsqueeze(1).unsqueeze(3).to_broadcast([P, HALF // 2, PACK, 2]),
+                out=hidden[branch, u // 2][:, cols].rearrange("p (c t) -> p c t", t=PACK),
+                in0=acts[branch, u // 2][:, cols].rearrange("p (c t) -> p c t", t=PACK),
+                in1=gain.unsqueeze(1).to_broadcast([P, count * UNIT, PACK]),
                 op=MULT,
             )
 
-        hidden_codes = {}
-        hidden_plane = {}
-
-        def quantise_hidden(branch, h):
-            hidden_codes[branch, h] = held([P, HALF], U32, "hidden_codes_%s%d" % (branch, h))
-            hidden_plane[branch, h] = held([P, HALF], U8, "hidden_plane_%s%d" % (branch, h))
+        def quantise_hidden(branch, u, count):
+            h, at = divmod(u * UNIT, HALF)
+            lo = (u % 2) * UNIT * PACK
             nc.vector.quantize_mx(
-                out=hidden_codes[branch, h][:].bitcast(FP8X4),
-                scales=hidden_plane[branch, h][:],
-                in_=hidden[branch, h][:],
+                out=hidden_codes[branch, h][:, at : at + count * UNIT].bitcast(FP8X4),
+                scales=hidden_plane[branch, h][:, at : at + count * UNIT],
+                in_=hidden[branch, u // 2][:, lo : lo + count * UNIT * PACK],
             )
 
         wt_grouped = [held([P, H * PACK], BF16, "wt_grouped%d" % a) for a in range(PASSES)]
         wt_codes = [held([P, H], U32, "wt_codes%d" % a) for a in range(PASSES)]
         wt_plane = [held([P, H], U8, "wt_plane%d" % a) for a in range(PASSES)]
 
-        def round_wt(a, on_vector):
+        def round_wt(a, copy, lo, hi):
             dst = wt_grouped[a][:].rearrange("p (t m j) -> p m t j", t=PACK, j=PACK)
             src = wt_raw[:, a, :, :].rearrange("p j (m t) -> p m t j", t=PACK)
-            if on_vector:
-                nc.vector.tensor_copy(out=dst, in_=src)
-            else:
-                nc.scalar.copy(out=dst, in_=src)
+            copy(out=dst[:, :, lo:hi, :], in_=src[:, :, lo:hi, :])
 
         def quantise_wt(a):
             nc.vector.quantize_mx(out=wt_codes[a][:].bitcast(FP8X4), scales=wt_plane[a][:], in_=wt_grouped[a][:])
@@ -212,84 +220,127 @@ def tile_list_campaign_branch_bids_kernel(
         wq_codes = held([P, N], U32, "wq_codes")
         wq_plane = held([P, N], U8, "wq_plane")
 
-        def second_layer(branch, h):
+        response = {}
+
+        def respond(h):
+            response[h] = held([P, SLOT_TILES, HALF], F32, "response%d" % h)
             for n in range(SLOT_TILES):
                 cols = slice(P * n, P * (n + 1))
-                banks[branch, h, "slots", n] = psum.tile([P, HALF], F32, name="bank")
-                if branch == "sigmoid":
-                    lhsT, lhsT_scale = wq_codes[:, cols], wq_plane[:, cols]
-                else:
-                    lhsT, lhsT_scale = wp_codes[:, cols], wp_plane[:].bitcast(U8)[:, cols]
+                bank = psum.tile([P, HALF], F32, name="bank")
                 nc.tensor.matmul_mx(
-                    out=banks[branch, h, "slots", n][:],
-                    lhsT=lhsT.bitcast(FP8X4),
-                    lhsT_scale=lhsT_scale,
-                    rhs=hidden_codes[branch, h][:].bitcast(FP8X4),
-                    rhs_scale=hidden_plane[branch, h][:],
+                    out=bank[:],
+                    lhsT=wq_codes[:, cols].bitcast(FP8X4),
+                    lhsT_scale=wq_plane[:, cols],
+                    rhs=hidden_codes["sigmoid", h][:].bitcast(FP8X4),
+                    rhs_scale=hidden_plane["sigmoid", h][:],
+                    start=True,
+                    stop=True,
+                )
+                nc.scalar.copy(out=response[h][:, n, :], in_=bank[:])
+
+        values = {}
+
+        def value(u):
+            h, at = divmod(u * UNIT, HALF)
+            values[u] = psum.tile([P, SLOT_TILES, UNIT], F32, name="bank")
+            for n in range(SLOT_TILES):
+                cols = slice(P * n, P * (n + 1))
+                nc.tensor.matmul_mx(
+                    out=values[u][:, n, :],
+                    lhsT=wp_codes[:, cols].bitcast(FP8X4),
+                    lhsT_scale=wp_plane[:].bitcast(U8)[:, cols],
+                    rhs=hidden_codes["tanh", h][:, at : at + UNIT].bitcast(FP8X4),
+                    rhs_scale=hidden_plane["tanh", h][:, at : at + UNIT],
                     start=True,
                     stop=True,
                 )
 
-        response = {}
+        bids = [held([P, SLOT_TILES, 2 * UNIT], F32, "bids%d" % d) for d in range(UNITS // 2)]
+        out_tiles = out.rearrange("(n p) c -> p n c", p=P)
 
-        def keep_response(h):
-            for n in range(SLOT_TILES):
-                response[h, n] = held([P, HALF], F32, "response%d_%d" % (h, n))
-                nc.scalar.copy(out=response[h, n][:], in_=banks["sigmoid", h, "slots", n][:])
+        def multiply(u):
+            h, at = divmod(u * UNIT, HALF)
+            lo = (u % 2) * UNIT
+            nc.vector.tensor_tensor(
+                out=bids[u // 2][:, :, lo : lo + UNIT],
+                in0=values[u][:],
+                in1=response[h][:, :, at : at + UNIT],
+                op=MULT,
+            )
 
-        def multiply_and_store(h):
-            for n in range(SLOT_TILES):
-                bids = held([P, HALF], F32, "bids%d_%d" % (h, n))
-                nc.vector.tensor_tensor(
-                    out=bids[:], in0=banks["tanh", h, "slots", n][:], in1=response[h, n][:], op=MULT
-                )
-                nc.sync.dma_start(out=out[P * n : P * (n + 1), h * HALF : (h + 1) * HALF], in_=bids[:])
+        def store(u, count):
+            lo = (u % 2) * UNIT
+            nc.sync.dma_start(
+                out=out_tiles[:, :, UNIT * u : UNIT * (u + count)], in_=bids[u // 2][:, :, lo : lo + count * UNIT]
+            )
 
-        for a in range(PASSES - 1):
-            for h in range(HALVES):
-                first_layer("sigmoid", h, a)
+        per_half = UNITS // HALVES
         for h in range(HALVES):
+            for a in range(PASSES - 1):
+                for u in range(h * per_half, (h + 1) * per_half):
+                    first_layer("sigmoid", u, a)
             gather_half(PASSES - 1, h)
-            first_layer("sigmoid", h, PASSES - 1)
-        activate("sigmoid", 0)
-        round_wt(0, True)
-        activate("sigmoid", 1)
+            for u in range(h * per_half, (h + 1) * per_half):
+                first_layer("sigmoid", u, PASSES - 1)
+        for u in range(4):
+            activate("sigmoid", u)
+        round_wt(0, nc.vector.tensor_copy, 0, PACK)
         quantise_wt(0)
-        round_wt(1, True)
-        first_layer("tanh", 0, 0)
-        first_layer("tanh", 1, 0)
+        round_wt(1, nc.scalar.copy, 0, PACK)
+        round_wt(2, nc.vector.tensor_copy, 0, 2)
+        round_wt(2, nc.scalar.copy, 2, PACK)
         quantise_wt(1)
-        round_wt(2, False)
-        first_layer("tanh", 0, 1)
-        first_layer("tanh", 1, 1)
-        apply_gain("sigmoid", 0)
         quantise_wt(2)
-        first_layer("tanh", 0, 2)
-        first_layer("tanh", 1, 2)
-        quantise_hidden("sigmoid", 0)
+        for u in range(4, UNITS):
+            activate("sigmoid", u)
+        for a in range(PASSES - 1):
+            for u in range(4):
+                first_layer("tanh", u, a)
+        for u in range(4):
+            first_layer("tanh", u, PASSES - 1)
+        for u in range(4, UNITS):
+            for a in range(PASSES):
+                first_layer("tanh", u, a)
+        apply_gain("sigmoid", 0, 2)
+        apply_gain("sigmoid", 2, 2)
+        quantise_hidden("sigmoid", 0, 2)
+        quantise_hidden("sigmoid", 2, 2)
+        apply_gain("sigmoid", 4, 2)
+        apply_gain("sigmoid", 6, 2)
+        quantise_hidden("sigmoid", 4, 2)
+        quantise_hidden("sigmoid", 6, 2)
+        for u in range(4):
+            activate("tanh", u)
         nc.scalar.copy(
             out=wq_grouped[:].rearrange("p (c i j) -> p c j i", i=2, j=PACK),
             in_=wq_raw[:].rearrange("p j (c i) -> p c j i", i=2),
         )
-        apply_gain("sigmoid", 1)
-        activate("tanh", 0)
         for lo, hi in ((0, 256), (256, N)):
             nc.vector.quantize_mx(
                 out=wq_codes[:, lo:hi].bitcast(FP8X4),
                 scales=wq_plane[:, lo:hi],
                 in_=wq_grouped[:, PACK * lo : PACK * hi],
             )
-        quantise_hidden("sigmoid", 1)
-        activate("tanh", 1)
-        second_layer("sigmoid", 0)
-        apply_gain("tanh", 0)
-        second_layer("sigmoid", 1)
-        keep_response(0)
-        quantise_hidden("tanh", 0)
-        apply_gain("tanh", 1)
-        second_layer("tanh", 0)
-        keep_response(1)
-        quantise_hidden("tanh", 1)
-        multiply_and_store(0)
-        second_layer("tanh", 1)
-        multiply_and_store(1)
+        for u in range(4, UNITS):
+            activate("tanh", u)
+        respond(0)
+        respond(1)
+        apply_gain("tanh", 0, 2)
+        apply_gain("tanh", 2, 2)
+        quantise_hidden("tanh", 0, 2)
+        apply_gain("tanh", 4, 2)
+        quantise_hidden("tanh", 2, 2)
+        apply_gain("tanh", 6, 2)
+        quantise_hidden("tanh", 4, 2)
+        quantise_hidden("tanh", 6, 2)
+        for d in range(UNITS // 2):
+            value(2 * d)
+            value(2 * d + 1)
+            multiply(2 * d)
+            if d == UNITS // 2 - 1:
+                store(2 * d, 1)
+            multiply(2 * d + 1)
+            if d == UNITS // 2 - 1:
+                store(2 * d + 1, 1)
+            else:
+                store(2 * d, 2)

@@ -53,9 +53,13 @@ def tile_list_campaign_branch_bids_kernel(
             nc.vector.memset(table_scales[lo:hi, :], 0)
         nc.vector.memset(v_plane_words[:], 0)
 
-        def load_table(a, kib):
+        def load_table(a, part):
+            cols = slice(part * T // 2, (part + 1) * T // 2)
+            words = tab_words[a].rearrange("p t i -> p (t i)").bitcast(I32)
+            nc.sync.dma_start(out=table[a][:, cols], in_=words[:, cols])
+
+        for a, kib in enumerate((58, 0, 18)):
             table[a] = placed([P, T], I32, "table%d" % a, kib)
-            nc.sync.dma_start(out=table[a][:], in_=tab_words[a].rearrange("p t i -> p (t i)").bitcast(I32))
 
         nc.sync.dma_start(offsets[:], offs)
         scale_rows = tab_scales.rearrange("a q t -> (a q) t").bitcast(I32)
@@ -63,12 +67,19 @@ def tile_list_campaign_branch_bids_kernel(
         nc.sync.dma_start(out=table_scales[96:128, :], in_=scale_rows[16:48, :])
         first_row = (16, 96, 112)
         nc.sync.dma_start(out=wg_raw[:], in_=wg_words.rearrange("a p c -> p a c").bitcast(I32))
-        load_table(0, 58)
+        load_table(0, 0)
         for q in range(4):
             nc.sync.dma_start(
                 out=wg_scales_raw[32 * q : 32 * q + 4, :, :],
                 in_=wg_scales[:, 4 * q : 4 * q + 4, :].rearrange("a r c -> r a c").bitcast(I32),
             )
+
+        gains = held([P, 2, 2 * PACK], F32, "gains")
+        gs_sb = gains[:, 0, 0:PACK]
+        gt_sb = gains[:, 1, 0:PACK]
+        nc.sync.dma_start(out=gs_sb, in_=gs.rearrange("(p t) -> p t", t=PACK))
+        nc.sync.dma_start(out=gt_sb, in_=gt.rearrange("(p t) -> p t", t=PACK))
+        load_table(0, 1)
 
         picked_scales = held([P, S], U8, "picked_scales")
         nc.vector.tensor_copy(picked_scales[:], table_scales[:].bitcast(U8).indirect(offsets[:]))
@@ -80,21 +91,15 @@ def tile_list_campaign_branch_bids_kernel(
                 in_=picked_scales[row : row + 4, :].bitcast(I32),
             )
 
-        move_scale_rows(0, 0)
-        move_scale_rows(0, 1)
+        moves = [(a, q) for a in range(PASSES) for q in range(4)]
         load_table(1, 0)
-        move_scale_rows(0, 2)
-        move_scale_rows(0, 3)
-        for q in range(4):
-            move_scale_rows(1, q)
-        load_table(2, 18)
-        for q in range(4):
-            move_scale_rows(2, q)
-        gains = placed([P, 2, 2 * PACK], F32, "gains", 16)
-        gs_sb = gains[:, 0, 0:PACK]
-        gt_sb = gains[:, 1, 0:PACK]
-        nc.sync.dma_start(out=gs_sb, in_=gs.rearrange("(p t) -> p t", t=PACK))
-        nc.sync.dma_start(out=gt_sb, in_=gt.rearrange("(p t) -> p t", t=PACK))
+        for a, q in moves[:6]:
+            move_scale_rows(a, q)
+        load_table(1, 1)
+        for a, q in moves[6:]:
+            move_scale_rows(a, q)
+        load_table(2, 0)
+        load_table(2, 1)
         v_planes = [v_plane_words[:, a, :].bitcast(U8) for a in range(PASSES)]
 
         wg_codes = held([P, PASSES, 2 * H], U8, "wg_codes")
@@ -208,10 +213,10 @@ def tile_list_campaign_branch_bids_kernel(
         wt_codes = [held([P, H], U32, "wt_codes%d" % a) for a in range(PASSES)]
         wt_plane = [held([P, H], U8, "wt_plane%d" % a) for a in range(PASSES)]
 
-        def round_wt(a, copy, lo, hi):
-            dst = wt_grouped[a][:].rearrange("p (t m j) -> p m t j", t=PACK, j=PACK)
-            src = wt_raw[:, a, :, :].rearrange("p j (m t) -> p m t j", t=PACK)
-            copy(out=dst[:, :, lo:hi, :], in_=src[:, :, lo:hi, :])
+        def round_wt(a, copy, u):
+            dst = wt_grouped[a][:].rearrange("p (t m j) -> p m j t", t=PACK, j=PACK)
+            src = wt_raw[:, a, :, :].rearrange("p j (m t) -> p m j t", t=PACK)
+            copy(out=dst[:, :, :, 2 * u : 2 * u + 2], in_=src[:, :, :, 2 * u : 2 * u + 2])
 
         def quantise_wt(a):
             nc.vector.quantize_mx(out=wt_codes[a][:].bitcast(FP8X4), scales=wt_plane[a][:], in_=wt_grouped[a][:])
@@ -284,11 +289,14 @@ def tile_list_campaign_branch_bids_kernel(
                 first_layer("sigmoid", u, PASSES - 1)
         for u in range(4):
             activate("sigmoid", u)
-        round_wt(0, nc.vector.tensor_copy, 0, PACK)
+        round_wt(0, nc.vector.tensor_copy, 0)
+        round_wt(0, nc.vector.tensor_copy, 1)
+        round_wt(1, nc.scalar.copy, 0)
+        round_wt(1, nc.scalar.copy, 1)
+        round_wt(2, nc.vector.tensor_copy, 0)
+        round_wt(2, nc.scalar.copy, 1)
+        apply_gain("sigmoid", 0, 2)
         quantise_wt(0)
-        round_wt(1, nc.scalar.copy, 0, PACK)
-        round_wt(2, nc.vector.tensor_copy, 0, 2)
-        round_wt(2, nc.scalar.copy, 2, PACK)
         quantise_wt(1)
         quantise_wt(2)
         for u in range(4, UNITS):
@@ -301,7 +309,6 @@ def tile_list_campaign_branch_bids_kernel(
         for u in range(4, UNITS):
             for a in range(PASSES):
                 first_layer("tanh", u, a)
-        apply_gain("sigmoid", 0, 2)
         apply_gain("sigmoid", 2, 2)
         quantise_hidden("sigmoid", 0, 2)
         quantise_hidden("sigmoid", 2, 2)

@@ -24,6 +24,7 @@ HALVES = S // HALF
 SLOT_TILES = N // P
 UNIT = 128
 UNITS = S // UNIT
+PAIR = 2 * UNIT
 
 
 def tile_list_campaign_branch_bids_kernel(
@@ -147,26 +148,37 @@ def tile_list_campaign_branch_bids_kernel(
 
         banks = {}
 
-        def first_layer(branch, u, a):
+        def sigmoid_pass(u, a):
             if a == 0:
-                banks[branch, u] = psum.tile([P, PACK, UNIT], F32, name="bank")
+                banks["sigmoid", u] = psum.tile([P, PACK, UNIT], F32, name="bank")
             h, lo = divmod(u * UNIT, HALF)
             for t in range(PACK):
-                if branch == "sigmoid":
-                    lhsT = wg_codes[:, a, 2 * P * t : 2 * P * (t + 1)].bitcast(FP4X4)
-                    lhsT_scale = wg_plane[:, a, P * t : P * (t + 1)]
-                else:
-                    lhsT = wt_codes[a][:, P * t : P * (t + 1)].bitcast(FP8X4)
-                    lhsT_scale = wt_plane[a][:, P * t : P * (t + 1)]
                 nc.tensor.matmul_mx(
-                    out=banks[branch, u][:, t, :],
-                    lhsT=lhsT,
-                    lhsT_scale=lhsT_scale,
+                    out=banks["sigmoid", u][:, t, :],
+                    lhsT=wg_codes[:, a, 2 * P * t : 2 * P * (t + 1)].bitcast(FP4X4),
+                    lhsT_scale=wg_plane[:, a, P * t : P * (t + 1)],
                     rhs=v_codes[a, h][:, lo : lo + UNIT].bitcast(FP8X4),
                     rhs_scale=v_planes[a][:, u * UNIT : (u + 1) * UNIT],
                     start=(a == 0 and t == 0),
                     stop=(a == PASSES - 1 and t == PACK - 1),
                 )
+
+        def tanh_pass(d, a):
+            h, lo = divmod(d * PAIR, HALF)
+            for side in range(2):
+                if a == 0:
+                    banks["tanh", d, side] = psum.tile([P, 2, PAIR], F32, name="bank")
+                for e in range(2):
+                    t = 2 * side + e
+                    nc.tensor.matmul_mx(
+                        out=banks["tanh", d, side][:, e, :],
+                        lhsT=wt_codes[a][:, P * t : P * (t + 1)].bitcast(FP8X4),
+                        lhsT_scale=wt_plane[a][:, P * t : P * (t + 1)],
+                        rhs=v_codes[a, h][:, lo : lo + PAIR].bitcast(FP8X4),
+                        rhs_scale=v_planes[a][:, d * PAIR : (d + 1) * PAIR],
+                        start=(a == 0 and e == 0),
+                        stop=(a == PASSES - 1 and e == 1),
+                    )
 
         acts = {}
         hidden = {}
@@ -180,23 +192,35 @@ def tile_list_campaign_branch_bids_kernel(
                 acts[branch, d] = held([P, 2 * UNIT * PACK], F32, "act_%s%d" % (branch, d))
                 hidden[branch, d] = held([P, 2 * UNIT * PACK], BF16, "hidden_%s%d" % (branch, d))
 
-        def activate(branch, u):
-            func = ACT.Sigmoid if branch == "sigmoid" else ACT.Tanh
+        def activate_sigmoid(u):
             lo = (u % 2) * UNIT * PACK
             nc.scalar.activation(
-                out=acts[branch, u // 2][:, lo : lo + UNIT * PACK].rearrange("p (c t) -> p c t", t=PACK),
-                in_=banks[branch, u][:].rearrange("p t c -> p c t"),
-                func=func,
+                out=acts["sigmoid", u // 2][:, lo : lo + UNIT * PACK].rearrange("p (c t) -> p c t", t=PACK),
+                in_=banks["sigmoid", u][:].rearrange("p t c -> p c t"),
+                func=ACT.Sigmoid,
             )
 
-        def apply_gain(branch, u, count):
-            gain = gs_sb if branch == "sigmoid" else gt_sb
-            lo = (u % 2) * UNIT * PACK
-            cols = slice(lo, lo + count * UNIT * PACK)
+        def activate_tanh(d):
+            for side in range(2):
+                nc.scalar.activation(
+                    out=acts["tanh", d][:, side * 2 * PAIR : (side + 1) * 2 * PAIR].rearrange("p (c e) -> p c e", e=2),
+                    in_=banks["tanh", d, side][:].rearrange("p e c -> p c e"),
+                    func=ACT.Tanh,
+                )
+
+        def gain_sigmoid(d):
             nc.vector.tensor_tensor(
-                out=hidden[branch, u // 2][:, cols].rearrange("p (c t) -> p c t", t=PACK),
-                in0=acts[branch, u // 2][:, cols].rearrange("p (c t) -> p c t", t=PACK),
-                in1=gain.unsqueeze(1).to_broadcast([P, count * UNIT, PACK]),
+                out=hidden["sigmoid", d][:].rearrange("p (c t) -> p c t", t=PACK),
+                in0=acts["sigmoid", d][:].rearrange("p (c t) -> p c t", t=PACK),
+                in1=gs_sb.unsqueeze(1).to_broadcast([P, PAIR, PACK]),
+                op=MULT,
+            )
+
+        def gain_tanh(d):
+            nc.vector.tensor_tensor(
+                out=hidden["tanh", d][:].rearrange("p (c s e) -> p c s e", s=2, e=2),
+                in0=acts["tanh", d][:].rearrange("p (s c e) -> p c s e", s=2, e=2),
+                in1=gt_sb.rearrange("p (s e) -> p s e", s=2).unsqueeze(1).to_broadcast([P, PAIR, 2, 2]),
                 op=MULT,
             )
 
@@ -243,81 +267,70 @@ def tile_list_campaign_branch_bids_kernel(
                 )
                 nc.scalar.copy(out=response[h][:, n, :], in_=bank[:])
 
+        out_tiles = out.rearrange("(n p) c -> p n c", p=P)
         values = {}
 
-        def value(u):
-            h, at = divmod(u * UNIT, HALF)
-            values[u] = psum.tile([P, SLOT_TILES, UNIT], F32, name="bank")
-            for n in range(SLOT_TILES):
+        def value(lo, width, tiles):
+            h, at = divmod(lo, HALF)
+            values[lo, tiles] = psum.tile([P, len(tiles), width], F32, name="bank")
+            for i, n in enumerate(tiles):
                 cols = slice(P * n, P * (n + 1))
                 nc.tensor.matmul_mx(
-                    out=values[u][:, n, :],
+                    out=values[lo, tiles][:, i, :],
                     lhsT=wp_codes[:, cols].bitcast(FP8X4),
                     lhsT_scale=wp_plane[:].bitcast(U8)[:, cols],
-                    rhs=hidden_codes["tanh", h][:, at : at + UNIT].bitcast(FP8X4),
-                    rhs_scale=hidden_plane["tanh", h][:, at : at + UNIT],
+                    rhs=hidden_codes["tanh", h][:, at : at + width].bitcast(FP8X4),
+                    rhs_scale=hidden_plane["tanh", h][:, at : at + width],
                     start=True,
                     stop=True,
                 )
 
-        bids = [held([P, SLOT_TILES, 2 * UNIT], F32, "bids%d" % d) for d in range(UNITS // 2)]
-        out_tiles = out.rearrange("(n p) c -> p n c", p=P)
-
-        def multiply(u):
-            h, at = divmod(u * UNIT, HALF)
-            lo = (u % 2) * UNIT
+        def multiply_and_store(lo, width, tiles):
+            h, at = divmod(lo, HALF)
+            bids = held([P, len(tiles), width], F32, "bids%d_%d" % (lo, tiles[0]))
+            rows = slice(tiles[0], tiles[-1] + 1)
             nc.vector.tensor_tensor(
-                out=bids[u // 2][:, :, lo : lo + UNIT],
-                in0=values[u][:],
-                in1=response[h][:, :, at : at + UNIT],
-                op=MULT,
+                out=bids[:], in0=values[lo, tiles][:], in1=response[h][:, rows, at : at + width], op=MULT
             )
-
-        def store(u, count):
-            lo = (u % 2) * UNIT
-            nc.sync.dma_start(
-                out=out_tiles[:, :, UNIT * u : UNIT * (u + count)], in_=bids[u // 2][:, :, lo : lo + count * UNIT]
-            )
+            nc.sync.dma_start(out=out_tiles[:, rows, lo : lo + width], in_=bids[:])
 
         per_half = UNITS // HALVES
         for h in range(HALVES):
             for a in range(PASSES - 1):
                 for u in range(h * per_half, (h + 1) * per_half):
-                    first_layer("sigmoid", u, a)
+                    sigmoid_pass(u, a)
             gather_half(PASSES - 1, h)
             for u in range(h * per_half, (h + 1) * per_half):
-                first_layer("sigmoid", u, PASSES - 1)
+                sigmoid_pass(u, PASSES - 1)
         for u in range(4):
-            activate("sigmoid", u)
+            activate_sigmoid(u)
         round_wt(0, nc.vector.tensor_copy, 0)
         round_wt(0, nc.vector.tensor_copy, 1)
         round_wt(1, nc.scalar.copy, 0)
         round_wt(1, nc.scalar.copy, 1)
         round_wt(2, nc.vector.tensor_copy, 0)
         round_wt(2, nc.scalar.copy, 1)
-        apply_gain("sigmoid", 0, 2)
+        gain_sigmoid(0)
         quantise_wt(0)
         quantise_wt(1)
         quantise_wt(2)
         for u in range(4, UNITS):
-            activate("sigmoid", u)
-        for a in range(PASSES - 1):
-            for u in range(4):
-                first_layer("tanh", u, a)
-        for u in range(4):
-            first_layer("tanh", u, PASSES - 1)
-        for u in range(4, UNITS):
+            activate_sigmoid(u)
+        for a in range(PASSES):
+            for d in range(2):
+                tanh_pass(d, a)
+        for d in range(2, 4):
             for a in range(PASSES):
-                first_layer("tanh", u, a)
-        apply_gain("sigmoid", 2, 2)
+                tanh_pass(d, a)
+        gain_sigmoid(1)
         quantise_hidden("sigmoid", 0, 2)
         quantise_hidden("sigmoid", 2, 2)
-        apply_gain("sigmoid", 4, 2)
-        apply_gain("sigmoid", 6, 2)
+        gain_sigmoid(2)
+        gain_sigmoid(3)
         quantise_hidden("sigmoid", 4, 2)
         quantise_hidden("sigmoid", 6, 2)
-        for u in range(4):
-            activate("tanh", u)
+        activate_tanh(0)
+        activate_tanh(1)
         nc.scalar.copy(
             out=wq_grouped[:].rearrange("p (c i j) -> p c j i", i=2, j=PACK),
             in_=wq_raw[:].rearrange("p j (c i) -> p c j i", i=2),
@@ -328,26 +341,20 @@ def tile_list_campaign_branch_bids_kernel(
                 scales=wq_plane[:, lo:hi],
                 in_=wq_grouped[:, PACK * lo : PACK * hi],
             )
-        for u in range(4, UNITS):
-            activate("tanh", u)
+        activate_tanh(2)
+        activate_tanh(3)
         respond(0)
         respond(1)
-        apply_gain("tanh", 0, 2)
-        apply_gain("tanh", 2, 2)
+        gain_tanh(0)
+        gain_tanh(1)
         quantise_hidden("tanh", 0, 2)
-        apply_gain("tanh", 4, 2)
+        gain_tanh(2)
         quantise_hidden("tanh", 2, 2)
-        apply_gain("tanh", 6, 2)
+        gain_tanh(3)
         quantise_hidden("tanh", 4, 2)
         quantise_hidden("tanh", 6, 2)
-        for d in range(UNITS // 2):
-            value(2 * d)
-            value(2 * d + 1)
-            multiply(2 * d)
-            if d == UNITS // 2 - 1:
-                store(2 * d, 1)
-            multiply(2 * d + 1)
-            if d == UNITS // 2 - 1:
-                store(2 * d + 1, 1)
-            else:
-                store(2 * d, 2)
+        pieces = [(0, HALF, (n,)) for n in range(SLOT_TILES)]
+        pieces = pieces + [(lo, PAIR, tiles) for lo in (HALF, HALF + PAIR) for tiles in ((0, 1), (2,))]
+        for lo, width, tiles in pieces:
+            value(lo, width, tiles)
+            multiply_and_store(lo, width, tiles)

@@ -54,13 +54,9 @@ def tile_list_campaign_branch_bids_kernel(
             nc.vector.memset(table_scales[lo:hi, :], 0)
         nc.vector.memset(v_plane_words[:], 0)
 
-        def load_table(a, part):
-            cols = slice(part * T // 2, (part + 1) * T // 2)
-            words = tab_words[a].rearrange("p t i -> p (t i)").bitcast(I32)
-            nc.sync.dma_start(out=table[a][:, cols], in_=words[:, cols])
-
-        for a, kib in enumerate((58, 0, 18)):
+        def load_table(a, kib):
             table[a] = placed([P, T], I32, "table%d" % a, kib)
+            nc.sync.dma_start(out=table[a][:], in_=tab_words[a].rearrange("p t i -> p (t i)").bitcast(I32))
 
         nc.sync.dma_start(offsets[:], offs)
         scale_rows = tab_scales.rearrange("a q t -> (a q) t").bitcast(I32)
@@ -68,19 +64,12 @@ def tile_list_campaign_branch_bids_kernel(
         nc.sync.dma_start(out=table_scales[96:128, :], in_=scale_rows[16:48, :])
         first_row = (16, 96, 112)
         nc.sync.dma_start(out=wg_raw[:], in_=wg_words.rearrange("a p c -> p a c").bitcast(I32))
-        load_table(0, 0)
+        load_table(0, 58)
         for q in range(4):
             nc.sync.dma_start(
                 out=wg_scales_raw[32 * q : 32 * q + 4, :, :],
                 in_=wg_scales[:, 4 * q : 4 * q + 4, :].rearrange("a r c -> r a c").bitcast(I32),
             )
-
-        gains = held([P, 2, 2 * PACK], F32, "gains")
-        gs_sb = gains[:, 0, 0:PACK]
-        gt_sb = gains[:, 1, 0:PACK]
-        nc.sync.dma_start(out=gs_sb, in_=gs.rearrange("(p t) -> p t", t=PACK))
-        nc.sync.dma_start(out=gt_sb, in_=gt.rearrange("(p t) -> p t", t=PACK))
-        load_table(0, 1)
 
         picked_scales = held([P, S], U8, "picked_scales")
         nc.vector.tensor_copy(picked_scales[:], table_scales[:].bitcast(U8).indirect(offsets[:]))
@@ -92,15 +81,21 @@ def tile_list_campaign_branch_bids_kernel(
                 in_=picked_scales[row : row + 4, :].bitcast(I32),
             )
 
-        moves = [(a, q) for a in range(PASSES) for q in range(4)]
+        move_scale_rows(0, 0)
+        move_scale_rows(0, 1)
         load_table(1, 0)
-        for a, q in moves[:6]:
-            move_scale_rows(a, q)
-        load_table(1, 1)
-        for a, q in moves[6:]:
-            move_scale_rows(a, q)
-        load_table(2, 0)
-        load_table(2, 1)
+        move_scale_rows(0, 2)
+        move_scale_rows(0, 3)
+        for q in range(4):
+            move_scale_rows(1, q)
+        load_table(2, 18)
+        for q in range(4):
+            move_scale_rows(2, q)
+        gains = placed([P, 2, 2 * PACK], F32, "gains", 16)
+        gs_sb = gains[:, 0, 0:PACK]
+        gt_sb = gains[:, 1, 0:PACK]
+        nc.sync.dma_start(out=gs_sb, in_=gs.rearrange("(p t) -> p t", t=PACK))
+        nc.sync.dma_start(out=gt_sb, in_=gt.rearrange("(p t) -> p t", t=PACK))
         v_planes = [v_plane_words[:, a, :].bitcast(U8) for a in range(PASSES)]
 
         wg_codes = held([P, PASSES, 2 * H], U8, "wg_codes")
@@ -148,19 +143,18 @@ def tile_list_campaign_branch_bids_kernel(
 
         banks = {}
 
-        def sigmoid_pass(u, a):
-            if a == 0:
-                banks["sigmoid", u] = psum.tile([P, PACK, UNIT], F32, name="bank")
-            h, lo = divmod(u * UNIT, HALF)
+        def sigmoid_pass(h, a):
             for t in range(PACK):
+                if a == 0:
+                    banks["sigmoid", h, t] = psum.tile([P, HALF], F32, name="bank")
                 nc.tensor.matmul_mx(
-                    out=banks["sigmoid", u][:, t, :],
+                    out=banks["sigmoid", h, t][:],
                     lhsT=wg_codes[:, a, 2 * P * t : 2 * P * (t + 1)].bitcast(FP4X4),
                     lhsT_scale=wg_plane[:, a, P * t : P * (t + 1)],
-                    rhs=v_codes[a, h][:, lo : lo + UNIT].bitcast(FP8X4),
-                    rhs_scale=v_planes[a][:, u * UNIT : (u + 1) * UNIT],
-                    start=(a == 0 and t == 0),
-                    stop=(a == PASSES - 1 and t == PACK - 1),
+                    rhs=v_codes[a, h].bitcast(FP8X4),
+                    rhs_scale=v_planes[a][:, h * HALF : (h + 1) * HALF],
+                    start=(a == 0),
+                    stop=(a == PASSES - 1),
                 )
 
         def tanh_pass(d, a):
@@ -189,16 +183,15 @@ def tile_list_campaign_branch_bids_kernel(
                 hidden_codes[branch, h] = held([P, HALF], U32, "hidden_codes_%s%d" % (branch, h))
                 hidden_plane[branch, h] = held([P, HALF], U8, "hidden_plane_%s%d" % (branch, h))
             for d in range(UNITS // 2):
-                acts[branch, d] = held([P, 2 * UNIT * PACK], F32, "act_%s%d" % (branch, d))
+                if branch == "tanh":
+                    acts[branch, d] = held([P, 2 * UNIT * PACK], F32, "act_%s%d" % (branch, d))
                 hidden[branch, d] = held([P, 2 * UNIT * PACK], BF16, "hidden_%s%d" % (branch, d))
 
-        def activate_sigmoid(u):
-            lo = (u % 2) * UNIT * PACK
-            nc.scalar.activation(
-                out=acts["sigmoid", u // 2][:, lo : lo + UNIT * PACK].rearrange("p (c t) -> p c t", t=PACK),
-                in_=banks["sigmoid", u][:].rearrange("p t c -> p c t"),
-                func=ACT.Sigmoid,
-            )
+        planar = [held([P, PACK, HALF], F32, "sigmoid_planar%d" % h) for h in range(HALVES)]
+
+        def activate_sigmoid(h):
+            for t in range(PACK):
+                nc.scalar.activation(out=planar[h][:, t, :], in_=banks["sigmoid", h, t][:], func=ACT.Sigmoid)
 
         def activate_tanh(d):
             for side in range(2):
@@ -209,10 +202,11 @@ def tile_list_campaign_branch_bids_kernel(
                 )
 
         def gain_sigmoid(d):
+            h, lo = divmod(d * PAIR, HALF)
             nc.vector.tensor_tensor(
-                out=hidden["sigmoid", d][:].rearrange("p (c t) -> p c t", t=PACK),
-                in0=acts["sigmoid", d][:].rearrange("p (c t) -> p c t", t=PACK),
-                in1=gs_sb.unsqueeze(1).to_broadcast([P, PAIR, PACK]),
+                out=hidden["sigmoid", d][:].rearrange("p (c i t) -> p c t i", i=2, t=PACK),
+                in0=planar[h][:, :, lo : lo + PAIR].rearrange("p t (c i) -> p c t i", i=2),
+                in1=gs_sb.unsqueeze(1).unsqueeze(3).to_broadcast([P, PAIR // 2, PACK, 2]),
                 op=MULT,
             )
 
@@ -294,16 +288,12 @@ def tile_list_campaign_branch_bids_kernel(
             )
             nc.sync.dma_start(out=out_tiles[:, rows, lo : lo + width], in_=bids[:])
 
-        per_half = UNITS // HALVES
         for h in range(HALVES):
             for a in range(PASSES - 1):
-                for u in range(h * per_half, (h + 1) * per_half):
-                    sigmoid_pass(u, a)
+                sigmoid_pass(h, a)
             gather_half(PASSES - 1, h)
-            for u in range(h * per_half, (h + 1) * per_half):
-                sigmoid_pass(u, PASSES - 1)
-        for u in range(4):
-            activate_sigmoid(u)
+            sigmoid_pass(h, PASSES - 1)
+        activate_sigmoid(0)
         round_wt(0, nc.vector.tensor_copy, 0)
         round_wt(0, nc.vector.tensor_copy, 1)
         round_wt(1, nc.scalar.copy, 0)
@@ -314,8 +304,7 @@ def tile_list_campaign_branch_bids_kernel(
         quantise_wt(0)
         quantise_wt(1)
         quantise_wt(2)
-        for u in range(4, UNITS):
-            activate_sigmoid(u)
+        activate_sigmoid(1)
         for a in range(PASSES):
             for d in range(2):
                 tanh_pass(d, a)

@@ -19,12 +19,28 @@ MULT = mybir.AluOpType.mult
 P = 128
 PACK = 4
 PASSES = K // (P * PACK)
+LAST = PASSES - 1
 HALF = 512
 HALVES = S // HALF
+QUARTER = HALF // 2
+QUARTERS = S // QUARTER
 SLOT_TILES = N // P
-UNIT = 128
-UNITS = S // UNIT
-PAIR = 2 * UNIT
+
+AT_SCALE_WINDOW = 15
+AT_TABLE = (58, 0, 18)
+AT_GAINS = 16
+AT_WT = 35
+AT_WQ = 60
+AT_WP_CODES = 66
+AT_WP_PLANE = 68
+
+SCALE_ROW_LOADS = ((0, 8, 40), (8, 16, 48), (24, 8, 104), (32, 16, 112))
+SCALE_WINDOW_GAPS = ((0, 40), (64, 104))
+QUADRANT_ORDER = (0, 2, 1, 3)
+
+
+def scale_row_partition(row):
+    return [at + row - first for first, count, at in SCALE_ROW_LOADS if first <= row < first + count][0]
 
 
 def tile_list_campaign_branch_bids_kernel(
@@ -36,36 +52,35 @@ def tile_list_campaign_branch_bids_kernel(
         rooms = ctx.enter_context(tc.tile_pool(name="rooms", bufs=1))
         psum = ctx.enter_context(tc.psum_pool(name="psum", bufs=8))
 
-        def held(shape, dtype, name, tag=""):
-            return keep.tile(shape, dtype, name=name, tag=tag or name, align_bytes=64)
+        def held(shape, dtype, name):
+            return keep.tile(shape, dtype, name=name, tag=name, align_bytes=64)
 
         def placed(shape, dtype, name, kib):
-            return rooms.tile(shape, dtype, name=name, align_bytes=64, offset=int(kib * 1024))
+            return rooms.tile(shape, dtype, name=name, align_bytes=64, offset=kib * 1024)
 
         offsets = keep.tile([P, S // 16], U16, name="offsets")
         table = {}
-        table_scales = placed([P, T // 4], I32, "table_scales", 15)
+        table_scales = placed([P, T // 4], I32, "table_scales", AT_SCALE_WINDOW)
         wg_raw = held([P, PASSES, H // 2], I32, "wg_raw")
         wg_scales_raw = held([P, PASSES, H // 4], I32, "wg_scales_raw")
         v_plane_words = held([P, PASSES, S // 4], I32, "v_plane_words")
 
         nc.vector.memset(wg_scales_raw[:], 0)
-        for lo, hi in ((0, 16), (32, 64), (64, 96)):
+        for lo, hi in SCALE_WINDOW_GAPS:
             nc.vector.memset(table_scales[lo:hi, :], 0)
         nc.vector.memset(v_plane_words[:], 0)
 
-        def load_table(a, kib):
-            table[a] = placed([P, T], I32, "table%d" % a, kib)
+        def load_table(a):
+            table[a] = placed([P, T], I32, "table%d" % a, AT_TABLE[a])
             nc.sync.dma_start(out=table[a][:], in_=tab_words[a].rearrange("p t i -> p (t i)").bitcast(I32))
 
         nc.sync.dma_start(offsets[:], offs)
         scale_rows = tab_scales.rearrange("a q t -> (a q) t").bitcast(I32)
-        nc.sync.dma_start(out=table_scales[16:32, :], in_=scale_rows[0:16, :])
-        nc.sync.dma_start(out=table_scales[96:128, :], in_=scale_rows[16:48, :])
-        first_row = (16, 96, 112)
+        for first, count, at in SCALE_ROW_LOADS:
+            nc.sync.dma_start(out=table_scales[at : at + count, :], in_=scale_rows[first : first + count, :])
         nc.sync.dma_start(out=wg_raw[:], in_=wg_words.rearrange("a p c -> p a c").bitcast(I32))
-        load_table(0, 58)
-        for q in range(4):
+        load_table(0)
+        for q in QUADRANT_ORDER:
             nc.sync.dma_start(
                 out=wg_scales_raw[32 * q : 32 * q + 4, :, :],
                 in_=wg_scales[:, 4 * q : 4 * q + 4, :].rearrange("a r c -> r a c").bitcast(I32),
@@ -75,23 +90,22 @@ def tile_list_campaign_branch_bids_kernel(
         nc.vector.tensor_copy(picked_scales[:], table_scales[:].bitcast(U8).indirect(offsets[:]))
 
         def move_scale_rows(a, q):
-            row = first_row[a] + 4 * q
+            at = scale_row_partition(16 * a + 4 * q)
             nc.sync.dma_start(
                 out=v_plane_words[32 * q : 32 * q + 4, a, :],
-                in_=picked_scales[row : row + 4, :].bitcast(I32),
+                in_=picked_scales[at : at + 4, :].bitcast(I32),
             )
 
-        move_scale_rows(0, 0)
-        move_scale_rows(0, 1)
-        load_table(1, 0)
-        move_scale_rows(0, 2)
-        move_scale_rows(0, 3)
-        for q in range(4):
-            move_scale_rows(1, q)
-        load_table(2, 18)
-        for q in range(4):
-            move_scale_rows(2, q)
-        gains = placed([P, 2, 2 * PACK], F32, "gains", 16)
+        moves = [(a, q) for a in range(PASSES) for q in QUADRANT_ORDER]
+        for a, q in moves[:2]:
+            move_scale_rows(a, q)
+        load_table(1)
+        for a, q in moves[2:8]:
+            move_scale_rows(a, q)
+        load_table(2)
+        for a, q in moves[8:]:
+            move_scale_rows(a, q)
+        gains = placed([P, 2, 2 * PACK], F32, "gains", AT_GAINS)
         gs_sb = gains[:, 0, 0:PACK]
         gt_sb = gains[:, 1, 0:PACK]
         nc.sync.dma_start(out=gs_sb, in_=gs.rearrange("(p t) -> p t", t=PACK))
@@ -124,17 +138,17 @@ def tile_list_campaign_branch_bids_kernel(
             v_codes[a, h] = picked[:]
 
         gather_whole(0)
-        wt_raw = placed([P, PASSES, PACK, H], F32, "wt_raw", 35)
+        wt_raw = placed([P, PASSES, PACK, H], F32, "wt_raw", AT_WT)
         for a in range(PASSES):
             rows = wt[a * P * PACK : (a + 1) * P * PACK, :]
             nc.sync.dma_start(out=wt_raw[:, a, :, :], in_=rows.rearrange("(p j) c -> p j c", j=PACK))
-        wq_raw = placed([P, PACK, N], F32, "wq_raw", 60)
+        wq_raw = placed([P, PACK, N], F32, "wq_raw", AT_WQ)
         nc.sync.dma_start(out=wq_raw[:], in_=wq.rearrange("(p j) c -> p j c", j=PACK))
-        wp_codes = placed([P, N], I32, "wp_codes", 66)
+        wp_codes = placed([P, N], I32, "wp_codes", AT_WP_CODES)
         nc.sync.dma_start(out=wp_codes[:], in_=wp_words[0].rearrange("p c i -> p (c i)").bitcast(I32))
-        wp_plane = placed([P, N // 4], I32, "wp_plane", 68)
+        wp_plane = placed([P, N // 4], I32, "wp_plane", AT_WP_PLANE)
         nc.vector.memset(wp_plane[:], 0)
-        for q in range(4):
+        for q in QUADRANT_ORDER:
             nc.sync.dma_start(
                 out=wp_plane[32 * q : 32 * q + 4, :],
                 in_=wp_scales[0, 4 * q : 4 * q + 4, :].bitcast(I32),
@@ -154,27 +168,27 @@ def tile_list_campaign_branch_bids_kernel(
                     rhs=v_codes[a, h].bitcast(FP8X4),
                     rhs_scale=v_planes[a][:, h * HALF : (h + 1) * HALF],
                     start=(a == 0),
-                    stop=(a == PASSES - 1),
+                    stop=(a == LAST),
                 )
 
         def tanh_pass(d, a):
-            h, lo = divmod(d * PAIR, HALF)
+            h, lo = divmod(d * QUARTER, HALF)
             for side in range(2):
                 if a == 0:
-                    banks["tanh", d, side] = psum.tile([P, 2, PAIR], F32, name="bank")
+                    banks["tanh", d, side] = psum.tile([P, 2, QUARTER], F32, name="bank")
                 for e in range(2):
                     t = 2 * side + e
                     nc.tensor.matmul_mx(
                         out=banks["tanh", d, side][:, e, :],
                         lhsT=wt_codes[a][:, P * t : P * (t + 1)].bitcast(FP8X4),
                         lhsT_scale=wt_plane[a][:, P * t : P * (t + 1)],
-                        rhs=v_codes[a, h][:, lo : lo + PAIR].bitcast(FP8X4),
-                        rhs_scale=v_planes[a][:, d * PAIR : (d + 1) * PAIR],
+                        rhs=v_codes[a, h][:, lo : lo + QUARTER].bitcast(FP8X4),
+                        rhs_scale=v_planes[a][:, d * QUARTER : (d + 1) * QUARTER],
                         start=(a == 0 and e == 0),
-                        stop=(a == PASSES - 1 and e == 1),
+                        stop=(a == LAST and e == 1),
                     )
 
-        acts = {}
+        tanh_values = {}
         hidden = {}
         hidden_codes = {}
         hidden_plane = {}
@@ -182,59 +196,60 @@ def tile_list_campaign_branch_bids_kernel(
             for h in range(HALVES):
                 hidden_codes[branch, h] = held([P, HALF], U32, "hidden_codes_%s%d" % (branch, h))
                 hidden_plane[branch, h] = held([P, HALF], U8, "hidden_plane_%s%d" % (branch, h))
-            for d in range(UNITS // 2):
+            for d in range(QUARTERS):
                 if branch == "tanh":
-                    acts[branch, d] = held([P, 2 * UNIT * PACK], F32, "act_%s%d" % (branch, d))
-                hidden[branch, d] = held([P, 2 * UNIT * PACK], BF16, "hidden_%s%d" % (branch, d))
+                    tanh_values[d] = held([P, QUARTER * PACK], F32, "tanh_values%d" % d)
+                hidden[branch, d] = held([P, QUARTER * PACK], BF16, "hidden_%s%d" % (branch, d))
+        sigmoid_values = [held([P, PACK, HALF], F32, "sigmoid_values%d" % h) for h in range(HALVES)]
 
-        planar = [held([P, PACK, HALF], F32, "sigmoid_planar%d" % h) for h in range(HALVES)]
-
-        def activate_sigmoid(h):
+        def activate_sigmoid(h, lo, hi):
             for t in range(PACK):
-                nc.scalar.activation(out=planar[h][:, t, :], in_=banks["sigmoid", h, t][:], func=ACT.Sigmoid)
+                nc.scalar.activation(
+                    out=sigmoid_values[h][:, t, lo:hi], in_=banks["sigmoid", h, t][:, lo:hi], func=ACT.Sigmoid
+                )
 
         def activate_tanh(d):
             for side in range(2):
+                run = tanh_values[d][:, side * 2 * QUARTER : (side + 1) * 2 * QUARTER]
                 nc.scalar.activation(
-                    out=acts["tanh", d][:, side * 2 * PAIR : (side + 1) * 2 * PAIR].rearrange("p (c e) -> p c e", e=2),
+                    out=run.rearrange("p (c e) -> p c e", e=2),
                     in_=banks["tanh", d, side][:].rearrange("p e c -> p c e"),
                     func=ACT.Tanh,
                 )
 
         def gain_sigmoid(d):
-            h, lo = divmod(d * PAIR, HALF)
+            h, lo = divmod(d * QUARTER, HALF)
             nc.vector.tensor_tensor(
                 out=hidden["sigmoid", d][:].rearrange("p (c i t) -> p c t i", i=2, t=PACK),
-                in0=planar[h][:, :, lo : lo + PAIR].rearrange("p t (c i) -> p c t i", i=2),
-                in1=gs_sb.unsqueeze(1).unsqueeze(3).to_broadcast([P, PAIR // 2, PACK, 2]),
+                in0=sigmoid_values[h][:, :, lo : lo + QUARTER].rearrange("p t (c i) -> p c t i", i=2),
+                in1=gs_sb.unsqueeze(1).unsqueeze(3).to_broadcast([P, QUARTER // 2, PACK, 2]),
                 op=MULT,
             )
 
         def gain_tanh(d):
             nc.vector.tensor_tensor(
                 out=hidden["tanh", d][:].rearrange("p (c s e) -> p c s e", s=2, e=2),
-                in0=acts["tanh", d][:].rearrange("p (s c e) -> p c s e", s=2, e=2),
-                in1=gt_sb.rearrange("p (s e) -> p s e", s=2).unsqueeze(1).to_broadcast([P, PAIR, 2, 2]),
+                in0=tanh_values[d][:].rearrange("p (s c e) -> p c s e", s=2, e=2),
+                in1=gt_sb.rearrange("p (s e) -> p s e", s=2).unsqueeze(1).to_broadcast([P, QUARTER, 2, 2]),
                 op=MULT,
             )
 
-        def quantise_hidden(branch, u, count):
-            h, at = divmod(u * UNIT, HALF)
-            lo = (u % 2) * UNIT * PACK
+        def quantise_hidden(branch, d):
+            h, lo = divmod(d * QUARTER, HALF)
             nc.vector.quantize_mx(
-                out=hidden_codes[branch, h][:, at : at + count * UNIT].bitcast(FP8X4),
-                scales=hidden_plane[branch, h][:, at : at + count * UNIT],
-                in_=hidden[branch, u // 2][:, lo : lo + count * UNIT * PACK],
+                out=hidden_codes[branch, h][:, lo : lo + QUARTER].bitcast(FP8X4),
+                scales=hidden_plane[branch, h][:, lo : lo + QUARTER],
+                in_=hidden[branch, d][:],
             )
 
         wt_grouped = [held([P, H * PACK], BF16, "wt_grouped%d" % a) for a in range(PASSES)]
         wt_codes = [held([P, H], U32, "wt_codes%d" % a) for a in range(PASSES)]
         wt_plane = [held([P, H], U8, "wt_plane%d" % a) for a in range(PASSES)]
 
-        def round_wt(a, copy, u):
+        def round_wt(a, copy, side):
             dst = wt_grouped[a][:].rearrange("p (t m j) -> p m j t", t=PACK, j=PACK)
             src = wt_raw[:, a, :, :].rearrange("p j (m t) -> p m j t", t=PACK)
-            copy(out=dst[:, :, :, 2 * u : 2 * u + 2], in_=src[:, :, :, 2 * u : 2 * u + 2])
+            copy(out=dst[:, :, :, 2 * side : 2 * side + 2], in_=src[:, :, :, 2 * side : 2 * side + 2])
 
         def quantise_wt(a):
             nc.vector.quantize_mx(out=wt_codes[a][:].bitcast(FP8X4), scales=wt_plane[a][:], in_=wt_grouped[a][:])
@@ -262,69 +277,63 @@ def tile_list_campaign_branch_bids_kernel(
                 nc.scalar.copy(out=response[h][:, n, :], in_=bank[:])
 
         out_tiles = out.rearrange("(n p) c -> p n c", p=P)
-        values = {}
 
-        def value(lo, width, tiles):
-            h, at = divmod(lo, HALF)
-            values[lo, tiles] = psum.tile([P, len(tiles), width], F32, name="bank")
+        def bid(first, width, tiles):
+            h, lo = divmod(first, HALF)
+            value = psum.tile([P, len(tiles), width], F32, name="bank")
             for i, n in enumerate(tiles):
                 cols = slice(P * n, P * (n + 1))
                 nc.tensor.matmul_mx(
-                    out=values[lo, tiles][:, i, :],
+                    out=value[:, i, :],
                     lhsT=wp_codes[:, cols].bitcast(FP8X4),
                     lhsT_scale=wp_plane[:].bitcast(U8)[:, cols],
-                    rhs=hidden_codes["tanh", h][:, at : at + width].bitcast(FP8X4),
-                    rhs_scale=hidden_plane["tanh", h][:, at : at + width],
+                    rhs=hidden_codes["tanh", h][:, lo : lo + width].bitcast(FP8X4),
+                    rhs_scale=hidden_plane["tanh", h][:, lo : lo + width],
                     start=True,
                     stop=True,
                 )
-
-        def multiply_and_store(lo, width, tiles):
-            h, at = divmod(lo, HALF)
-            bids = held([P, len(tiles), width], F32, "bids%d_%d" % (lo, tiles[0]))
+            bids = held([P, len(tiles), width], F32, "bids%d_%d" % (first, tiles[0]))
             rows = slice(tiles[0], tiles[-1] + 1)
-            nc.vector.tensor_tensor(
-                out=bids[:], in0=values[lo, tiles][:], in1=response[h][:, rows, at : at + width], op=MULT
-            )
-            nc.sync.dma_start(out=out_tiles[:, rows, lo : lo + width], in_=bids[:])
+            nc.vector.tensor_tensor(out=bids[:], in0=value[:], in1=response[h][:, rows, lo : lo + width], op=MULT)
+            nc.sync.dma_start(out=out_tiles[:, rows, first : first + width], in_=bids[:])
 
         for h in range(HALVES):
-            for a in range(PASSES - 1):
+            for a in range(LAST):
                 sigmoid_pass(h, a)
-            gather_half(PASSES - 1, h)
-            sigmoid_pass(h, PASSES - 1)
-        activate_sigmoid(0)
+            gather_half(LAST, h)
+            sigmoid_pass(h, LAST)
+        activate_sigmoid(0, 0, QUARTER)
+        activate_sigmoid(0, QUARTER, HALF)
         round_wt(0, nc.vector.tensor_copy, 0)
         round_wt(0, nc.vector.tensor_copy, 1)
         round_wt(1, nc.scalar.copy, 0)
         round_wt(1, nc.scalar.copy, 1)
-        round_wt(2, nc.vector.tensor_copy, 0)
-        round_wt(2, nc.scalar.copy, 1)
+        round_wt(LAST, nc.vector.tensor_copy, 0)
+        round_wt(LAST, nc.scalar.copy, 1)
         gain_sigmoid(0)
-        quantise_wt(0)
-        quantise_wt(1)
-        quantise_wt(2)
-        activate_sigmoid(1)
         for a in range(PASSES):
-            for d in range(2):
+            quantise_wt(a)
+        activate_sigmoid(1, 0, HALF)
+        for a in range(PASSES):
+            for d in (0, 1):
                 tanh_pass(d, a)
-        for d in range(2, 4):
+        for d in (2, 3):
             for a in range(PASSES):
                 tanh_pass(d, a)
         gain_sigmoid(1)
-        quantise_hidden("sigmoid", 0, 2)
-        quantise_hidden("sigmoid", 2, 2)
+        quantise_hidden("sigmoid", 0)
+        quantise_hidden("sigmoid", 1)
         gain_sigmoid(2)
         gain_sigmoid(3)
-        quantise_hidden("sigmoid", 4, 2)
-        quantise_hidden("sigmoid", 6, 2)
+        quantise_hidden("sigmoid", 2)
+        quantise_hidden("sigmoid", 3)
         activate_tanh(0)
         activate_tanh(1)
         nc.scalar.copy(
             out=wq_grouped[:].rearrange("p (c i j) -> p c j i", i=2, j=PACK),
             in_=wq_raw[:].rearrange("p j (c i) -> p c j i", i=2),
         )
-        for lo, hi in ((0, 256), (256, N)):
+        for lo, hi in ((0, 2 * P), (2 * P, N)):
             nc.vector.quantize_mx(
                 out=wq_codes[:, lo:hi].bitcast(FP8X4),
                 scales=wq_plane[:, lo:hi],
@@ -335,15 +344,12 @@ def tile_list_campaign_branch_bids_kernel(
         respond(0)
         respond(1)
         gain_tanh(0)
-        gain_tanh(1)
-        quantise_hidden("tanh", 0, 2)
-        gain_tanh(2)
-        quantise_hidden("tanh", 2, 2)
-        gain_tanh(3)
-        quantise_hidden("tanh", 4, 2)
-        quantise_hidden("tanh", 6, 2)
-        pieces = [(0, HALF, (n,)) for n in range(SLOT_TILES)]
-        pieces = pieces + [(lo, PAIR, tiles) for lo in (HALF, HALF + PAIR) for tiles in ((0, 1), (2,))]
-        for lo, width, tiles in pieces:
-            value(lo, width, tiles)
-            multiply_and_store(lo, width, tiles)
+        for d in range(1, QUARTERS):
+            gain_tanh(d)
+            quantise_hidden("tanh", d - 1)
+        quantise_hidden("tanh", QUARTERS - 1)
+        for n in range(SLOT_TILES):
+            bid(0, HALF, (n,))
+        for first in (HALF, HALF + QUARTER):
+            for tiles in ((0, 1), (2,)):
+                bid(first, QUARTER, tiles)

@@ -1,6 +1,7 @@
 from contextlib import ExitStack
 
 import concourse.mybir as mybir
+from concourse.masks import make_identity
 
 K, T, S, H, N = 1536, 4096, 1024, 512, 384
 FLOPS = 2 * 2 * K * H * S + 2 * 2 * H * N * S
@@ -15,6 +16,7 @@ FP8X4 = mybir.dt.float8_e4m3fn_x4
 FP4X4 = mybir.dt.float4_e2m1fn_x4
 ACT = mybir.ActivationFunctionType
 MULT = mybir.AluOpType.mult
+ADD = mybir.AluOpType.add
 
 P = 128
 PACK = 4
@@ -29,10 +31,22 @@ SLOT_TILES = N // P
 AT_SCALE_WINDOW = 15
 AT_TABLE = (58, 0, 18)
 AT_GAINS = 16
-AT_WT = 35
-AT_WQ = 60
-AT_WP_CODES = 66
-AT_WP_PLANE = 68
+AT_IDENTITY = 17
+AT_GT_PADDED = 17.5
+AT_WT = (51, 59, 73)
+AT_WQ = 67
+AT_WP_CODES = 0
+AT_WP_PLANE = 2
+AT_LAST_SIGMOID = 82
+AT_TANH_1 = 85
+AT_TANH_LATE = 84
+AT_RESPONSE = 92
+AT_TANH_VALUES_1 = 88
+AT_FIRST_HIDDEN = AT_WT[0]
+
+TANH_BANKS = ((0, 2), (1, 3), (5, 6), (7, 0))
+GAIN_BANK = 4
+RESPONSE_BANKS = ((1, 2, 3), (0, 1, 2))
 
 SCALE_ROW_LOADS = ((0, 8, 40), (8, 16, 48), (24, 8, 104), (32, 16, 112))
 SCALE_WINDOW_GAPS = ((0, 40), (64, 104))
@@ -50,13 +64,16 @@ def tile_list_campaign_branch_bids_kernel(
     with ExitStack() as ctx:
         keep = ctx.enter_context(tc.tile_pool(name="keep", bufs=1))
         rooms = ctx.enter_context(tc.tile_pool(name="rooms", bufs=1))
-        psum = ctx.enter_context(tc.psum_pool(name="psum", bufs=8))
+        psum = ctx.enter_context(tc.psum_pool(name="psum", bufs=1))
 
         def held(shape, dtype, name):
             return keep.tile(shape, dtype, name=name, tag=name, align_bytes=64)
 
         def placed(shape, dtype, name, kib):
-            return rooms.tile(shape, dtype, name=name, align_bytes=64, offset=kib * 1024)
+            return rooms.tile(shape, dtype, name=name, align_bytes=64, offset=int(kib * 1024))
+
+        def in_bank(number, shape):
+            return psum.tile(shape, F32, name="bank%d" % number, tag="bank%d" % number)
 
         offsets = keep.tile([P, S // 16], U16, name="offsets")
         table = {}
@@ -79,6 +96,8 @@ def tile_list_campaign_branch_bids_kernel(
         for first, count, at in SCALE_ROW_LOADS:
             nc.sync.dma_start(out=table_scales[at : at + count, :], in_=scale_rows[first : first + count, :])
         nc.sync.dma_start(out=wg_raw[:], in_=wg_words.rearrange("a p c -> p a c").bitcast(I32))
+        gt_sb = held([P, PACK], F32, "gt_sb")
+        nc.sync.dma_start(out=gt_sb[:], in_=gt.rearrange("(p t) -> p t", t=PACK))
         load_table(0)
         for q in QUADRANT_ORDER:
             nc.sync.dma_start(
@@ -105,11 +124,19 @@ def tile_list_campaign_branch_bids_kernel(
         load_table(2)
         for a, q in moves[8:]:
             move_scale_rows(a, q)
-        gains = placed([P, 2, 2 * PACK], F32, "gains", AT_GAINS)
-        gs_sb = gains[:, 0, 0:PACK]
-        gt_sb = gains[:, 1, 0:PACK]
+        gs_tile = placed([P, PACK], F32, "gs_tile", AT_GAINS)
+        gs_sb = gs_tile[:]
         nc.sync.dma_start(out=gs_sb, in_=gs.rearrange("(p t) -> p t", t=PACK))
-        nc.sync.dma_start(out=gt_sb, in_=gt.rearrange("(p t) -> p t", t=PACK))
+
+        identity = placed([P, P], F32, "identity", AT_IDENTITY)[:]
+        gt_padded = placed([P, P], F32, "gt_padded", AT_GT_PADDED)[:]
+        make_identity(nc, identity)
+        nc.vector.memset(gt_padded, 0.0)
+        nc.vector.tensor_copy(out=gt_padded[:, 0:PACK], in_=gt_sb[:])
+        gt_turned = held([P, P], F32, "gt_turned")
+        first_turn = in_bank(7, [P, P])
+        nc.tensor.transpose(first_turn[:], gt_padded, identity)
+        nc.vector.tensor_copy(out=gt_turned[:], in_=first_turn[:])
         v_planes = [v_plane_words[:, a, :].bitcast(U8) for a in range(PASSES)]
 
         wg_codes = held([P, PASSES, 2 * H], U8, "wg_codes")
@@ -138,12 +165,13 @@ def tile_list_campaign_branch_bids_kernel(
             v_codes[a, h] = picked[:]
 
         gather_whole(0)
-        wt_raw = placed([P, PASSES, PACK, H], F32, "wt_raw", AT_WT)
+        wt_raw = [placed([P, PACK, H], F32, "wt_raw%d" % a, AT_WT[a]) for a in range(PASSES)]
         for a in range(PASSES):
             rows = wt[a * P * PACK : (a + 1) * P * PACK, :]
-            nc.sync.dma_start(out=wt_raw[:, a, :, :], in_=rows.rearrange("(p j) c -> p j c", j=PACK))
+            nc.sync.dma_start(out=wt_raw[a][:], in_=rows.rearrange("(p j) c -> p j c", j=PACK))
         wq_raw = placed([P, PACK, N], F32, "wq_raw", AT_WQ)
         nc.sync.dma_start(out=wq_raw[:], in_=wq.rearrange("(p j) c -> p j c", j=PACK))
+        gather_whole(1)
         wp_codes = placed([P, N], I32, "wp_codes", AT_WP_CODES)
         nc.sync.dma_start(out=wp_codes[:], in_=wp_words[0].rearrange("p c i -> p (c i)").bitcast(I32))
         wp_plane = placed([P, N // 4], I32, "wp_plane", AT_WP_PLANE)
@@ -153,14 +181,13 @@ def tile_list_campaign_branch_bids_kernel(
                 out=wp_plane[32 * q : 32 * q + 4, :],
                 in_=wp_scales[0, 4 * q : 4 * q + 4, :].bitcast(I32),
             )
-        gather_whole(1)
 
         banks = {}
 
         def sigmoid_pass(h, a):
             for t in range(PACK):
                 if a == 0:
-                    banks["sigmoid", h, t] = psum.tile([P, HALF], F32, name="bank")
+                    banks["sigmoid", h, t] = in_bank(PACK * h + t, [P, HALF])
                 nc.tensor.matmul_mx(
                     out=banks["sigmoid", h, t][:],
                     lhsT=wg_codes[:, a, 2 * P * t : 2 * P * (t + 1)].bitcast(FP4X4),
@@ -171,22 +198,20 @@ def tile_list_campaign_branch_bids_kernel(
                     stop=(a == LAST),
                 )
 
-        def tanh_pass(d, a):
+        def tanh_pass(d, side, a):
             h, lo = divmod(d * QUARTER, HALF)
-            for side in range(2):
-                if a == 0:
-                    banks["tanh", d, side] = psum.tile([P, 2, QUARTER], F32, name="bank")
-                for e in range(2):
-                    t = 2 * side + e
-                    nc.tensor.matmul_mx(
-                        out=banks["tanh", d, side][:, e, :],
-                        lhsT=wt_codes[a][:, P * t : P * (t + 1)].bitcast(FP8X4),
-                        lhsT_scale=wt_plane[a][:, P * t : P * (t + 1)],
-                        rhs=v_codes[a, h][:, lo : lo + QUARTER].bitcast(FP8X4),
-                        rhs_scale=v_planes[a][:, d * QUARTER : (d + 1) * QUARTER],
-                        start=(a == 0 and e == 0),
-                        stop=(a == LAST and e == 1),
-                    )
+            if a == 0:
+                banks["tanh", d, side] = in_bank(TANH_BANKS[d][side], [P, 2, QUARTER])
+            for e in range(2):
+                nc.tensor.matmul_mx(
+                    out=banks["tanh", d, side][:, e, :],
+                    lhsT=wt_codes[a, side][:, P * e : P * (e + 1)].bitcast(FP8X4),
+                    lhsT_scale=wt_plane[a, side][:, P * e : P * (e + 1)],
+                    rhs=v_codes[a, h][:, lo : lo + QUARTER].bitcast(FP8X4),
+                    rhs_scale=v_planes[a][:, d * QUARTER : (d + 1) * QUARTER],
+                    start=(a == 0 and e == 0),
+                    stop=(a == LAST and e == 1),
+                )
 
         tanh_values = {}
         hidden = {}
@@ -194,12 +219,28 @@ def tile_list_campaign_branch_bids_kernel(
         hidden_plane = {}
         for branch in ("sigmoid", "tanh"):
             for h in range(HALVES):
-                hidden_codes[branch, h] = held([P, HALF], U32, "hidden_codes_%s%d" % (branch, h))
+                if (branch, h) == ("tanh", 0):
+                    hidden_codes[branch, h] = placed([P, HALF], U32, "hidden_codes_first", AT_TANH_VALUES_1)
+                elif branch == "tanh":
+                    hidden_codes[branch, h] = placed([P, HALF], U32, "hidden_codes_last", AT_RESPONSE)
+                else:
+                    hidden_codes[branch, h] = held([P, HALF], U32, "hidden_codes_%s%d" % (branch, h))
                 hidden_plane[branch, h] = held([P, HALF], U8, "hidden_plane_%s%d" % (branch, h))
-            for d in range(QUARTERS):
-                if branch == "tanh":
-                    tanh_values[d] = held([P, QUARTER * PACK], F32, "tanh_values%d" % d)
-                hidden[branch, d] = held([P, QUARTER * PACK], BF16, "hidden_%s%d" % (branch, d))
+        width = QUARTER * PACK
+        hidden["sigmoid", 0] = placed([P, width], BF16, "hidden_first", AT_FIRST_HIDDEN)[:]
+        for d in range(1, QUARTERS - 1):
+            hidden["sigmoid", d] = held([P, width], BF16, "hidden_sigmoid%d" % d)[:]
+        hidden["sigmoid", QUARTERS - 1] = placed([P, width], BF16, "hidden_sigmoid_last", AT_LAST_SIGMOID)[:]
+        hidden["tanh", 0] = held([P, width], BF16, "hidden_tanh0")[:]
+        hidden["tanh", 1] = placed([P, width], BF16, "hidden_tanh1", AT_TANH_1)[:]
+        hidden_late = placed([P, 2 * width], BF16, "hidden_late", AT_TANH_LATE)
+        hidden["tanh", 2] = hidden_late[:, 0:width]
+        hidden["tanh", 3] = hidden_late[:, width : 2 * width]
+        for d in range(QUARTERS):
+            if d == 1:
+                tanh_values[d] = placed([P, width], F32, "tanh_values1", AT_TANH_VALUES_1)
+            else:
+                tanh_values[d] = held([P, width], F32, "tanh_values%d" % d)
         sigmoid_values = [held([P, PACK, HALF], F32, "sigmoid_values%d" % h) for h in range(HALVES)]
 
         def activate_sigmoid(h, lo, hi):
@@ -220,17 +261,17 @@ def tile_list_campaign_branch_bids_kernel(
         def gain_sigmoid(d):
             h, lo = divmod(d * QUARTER, HALF)
             nc.vector.tensor_tensor(
-                out=hidden["sigmoid", d][:].rearrange("p (c i t) -> p c t i", i=2, t=PACK),
+                out=hidden["sigmoid", d].rearrange("p (c i t) -> p c t i", i=2, t=PACK),
                 in0=sigmoid_values[h][:, :, lo : lo + QUARTER].rearrange("p t (c i) -> p c t i", i=2),
                 in1=gs_sb.unsqueeze(1).unsqueeze(3).to_broadcast([P, QUARTER // 2, PACK, 2]),
                 op=MULT,
             )
 
-        def gain_tanh(d):
-            nc.vector.tensor_tensor(
-                out=hidden["tanh", d][:].rearrange("p (c s e) -> p c s e", s=2, e=2),
+        def gain_tanh(d, engine, gain):
+            engine.tensor_tensor(
+                out=hidden["tanh", d].rearrange("p (c s e) -> p c s e", s=2, e=2),
                 in0=tanh_values[d][:].rearrange("p (s c e) -> p c s e", s=2, e=2),
-                in1=gt_sb.rearrange("p (s e) -> p s e", s=2).unsqueeze(1).to_broadcast([P, QUARTER, 2, 2]),
+                in1=gain.rearrange("p (s e) -> p s e", s=2).unsqueeze(1).to_broadcast([P, QUARTER, 2, 2]),
                 op=MULT,
             )
 
@@ -239,32 +280,46 @@ def tile_list_campaign_branch_bids_kernel(
             nc.vector.quantize_mx(
                 out=hidden_codes[branch, h][:, lo : lo + QUARTER].bitcast(FP8X4),
                 scales=hidden_plane[branch, h][:, lo : lo + QUARTER],
-                in_=hidden[branch, d][:],
+                in_=hidden[branch, d],
             )
 
-        wt_grouped = [held([P, H * PACK], BF16, "wt_grouped%d" % a) for a in range(PASSES)]
-        wt_codes = [held([P, H], U32, "wt_codes%d" % a) for a in range(PASSES)]
-        wt_plane = [held([P, H], U8, "wt_plane%d" % a) for a in range(PASSES)]
+        wt_grouped = {}
+        wt_codes = {}
+        wt_plane = {}
+        for a in range(PASSES):
+            for side in range(2):
+                wt_grouped[a, side] = held([P, 2 * P * PACK], BF16, "wt_grouped%d_%d" % (a, side))
+                wt_codes[a, side] = held([P, 2 * P], U32, "wt_codes%d_%d" % (a, side))
+                wt_plane[a, side] = held([P, 2 * P], U8, "wt_plane%d_%d" % (a, side))
 
-        def round_wt(a, copy, side):
-            dst = wt_grouped[a][:].rearrange("p (t m j) -> p m j t", t=PACK, j=PACK)
-            src = wt_raw[:, a, :, :].rearrange("p j (m t) -> p m j t", t=PACK)
-            copy(out=dst[:, :, :, 2 * side : 2 * side + 2], in_=src[:, :, :, 2 * side : 2 * side + 2])
+        def round_wt(a, side, copy):
+            dst = wt_grouped[a, side][:].rearrange("p (e m j) -> p m j e", e=2, j=PACK)
+            src = wt_raw[a][:].rearrange("p j (m t) -> p m j t", t=PACK)
+            copy(out=dst, in_=src[:, :, :, 2 * side : 2 * side + 2])
 
-        def quantise_wt(a):
-            nc.vector.quantize_mx(out=wt_codes[a][:].bitcast(FP8X4), scales=wt_plane[a][:], in_=wt_grouped[a][:])
+        def quantise_wt(a, side):
+            nc.vector.quantize_mx(
+                out=wt_codes[a, side][:].bitcast(FP8X4), scales=wt_plane[a, side][:], in_=wt_grouped[a, side][:]
+            )
 
-        wq_grouped = held([P, N * PACK], BF16, "wq_grouped")
         wq_codes = held([P, N], U32, "wq_codes")
         wq_plane = held([P, N], U8, "wq_plane")
 
         response = {}
 
         def respond(h):
-            response[h] = held([P, SLOT_TILES, HALF], F32, "response%d" % h)
+            if h == 1:
+                whole = held([P, SLOT_TILES, HALF], F32, "response1")
+                response[h, 0, 2] = whole[:, 0:2, :]
             for n in range(SLOT_TILES):
+                if h == 1:
+                    response[h, n, n + 1] = whole[:, n : n + 1, :]
+                elif n == 1:
+                    response[h, n, n + 1] = placed([P, 1, HALF], F32, "response_held", AT_RESPONSE)[:]
+                else:
+                    response[h, n, n + 1] = held([P, 1, HALF], F32, "response0_%d" % n)[:]
                 cols = slice(P * n, P * (n + 1))
-                bank = psum.tile([P, HALF], F32, name="bank")
+                bank = in_bank(RESPONSE_BANKS[h][n], [P, HALF])
                 nc.tensor.matmul_mx(
                     out=bank[:],
                     lhsT=wq_codes[:, cols].bitcast(FP8X4),
@@ -274,13 +329,16 @@ def tile_list_campaign_branch_bids_kernel(
                     start=True,
                     stop=True,
                 )
-                nc.scalar.copy(out=response[h][:, n, :], in_=bank[:])
+                nc.scalar.copy(out=response[h, n, n + 1][:, 0, :], in_=bank[:])
 
         out_tiles = out.rearrange("(n p) c -> p n c", p=P)
 
-        def bid(first, width, tiles):
+        values = {}
+
+        def project(first, width, tiles, number):
             h, lo = divmod(first, HALF)
-            value = psum.tile([P, len(tiles), width], F32, name="bank")
+            value = in_bank(number, [P, len(tiles), width])
+            values[first, tiles] = value
             for i, n in enumerate(tiles):
                 cols = slice(P * n, P * (n + 1))
                 nc.tensor.matmul_mx(
@@ -292,9 +350,13 @@ def tile_list_campaign_branch_bids_kernel(
                     start=True,
                     stop=True,
                 )
+
+        def bid(first, width, tiles):
+            h, lo = divmod(first, HALF)
+            value = values[first, tiles]
             bids = held([P, len(tiles), width], F32, "bids%d_%d" % (first, tiles[0]))
             rows = slice(tiles[0], tiles[-1] + 1)
-            nc.vector.tensor_tensor(out=bids[:], in0=value[:], in1=response[h][:, rows, lo : lo + width], op=MULT)
+            nc.vector.tensor_tensor(out=bids[:], in0=value[:], in1=response[h, tiles[0], tiles[-1] + 1][:, :, lo : lo + width], op=MULT)
             nc.sync.dma_start(out=out_tiles[:, rows, first : first + width], in_=bids[:])
 
         for h in range(HALVES):
@@ -304,22 +366,25 @@ def tile_list_campaign_branch_bids_kernel(
             sigmoid_pass(h, LAST)
         activate_sigmoid(0, 0, QUARTER)
         activate_sigmoid(0, QUARTER, HALF)
-        round_wt(0, nc.vector.tensor_copy, 0)
-        round_wt(0, nc.vector.tensor_copy, 1)
-        round_wt(1, nc.scalar.copy, 0)
-        round_wt(1, nc.scalar.copy, 1)
-        round_wt(LAST, nc.vector.tensor_copy, 0)
-        round_wt(LAST, nc.scalar.copy, 1)
-        gain_sigmoid(0)
-        for a in range(PASSES):
-            quantise_wt(a)
         activate_sigmoid(1, 0, HALF)
-        for a in range(PASSES):
+        round_wt(0, 0, nc.vector.tensor_copy)
+        round_wt(0, 1, nc.vector.tensor_copy)
+        round_wt(1, 0, nc.scalar.copy)
+        round_wt(1, 1, nc.scalar.copy)
+        round_wt(LAST, 0, nc.vector.tensor_copy)
+        round_wt(LAST, 1, nc.scalar.copy)
+        gain_sigmoid(0)
+        wt_order = [(0, 0), (0, 1)] + [(a, side) for side in range(2) for a in range(1, PASSES)]
+        for a, side in wt_order:
+            quantise_wt(a, side)
+        for a, side in wt_order:
             for d in (0, 1):
-                tanh_pass(d, a)
-        for d in (2, 3):
+                tanh_pass(d, side, a)
+        gt_bank = in_bank(GAIN_BANK, [P, P])
+        nc.tensor.transpose(gt_bank[:], gt_turned[:], identity)
+        for d, side in ((2, 0), (2, 1), (3, 0)):
             for a in range(PASSES):
-                tanh_pass(d, a)
+                tanh_pass(d, side, a)
         gain_sigmoid(1)
         quantise_hidden("sigmoid", 0)
         quantise_hidden("sigmoid", 1)
@@ -328,28 +393,43 @@ def tile_list_campaign_branch_bids_kernel(
         quantise_hidden("sigmoid", 2)
         quantise_hidden("sigmoid", 3)
         activate_tanh(0)
-        activate_tanh(1)
-        nc.scalar.copy(
-            out=wq_grouped[:].rearrange("p (c i j) -> p c j i", i=2, j=PACK),
-            in_=wq_raw[:].rearrange("p j (c i) -> p c j i", i=2),
+        for a in range(PASSES):
+            tanh_pass(3, 1, a)
+        for d in range(1, QUARTERS):
+            activate_tanh(d)
+        wq_grouped = placed([P, N * PACK], BF16, "wq_grouped", AT_LAST_SIGMOID)
+        nc.gpsimd.tensor_scalar(
+            out=wq_grouped[:].rearrange("p (c j) -> p c j", j=PACK),
+            in0=wq_raw[:].rearrange("p j c -> p c j"),
+            scalar1=1.0,
+            scalar2=0.0,
+            op0=MULT,
+            op1=ADD,
         )
+        gain_tanh(0, nc.vector, gt_bank[:, 0:PACK])
+        gain_tanh(1, nc.vector, gt_bank[:, 0:PACK])
         for lo, hi in ((0, 2 * P), (2 * P, N)):
             nc.vector.quantize_mx(
                 out=wq_codes[:, lo:hi].bitcast(FP8X4),
                 scales=wq_plane[:, lo:hi],
                 in_=wq_grouped[:, PACK * lo : PACK * hi],
             )
-        activate_tanh(2)
-        activate_tanh(3)
         respond(0)
-        respond(1)
-        gain_tanh(0)
-        for d in range(1, QUARTERS):
-            gain_tanh(d)
-            quantise_hidden("tanh", d - 1)
-        quantise_hidden("tanh", QUARTERS - 1)
+        quantise_hidden("tanh", 0)
+        quantise_hidden("tanh", 1)
         for n in range(SLOT_TILES):
-            bid(0, HALF, (n,))
-        for first in (HALF, HALF + QUARTER):
-            for tiles in ((0, 1), (2,)):
-                bid(first, QUARTER, tiles)
+            project(0, HALF, (n,), 5 + n)
+        respond(1)
+        gain_tanh(2, nc.vector, gt_bank[:, 0:PACK])
+        gain_tanh(3, nc.gpsimd, gt_sb[:])
+        bid(0, HALF, (0,))
+        bid(0, HALF, (1,))
+        nc.vector.quantize_mx(
+            out=hidden_codes["tanh", 1][:].bitcast(FP8X4), scales=hidden_plane["tanh", 1][:], in_=hidden_late[:]
+        )
+        last_pieces = [(first, tiles) for first in (HALF, HALF + QUARTER) for tiles in ((0, 1), (2,))]
+        for i, (first, tiles) in enumerate(last_pieces):
+            project(first, QUARTER, tiles, 3 + i)
+        bid(0, HALF, (2,))
+        for first, tiles in last_pieces:
+            bid(first, QUARTER, tiles)

@@ -16,7 +16,6 @@ FP8X4 = mybir.dt.float8_e4m3fn_x4
 FP4X4 = mybir.dt.float4_e2m1fn_x4
 ACT = mybir.ActivationFunctionType
 MULT = mybir.AluOpType.mult
-ADD = mybir.AluOpType.add
 
 P = 128
 PACK = 4
@@ -30,26 +29,34 @@ SLOT_TILES = N // P
 
 AT_SCALE_WINDOW = 15
 AT_TABLE = (58, 0, 18)
-AT_GAINS = 16
 AT_IDENTITY = 17
-AT_GT_PADDED = 17.5
+AT_GAINS_PADDED = 17.5
 AT_WT = (51, 59, 73)
 AT_WQ = 67
 AT_WP_CODES = 0
 AT_WP_PLANE = 2
-AT_LAST_SIGMOID = 82
-AT_TANH_1 = 85
-AT_TANH_LATE = 84
-AT_RESPONSE = 92
-AT_TANH_VALUES_1 = 88
-AT_FIRST_HIDDEN = AT_WT[0]
+AT_ROUNDED_1 = 84
+AT_SIGMOID = (83, 85, 88, 88)
+AT_SIGMOID_VALUES = 90
+AT_LAST_WT_CODES = (90, 91)
+AT_B_CODES = (92, 94)
+AT_WQ_CODES = 96
+AT_TANH_VALUES_1 = 100
+AT_FIRST_A_CODES = 100
+AT_LAST_B_CODES = 102
+AT_TANH_1 = 106
+AT_TANH_LATE = 106
+AT_RESPONSE = 110
+GPSIMD_SHARE = 208
 
-TANH_BANKS = ((0, 2), (1, 3), (5, 6), (7, 0))
-GAIN_BANK = 4
-RESPONSE_BANKS = ((1, 2, 3), (0, 1, 2))
+TANH_BANKS = ((1, 3), (2, 4), (5, 6), (1, 3))
+GAIN_BANK = 0
+RESPONSE_BANKS = ((5, 6, 1), (3, 5, 2))
+VALUE_BANKS = ((2, 4, 5), (1, 0, 7))
+CROSSED = 2
 
-SCALE_ROW_LOADS = ((0, 8, 40), (8, 16, 48), (24, 8, 104), (32, 16, 112))
-SCALE_WINDOW_GAPS = ((0, 40), (64, 104))
+SCALE_ROW_LOADS = ((0, 16, 48), (16, 32, 96))
+SCALE_WINDOW_GAPS = ((0, 48), (64, 96))
 QUADRANT_ORDER = (0, 2, 1, 3)
 
 
@@ -96,8 +103,11 @@ def tile_list_campaign_branch_bids_kernel(
         for first, count, at in SCALE_ROW_LOADS:
             nc.sync.dma_start(out=table_scales[at : at + count, :], in_=scale_rows[first : first + count, :])
         nc.sync.dma_start(out=wg_raw[:], in_=wg_words.rearrange("a p c -> p a c").bitcast(I32))
-        gt_sb = held([P, PACK], F32, "gt_sb")
-        nc.sync.dma_start(out=gt_sb[:], in_=gt.rearrange("(p t) -> p t", t=PACK))
+        gains = held([P, 2, 2 * PACK], F32, "gains")
+        gs_sb = gains[:, 0, 0:PACK]
+        gt_sb = gains[:, 1, 0:PACK]
+        nc.sync.dma_start(out=gs_sb, in_=gs.rearrange("(p t) -> p t", t=PACK))
+        nc.sync.dma_start(out=gt_sb, in_=gt.rearrange("(p t) -> p t", t=PACK))
         load_table(0)
         for q in QUADRANT_ORDER:
             nc.sync.dma_start(
@@ -124,19 +134,18 @@ def tile_list_campaign_branch_bids_kernel(
         load_table(2)
         for a, q in moves[8:]:
             move_scale_rows(a, q)
-        gs_tile = placed([P, PACK], F32, "gs_tile", AT_GAINS)
-        gs_sb = gs_tile[:]
-        nc.sync.dma_start(out=gs_sb, in_=gs.rearrange("(p t) -> p t", t=PACK))
 
         identity = placed([P, P], F32, "identity", AT_IDENTITY)[:]
-        gt_padded = placed([P, P], F32, "gt_padded", AT_GT_PADDED)[:]
+        gains_padded = placed([P, P], F32, "gains_padded", AT_GAINS_PADDED)[:]
         make_identity(nc, identity)
-        nc.vector.memset(gt_padded, 0.0)
-        nc.vector.tensor_copy(out=gt_padded[:, 0:PACK], in_=gt_sb[:])
-        gt_turned = held([P, P], F32, "gt_turned")
+        nc.vector.memset(gains_padded, 0.0)
+        nc.vector.tensor_copy(
+            out=gains_padded[:, 0 : 2 * PACK].rearrange("p (b t) -> p b t", t=PACK), in_=gains[:, :, 0:PACK]
+        )
+        gains_turned = held([P, P], F32, "gains_turned")
         first_turn = in_bank(7, [P, P])
-        nc.tensor.transpose(first_turn[:], gt_padded, identity)
-        nc.vector.tensor_copy(out=gt_turned[:], in_=first_turn[:])
+        nc.tensor.transpose(first_turn[:], gains_padded, identity)
+        nc.vector.tensor_copy(out=gains_turned[:], in_=first_turn[:])
         v_planes = [v_plane_words[:, a, :].bitcast(U8) for a in range(PASSES)]
 
         wg_codes = held([P, PASSES, 2 * H], U8, "wg_codes")
@@ -203,10 +212,11 @@ def tile_list_campaign_branch_bids_kernel(
             if a == 0:
                 banks["tanh", d, side] = in_bank(TANH_BANKS[d][side], [P, 2, QUARTER])
             for e in range(2):
+                piece, tile = (e, side) if d == CROSSED else (side, e)
                 nc.tensor.matmul_mx(
                     out=banks["tanh", d, side][:, e, :],
-                    lhsT=wt_codes[a, side][:, P * e : P * (e + 1)].bitcast(FP8X4),
-                    lhsT_scale=wt_plane[a, side][:, P * e : P * (e + 1)],
+                    lhsT=wt_codes[a, piece][:, P * tile : P * (tile + 1)].bitcast(FP8X4),
+                    lhsT_scale=wt_plane[a, piece][:, P * tile : P * (tile + 1)],
                     rhs=v_codes[a, h][:, lo : lo + QUARTER].bitcast(FP8X4),
                     rhs_scale=v_planes[a][:, d * QUARTER : (d + 1) * QUARTER],
                     start=(a == 0 and e == 0),
@@ -217,20 +227,19 @@ def tile_list_campaign_branch_bids_kernel(
         hidden = {}
         hidden_codes = {}
         hidden_plane = {}
-        for branch in ("sigmoid", "tanh"):
-            for h in range(HALVES):
-                if (branch, h) == ("tanh", 0):
-                    hidden_codes[branch, h] = placed([P, HALF], U32, "hidden_codes_first", AT_TANH_VALUES_1)
-                elif branch == "tanh":
-                    hidden_codes[branch, h] = placed([P, HALF], U32, "hidden_codes_last", AT_RESPONSE)
-                else:
-                    hidden_codes[branch, h] = held([P, HALF], U32, "hidden_codes_%s%d" % (branch, h))
-                hidden_plane[branch, h] = held([P, HALF], U8, "hidden_plane_%s%d" % (branch, h))
+        codes_at = {
+            ("sigmoid", 0): AT_B_CODES[0],
+            ("sigmoid", 1): AT_B_CODES[1],
+            ("tanh", 0): AT_FIRST_A_CODES,
+            ("tanh", 1): AT_RESPONSE,
+        }
+        for (branch, h), at in codes_at.items():
+            hidden_codes[branch, h] = placed([P, HALF], U32, "hidden_codes_%s%d" % (branch, h), at)
+            hidden_plane[branch, h] = held([P, HALF], U8, "hidden_plane_%s%d" % (branch, h))
+        b_codes = [hidden_codes["sigmoid", 1][:, 0:QUARTER], placed([P, QUARTER], U32, "b_codes_last", AT_LAST_B_CODES)[:]]
         width = QUARTER * PACK
-        hidden["sigmoid", 0] = placed([P, width], BF16, "hidden_first", AT_FIRST_HIDDEN)[:]
-        for d in range(1, QUARTERS - 1):
-            hidden["sigmoid", d] = held([P, width], BF16, "hidden_sigmoid%d" % d)[:]
-        hidden["sigmoid", QUARTERS - 1] = placed([P, width], BF16, "hidden_sigmoid_last", AT_LAST_SIGMOID)[:]
+        for d in range(QUARTERS):
+            hidden["sigmoid", d] = placed([P, width], BF16, "hidden_sigmoid%d" % d, AT_SIGMOID[d])[:]
         hidden["tanh", 0] = held([P, width], BF16, "hidden_tanh0")[:]
         hidden["tanh", 1] = placed([P, width], BF16, "hidden_tanh1", AT_TANH_1)[:]
         hidden_late = placed([P, 2 * width], BF16, "hidden_late", AT_TANH_LATE)
@@ -241,7 +250,10 @@ def tile_list_campaign_branch_bids_kernel(
                 tanh_values[d] = placed([P, width], F32, "tanh_values1", AT_TANH_VALUES_1)
             else:
                 tanh_values[d] = held([P, width], F32, "tanh_values%d" % d)
-        sigmoid_values = [held([P, PACK, HALF], F32, "sigmoid_values%d" % h) for h in range(HALVES)]
+        sigmoid_values = [
+            placed([P, PACK, HALF], F32, "sigmoid_values0", AT_SIGMOID_VALUES),
+            held([P, PACK, HALF], F32, "sigmoid_values1"),
+        ]
 
         def activate_sigmoid(h, lo, hi):
             for t in range(PACK):
@@ -258,27 +270,39 @@ def tile_list_campaign_branch_bids_kernel(
                     func=ACT.Tanh,
                 )
 
-        def gain_sigmoid(d):
+        def gain_sigmoid(d, first):
             h, lo = divmod(d * QUARTER, HALF)
             nc.vector.tensor_tensor(
-                out=hidden["sigmoid", d].rearrange("p (c i t) -> p c t i", i=2, t=PACK),
-                in0=sigmoid_values[h][:, :, lo : lo + QUARTER].rearrange("p t (c i) -> p c t i", i=2),
-                in1=gs_sb.unsqueeze(1).unsqueeze(3).to_broadcast([P, QUARTER // 2, PACK, 2]),
+                out=hidden["sigmoid", d][:, PACK * first :].rearrange("p (c i t) -> p c t i", i=2, t=PACK),
+                in0=sigmoid_values[h][:, :, lo + first : lo + QUARTER].rearrange("p t (c i) -> p c t i", i=2),
+                in1=gain_bank[:, 0:PACK].unsqueeze(1).unsqueeze(3).to_broadcast([P, (QUARTER - first) // 2, PACK, 2]),
                 op=MULT,
             )
 
+        def gain_sigmoid_shared(d):
+            h, lo = divmod(d * QUARTER, HALF)
+            nc.gpsimd.tensor_tensor(
+                out=hidden["sigmoid", d][:, 0 : PACK * GPSIMD_SHARE].rearrange("p (c t) -> p c t", t=PACK),
+                in0=sigmoid_values[h][:, :, lo : lo + GPSIMD_SHARE].rearrange("p t c -> p c t"),
+                in1=gs_sb.unsqueeze(1).to_broadcast([P, GPSIMD_SHARE, PACK]),
+                op=MULT,
+            )
+            gain_sigmoid(d, GPSIMD_SHARE)
+
         def gain_tanh(d, engine, gain):
+            order = "e s" if d == CROSSED else "s e"
             engine.tensor_tensor(
-                out=hidden["tanh", d].rearrange("p (c s e) -> p c s e", s=2, e=2),
+                out=hidden["tanh", d].rearrange("p (c %s) -> p c s e" % order, s=2, e=2),
                 in0=tanh_values[d][:].rearrange("p (s c e) -> p c s e", s=2, e=2),
-                in1=gain.rearrange("p (s e) -> p s e", s=2).unsqueeze(1).to_broadcast([P, QUARTER, 2, 2]),
+                in1=gain.rearrange("p (%s) -> p s e" % order, s=2, e=2).unsqueeze(1).to_broadcast([P, QUARTER, 2, 2]),
                 op=MULT,
             )
 
         def quantise_hidden(branch, d):
             h, lo = divmod(d * QUARTER, HALF)
+            codes = b_codes[d - 2] if (branch, h) == ("sigmoid", 1) else hidden_codes[branch, h][:, lo : lo + QUARTER]
             nc.vector.quantize_mx(
-                out=hidden_codes[branch, h][:, lo : lo + QUARTER].bitcast(FP8X4),
+                out=codes.bitcast(FP8X4),
                 scales=hidden_plane[branch, h][:, lo : lo + QUARTER],
                 in_=hidden[branch, d],
             )
@@ -288,8 +312,14 @@ def tile_list_campaign_branch_bids_kernel(
         wt_plane = {}
         for a in range(PASSES):
             for side in range(2):
-                wt_grouped[a, side] = held([P, 2 * P * PACK], BF16, "wt_grouped%d_%d" % (a, side))
-                wt_codes[a, side] = held([P, 2 * P], U32, "wt_codes%d_%d" % (a, side))
+                if (a, side) == (1, 1):
+                    wt_grouped[a, side] = placed([P, 2 * P * PACK], BF16, "wt_grouped_held", AT_ROUNDED_1)
+                else:
+                    wt_grouped[a, side] = held([P, 2 * P * PACK], BF16, "wt_grouped%d_%d" % (a, side))
+                if a == LAST:
+                    wt_codes[a, side] = placed([P, 2 * P], U32, "wt_codes_last%d" % side, AT_LAST_WT_CODES[side])
+                else:
+                    wt_codes[a, side] = held([P, 2 * P], U32, "wt_codes%d_%d" % (a, side))
                 wt_plane[a, side] = held([P, 2 * P], U8, "wt_plane%d_%d" % (a, side))
 
         def round_wt(a, side, copy):
@@ -302,134 +332,127 @@ def tile_list_campaign_branch_bids_kernel(
                 out=wt_codes[a, side][:].bitcast(FP8X4), scales=wt_plane[a, side][:], in_=wt_grouped[a, side][:]
             )
 
-        wq_codes = held([P, N], U32, "wq_codes")
+        wq_codes = placed([P, N], U32, "wq_codes", AT_WQ_CODES)
         wq_plane = held([P, N], U8, "wq_plane")
 
         response = {}
 
-        def respond(h):
-            if h == 1:
-                whole = held([P, SLOT_TILES, HALF], F32, "response1")
-                response[h, 0, 2] = whole[:, 0:2, :]
+        for h in range(HALVES):
             for n in range(SLOT_TILES):
-                if h == 1:
-                    response[h, n, n + 1] = whole[:, n : n + 1, :]
-                elif n == 1:
-                    response[h, n, n + 1] = placed([P, 1, HALF], F32, "response_held", AT_RESPONSE)[:]
+                if (h, n) == (0, 1):
+                    response[h, n] = placed([P, HALF], F32, "response_held", AT_RESPONSE)
                 else:
-                    response[h, n, n + 1] = held([P, 1, HALF], F32, "response0_%d" % n)[:]
+                    response[h, n] = held([P, HALF], F32, "response%d_%d" % (h, n))
+
+        def respond(h, tiles):
+            for n in tiles:
                 cols = slice(P * n, P * (n + 1))
                 bank = in_bank(RESPONSE_BANKS[h][n], [P, HALF])
-                nc.tensor.matmul_mx(
-                    out=bank[:],
-                    lhsT=wq_codes[:, cols].bitcast(FP8X4),
-                    lhsT_scale=wq_plane[:, cols],
-                    rhs=hidden_codes["sigmoid", h][:].bitcast(FP8X4),
-                    rhs_scale=hidden_plane["sigmoid", h][:],
-                    start=True,
-                    stop=True,
-                )
-                nc.scalar.copy(out=response[h, n, n + 1][:, 0, :], in_=bank[:])
-
-        out_tiles = out.rearrange("(n p) c -> p n c", p=P)
+                pieces = [hidden_codes["sigmoid", 0][:]] if h == 0 else b_codes
+                step = HALF // len(pieces)
+                for i, codes in enumerate(pieces):
+                    nc.tensor.matmul_mx(
+                        out=bank[:, i * step : (i + 1) * step],
+                        lhsT=wq_codes[:, cols].bitcast(FP8X4),
+                        lhsT_scale=wq_plane[:, cols],
+                        rhs=codes.bitcast(FP8X4),
+                        rhs_scale=hidden_plane["sigmoid", h][:, i * step : (i + 1) * step],
+                        start=True,
+                        stop=True,
+                    )
+                nc.scalar.copy(out=response[h, n][:], in_=bank[:])
 
         values = {}
 
-        def project(first, width, tiles, number):
-            h, lo = divmod(first, HALF)
-            value = in_bank(number, [P, len(tiles), width])
-            values[first, tiles] = value
-            for i, n in enumerate(tiles):
-                cols = slice(P * n, P * (n + 1))
-                nc.tensor.matmul_mx(
-                    out=value[:, i, :],
-                    lhsT=wp_codes[:, cols].bitcast(FP8X4),
-                    lhsT_scale=wp_plane[:].bitcast(U8)[:, cols],
-                    rhs=hidden_codes["tanh", h][:, lo : lo + width].bitcast(FP8X4),
-                    rhs_scale=hidden_plane["tanh", h][:, lo : lo + width],
-                    start=True,
-                    stop=True,
-                )
+        def project(h, n):
+            cols = slice(P * n, P * (n + 1))
+            values[h, n] = in_bank(VALUE_BANKS[h][n], [P, HALF])
+            nc.tensor.matmul_mx(
+                out=values[h, n][:],
+                lhsT=wp_codes[:, cols].bitcast(FP8X4),
+                lhsT_scale=wp_plane[:].bitcast(U8)[:, cols],
+                rhs=hidden_codes["tanh", h][:].bitcast(FP8X4),
+                rhs_scale=hidden_plane["tanh", h][:],
+                start=True,
+                stop=True,
+            )
 
-        def bid(first, width, tiles):
-            h, lo = divmod(first, HALF)
-            value = values[first, tiles]
-            bids = held([P, len(tiles), width], F32, "bids%d_%d" % (first, tiles[0]))
-            rows = slice(tiles[0], tiles[-1] + 1)
-            nc.vector.tensor_tensor(out=bids[:], in0=value[:], in1=response[h, tiles[0], tiles[-1] + 1][:, :, lo : lo + width], op=MULT)
-            nc.sync.dma_start(out=out_tiles[:, rows, first : first + width], in_=bids[:])
+        def bid(h, n, lo, hi):
+            bids = held([P, hi - lo], F32, "bids%d_%d_%d" % (h, n, lo))
+            nc.vector.tensor_tensor(out=bids[:], in0=values[h, n][:, lo:hi], in1=response[h, n][:, lo:hi], op=MULT)
+            nc.sync.dma_start(out=out[P * n : P * (n + 1), h * HALF + lo : h * HALF + hi], in_=bids[:])
 
         for h in range(HALVES):
             for a in range(LAST):
                 sigmoid_pass(h, a)
             gather_half(LAST, h)
             sigmoid_pass(h, LAST)
-        activate_sigmoid(0, 0, QUARTER)
-        activate_sigmoid(0, QUARTER, HALF)
-        activate_sigmoid(1, 0, HALF)
-        round_wt(0, 0, nc.vector.tensor_copy)
-        round_wt(0, 1, nc.vector.tensor_copy)
-        round_wt(1, 0, nc.scalar.copy)
-        round_wt(1, 1, nc.scalar.copy)
-        round_wt(LAST, 0, nc.vector.tensor_copy)
-        round_wt(LAST, 1, nc.scalar.copy)
-        gain_sigmoid(0)
-        wt_order = [(0, 0), (0, 1)] + [(a, side) for side in range(2) for a in range(1, PASSES)]
-        for a, side in wt_order:
-            quantise_wt(a, side)
-        for a, side in wt_order:
-            for d in (0, 1):
-                tanh_pass(d, side, a)
-        gt_bank = in_bank(GAIN_BANK, [P, P])
-        nc.tensor.transpose(gt_bank[:], gt_turned[:], identity)
-        for d, side in ((2, 0), (2, 1), (3, 0)):
-            for a in range(PASSES):
-                tanh_pass(d, side, a)
-        gain_sigmoid(1)
+        for h in range(HALVES):
+            activate_sigmoid(h, 0, HALF)
+        gain_bank = in_bank(GAIN_BANK, [P, P])
+        nc.tensor.transpose(gain_bank[:], gains_turned[:], identity)
+        gt_psum = gain_bank[:, PACK : 2 * PACK]
+        for a in range(PASSES):
+            for side in range(2):
+                round_wt(a, side, nc.scalar.copy if a == LAST else nc.vector.tensor_copy)
+            if a < LAST:
+                for side in range(2):
+                    quantise_wt(a, side)
+        wq_grouped = held([P, N * PACK], BF16, "wq_grouped")
+        nc.scalar.copy(
+            out=wq_grouped[:].rearrange("p (c i j) -> p c j i", i=2, j=PACK),
+            in_=wq_raw[:].rearrange("p j (c i) -> p c j i", i=2),
+        )
+        gain_sigmoid_shared(1)
+        gain_sigmoid(0, 0)
+        gain_sigmoid(2, 0)
+        for side in range(2):
+            quantise_wt(LAST, side)
+        for a in range(PASSES):
+            for side in range(2):
+                for d in (0, 1):
+                    tanh_pass(d, side, a)
+        for a in range(PASSES):
+            for side in range(2):
+                tanh_pass(2, side, a)
         quantise_hidden("sigmoid", 0)
         quantise_hidden("sigmoid", 1)
-        gain_sigmoid(2)
-        gain_sigmoid(3)
-        quantise_hidden("sigmoid", 2)
-        quantise_hidden("sigmoid", 3)
-        activate_tanh(0)
-        for a in range(PASSES):
-            tanh_pass(3, 1, a)
-        for d in range(1, QUARTERS):
-            activate_tanh(d)
-        wq_grouped = placed([P, N * PACK], BF16, "wq_grouped", AT_LAST_SIGMOID)
-        nc.gpsimd.tensor_scalar(
-            out=wq_grouped[:].rearrange("p (c j) -> p c j", j=PACK),
-            in0=wq_raw[:].rearrange("p j c -> p c j"),
-            scalar1=1.0,
-            scalar2=0.0,
-            op0=MULT,
-            op1=ADD,
-        )
-        gain_tanh(0, nc.vector, gt_bank[:, 0:PACK])
-        gain_tanh(1, nc.vector, gt_bank[:, 0:PACK])
         for lo, hi in ((0, 2 * P), (2 * P, N)):
             nc.vector.quantize_mx(
                 out=wq_codes[:, lo:hi].bitcast(FP8X4),
                 scales=wq_plane[:, lo:hi],
                 in_=wq_grouped[:, PACK * lo : PACK * hi],
             )
-        respond(0)
+        quantise_hidden("sigmoid", 2)
+        gain_sigmoid_shared(3)
+        activate_tanh(0)
+        for side in range(2):
+            for a in range(PASSES):
+                tanh_pass(3, side, a)
+        for d in range(1, QUARTERS):
+            activate_tanh(d)
+        gain_tanh(0, nc.vector, gt_psum)
+        gain_tanh(1, nc.vector, gt_psum)
+        quantise_hidden("sigmoid", 3)
         quantise_hidden("tanh", 0)
         quantise_hidden("tanh", 1)
-        for n in range(SLOT_TILES):
-            project(0, HALF, (n,), 5 + n)
-        respond(1)
-        gain_tanh(2, nc.vector, gt_bank[:, 0:PACK])
-        gain_tanh(3, nc.gpsimd, gt_sb[:])
-        bid(0, HALF, (0,))
-        bid(0, HALF, (1,))
+        respond(0, range(SLOT_TILES))
+        project(0, 0)
+        project(0, 1)
+        respond(1, (0, 1))
+        gain_tanh(2, nc.vector, gt_psum)
+        gain_tanh(3, nc.gpsimd, gt_sb)
+        bid(0, 0, 0, HALF)
+        respond(1, (2,))
+        project(0, 2)
+        bid(0, 1, 0, HALF)
         nc.vector.quantize_mx(
             out=hidden_codes["tanh", 1][:].bitcast(FP8X4), scales=hidden_plane["tanh", 1][:], in_=hidden_late[:]
         )
-        last_pieces = [(first, tiles) for first in (HALF, HALF + QUARTER) for tiles in ((0, 1), (2,))]
-        for i, (first, tiles) in enumerate(last_pieces):
-            project(first, QUARTER, tiles, 3 + i)
-        bid(0, HALF, (2,))
-        for first, tiles in last_pieces:
-            bid(first, QUARTER, tiles)
+        for n in range(SLOT_TILES):
+            project(1, n)
+        bid(0, 2, 0, HALF)
+        bid(1, 0, 0, HALF)
+        bid(1, 1, 0, HALF)
+        bid(1, 2, 0, QUARTER)
+        bid(1, 2, QUARTER, HALF)

@@ -16,6 +16,7 @@ FP8X4 = mybir.dt.float8_e4m3fn_x4
 FP4X4 = mybir.dt.float4_e2m1fn_x4
 ACT = mybir.ActivationFunctionType
 MULT = mybir.AluOpType.mult
+ADD = mybir.AluOpType.add
 
 P = 128
 PACK = 4
@@ -36,23 +37,25 @@ AT_WQ = 67
 AT_WP_CODES = 0
 AT_WP_PLANE = 2
 AT_ROUNDED_1 = 84
-AT_SIGMOID = (83, 85, 88, 88)
+AT_SIGMOID = (83, 85, 105, 104)
+AT_WQ_ROUNDED = 106
 AT_SIGMOID_VALUES = 90
 AT_LAST_WT_CODES = (90, 91)
 AT_B_CODES = (92, 94)
-AT_WQ_CODES = 96
 AT_TANH_VALUES_1 = 100
-AT_FIRST_A_CODES = 100
-AT_LAST_B_CODES = 102
-AT_TANH_1 = 106
-AT_TANH_LATE = 106
-AT_RESPONSE = 110
-GPSIMD_SHARE = 208
+AT_WQ_CODES = 99
+AT_LAST_B_CODES = 100.5
+AT_FIRST_A_CODES = 101.5
+AT_TANH_1 = 110
+AT_TANH_LATE = 110
+AT_RESPONSE = 114
+GPSIMD_SHARE = 176
+TANH_SHARES = (0, 80, 0, 256)
 
-TANH_BANKS = ((1, 3), (2, 4), (5, 6), (1, 3))
+TANH_BANKS = ((1, 3), (2, 4), (5, 6), (2, 4))
 GAIN_BANK = 0
-RESPONSE_BANKS = ((5, 6, 1), (3, 5, 2))
-VALUE_BANKS = ((2, 4, 5), (1, 0, 7))
+RESPONSE_BANKS = ((5, 6, 1), (2, 4, 3))
+VALUE_BANKS = ((3, 7, 4), (5, 6, 1))
 CROSSED = 2
 
 SCALE_ROW_LOADS = ((0, 16, 48), (16, 32, 96))
@@ -282,21 +285,24 @@ def tile_list_campaign_branch_bids_kernel(
         def gain_sigmoid_shared(d):
             h, lo = divmod(d * QUARTER, HALF)
             nc.gpsimd.tensor_tensor(
-                out=hidden["sigmoid", d][:, 0 : PACK * GPSIMD_SHARE].rearrange("p (c t) -> p c t", t=PACK),
-                in0=sigmoid_values[h][:, :, lo : lo + GPSIMD_SHARE].rearrange("p t c -> p c t"),
-                in1=gs_sb.unsqueeze(1).to_broadcast([P, GPSIMD_SHARE, PACK]),
+                out=hidden["sigmoid", d][:, 0 : PACK * GPSIMD_SHARE].rearrange("p (c i t) -> p c t i", i=2, t=PACK),
+                in0=sigmoid_values[h][:, :, lo : lo + GPSIMD_SHARE].rearrange("p t (c i) -> p c t i", i=2),
+                in1=gs_sb.unsqueeze(1).unsqueeze(3).to_broadcast([P, GPSIMD_SHARE // 2, PACK, 2]),
                 op=MULT,
             )
             gain_sigmoid(d, GPSIMD_SHARE)
 
-        def gain_tanh(d, engine, gain):
+        def gain_tanh(d):
             order = "e s" if d == CROSSED else "s e"
-            engine.tensor_tensor(
-                out=hidden["tanh", d].rearrange("p (c %s) -> p c s e" % order, s=2, e=2),
-                in0=tanh_values[d][:].rearrange("p (s c e) -> p c s e", s=2, e=2),
-                in1=gain.rearrange("p (%s) -> p s e" % order, s=2, e=2).unsqueeze(1).to_broadcast([P, QUARTER, 2, 2]),
-                op=MULT,
-            )
+            share = TANH_SHARES[d]
+            for engine, gain, lo, hi in ((nc.gpsimd, gt_sb, 0, share), (nc.vector, gt_psum, share, QUARTER)):
+                if lo < hi:
+                    engine.tensor_tensor(
+                        out=hidden["tanh", d].rearrange("p (c %s) -> p c s e" % order, s=2, e=2)[:, lo:hi, :, :],
+                        in0=tanh_values[d][:].rearrange("p (s c e) -> p c s e", s=2, e=2)[:, lo:hi, :, :],
+                        in1=gain.rearrange("p (%s) -> p s e" % order, s=2, e=2).unsqueeze(1).to_broadcast([P, hi - lo, 2, 2]),
+                        op=MULT,
+                    )
 
         def quantise_hidden(branch, d):
             h, lo = divmod(d * QUARTER, HALF)
@@ -398,11 +404,6 @@ def tile_list_campaign_branch_bids_kernel(
             if a < LAST:
                 for side in range(2):
                     quantise_wt(a, side)
-        wq_grouped = held([P, N * PACK], BF16, "wq_grouped")
-        nc.scalar.copy(
-            out=wq_grouped[:].rearrange("p (c i j) -> p c j i", i=2, j=PACK),
-            in_=wq_raw[:].rearrange("p j (c i) -> p c j i", i=2),
-        )
         gain_sigmoid_shared(1)
         gain_sigmoid(0, 0)
         gain_sigmoid(2, 0)
@@ -417,22 +418,32 @@ def tile_list_campaign_branch_bids_kernel(
                 tanh_pass(2, side, a)
         quantise_hidden("sigmoid", 0)
         quantise_hidden("sigmoid", 1)
+        quantise_hidden("sigmoid", 2)
+        wq_grouped = placed([P, N * PACK], BF16, "wq_grouped", AT_WQ_ROUNDED)
+        nc.gpsimd.tensor_scalar(
+            out=wq_grouped[:].rearrange("p (c j) -> p c j", j=PACK),
+            in0=wq_raw[:].rearrange("p j c -> p c j"),
+            scalar1=1.0,
+            scalar2=0.0,
+            op0=MULT,
+            op1=ADD,
+        )
+        gain_sigmoid(3, 0)
+        activate_tanh(0)
+        activate_tanh(1)
+        for side in range(2):
+            for a in range(PASSES):
+                tanh_pass(3, side, a)
+        activate_tanh(2)
+        activate_tanh(3)
+        gain_tanh(0)
+        gain_tanh(1)
         for lo, hi in ((0, 2 * P), (2 * P, N)):
             nc.vector.quantize_mx(
                 out=wq_codes[:, lo:hi].bitcast(FP8X4),
                 scales=wq_plane[:, lo:hi],
                 in_=wq_grouped[:, PACK * lo : PACK * hi],
             )
-        quantise_hidden("sigmoid", 2)
-        gain_sigmoid_shared(3)
-        activate_tanh(0)
-        for side in range(2):
-            for a in range(PASSES):
-                tanh_pass(3, side, a)
-        for d in range(1, QUARTERS):
-            activate_tanh(d)
-        gain_tanh(0, nc.vector, gt_psum)
-        gain_tanh(1, nc.vector, gt_psum)
         quantise_hidden("sigmoid", 3)
         quantise_hidden("tanh", 0)
         quantise_hidden("tanh", 1)
@@ -440,8 +451,8 @@ def tile_list_campaign_branch_bids_kernel(
         project(0, 0)
         project(0, 1)
         respond(1, (0, 1))
-        gain_tanh(2, nc.vector, gt_psum)
-        gain_tanh(3, nc.gpsimd, gt_sb)
+        gain_tanh(2)
+        gain_tanh(3)
         bid(0, 0, 0, HALF)
         respond(1, (2,))
         project(0, 2)

@@ -36,24 +36,24 @@ AT_WT = (51, 59, 73)
 AT_WQ = 67
 AT_WP_CODES = 0
 AT_WP_PLANE = 2
-AT_ROUNDED_1 = 84
-AT_SIGMOID = (83, 85, 105, 104)
+AT_WT_ROUNDED_1 = 84
+AT_B_FIRST = 84
+AT_SIGMOID_FIRST = 90
+AT_WT_CODES_LAST = (90, 91)
+AT_B_CODES = (92, 94, 100.5)
+AT_B_LATE = (105, 104)
 AT_WQ_ROUNDED = 106
-AT_SIGMOID_VALUES = 90
-AT_LAST_WT_CODES = (90, 91)
-AT_B_CODES = (92, 94)
-AT_TANH_VALUES_1 = 100
+AT_TANH_1 = 100
 AT_WQ_CODES = 99
-AT_LAST_B_CODES = 100.5
-AT_FIRST_A_CODES = 101.5
-AT_TANH_1 = 110
-AT_TANH_LATE = 110
-AT_RESPONSE = 114
-GPSIMD_SHARE = 176
-TANH_SHARES = (0, 80, 0, 256)
+AT_A_CODES = (101.5, 114)
+AT_A = 110
+AT_RESPONSE_1 = 114
+SIGMOID_SHARE = 176
+TANH_SHARES = (0, 80, 0, QUARTER)
 
-TANH_BANKS = ((1, 3), (2, 4), (5, 6), (2, 4))
+GAINS_TRANSPOSED_BANK = 7
 GAIN_BANK = 0
+TANH_BANKS = ((1, 3), (2, 4), (5, 6), (2, 4))
 RESPONSE_BANKS = ((5, 6, 1), (2, 4, 3))
 VALUE_BANKS = ((3, 7, 4), (5, 6, 1))
 CROSSED = 2
@@ -145,10 +145,10 @@ def tile_list_campaign_branch_bids_kernel(
         nc.vector.tensor_copy(
             out=gains_padded[:, 0 : 2 * PACK].rearrange("p (b t) -> p b t", t=PACK), in_=gains[:, :, 0:PACK]
         )
-        gains_turned = held([P, P], F32, "gains_turned")
-        first_turn = in_bank(7, [P, P])
-        nc.tensor.transpose(first_turn[:], gains_padded, identity)
-        nc.vector.tensor_copy(out=gains_turned[:], in_=first_turn[:])
+        gains_transposed = held([P, P], F32, "gains_transposed")
+        transposed_bank = in_bank(GAINS_TRANSPOSED_BANK, [P, P])
+        nc.tensor.transpose(transposed_bank[:], gains_padded, identity)
+        nc.vector.tensor_copy(out=gains_transposed[:], in_=transposed_bank[:])
         v_planes = [v_plane_words[:, a, :].bitcast(U8) for a in range(PASSES)]
 
         wg_codes = held([P, PASSES, 2 * H], U8, "wg_codes")
@@ -226,43 +226,27 @@ def tile_list_campaign_branch_bids_kernel(
                     stop=(a == LAST and e == 1),
                 )
 
-        tanh_values = {}
-        hidden = {}
-        hidden_codes = {}
-        hidden_plane = {}
-        codes_at = {
-            ("sigmoid", 0): AT_B_CODES[0],
-            ("sigmoid", 1): AT_B_CODES[1],
-            ("tanh", 0): AT_FIRST_A_CODES,
-            ("tanh", 1): AT_RESPONSE,
-        }
-        for (branch, h), at in codes_at.items():
-            hidden_codes[branch, h] = placed([P, HALF], U32, "hidden_codes_%s%d" % (branch, h), at)
-            hidden_plane[branch, h] = held([P, HALF], U8, "hidden_plane_%s%d" % (branch, h))
-        b_codes = [hidden_codes["sigmoid", 1][:, 0:QUARTER], placed([P, QUARTER], U32, "b_codes_last", AT_LAST_B_CODES)[:]]
         width = QUARTER * PACK
-        for d in range(QUARTERS):
-            hidden["sigmoid", d] = placed([P, width], BF16, "hidden_sigmoid%d" % d, AT_SIGMOID[d])[:]
-        hidden["tanh", 0] = held([P, width], BF16, "hidden_tanh0")[:]
-        hidden["tanh", 1] = placed([P, width], BF16, "hidden_tanh1", AT_TANH_1)[:]
-        hidden_late = placed([P, 2 * width], BF16, "hidden_late", AT_TANH_LATE)
-        hidden["tanh", 2] = hidden_late[:, 0:width]
-        hidden["tanh", 3] = hidden_late[:, width : 2 * width]
-        for d in range(QUARTERS):
-            if d == 1:
-                tanh_values[d] = placed([P, width], F32, "tanh_values1", AT_TANH_VALUES_1)
-            else:
-                tanh_values[d] = held([P, width], F32, "tanh_values%d" % d)
+        b_spans = ((0, HALF), (HALF, HALF + QUARTER), (HALF + QUARTER, S))
+        b_rounded = [placed([P, HALF * PACK], BF16, "b_rounded0", AT_B_FIRST)]
+        b_rounded = b_rounded + [placed([P, width], BF16, "b_rounded%d" % (i + 1), AT_B_LATE[i]) for i in range(2)]
+        b_codes = [placed([P, hi - lo], U32, "b_codes%d" % i, AT_B_CODES[i]) for i, (lo, hi) in enumerate(b_spans)]
+        b_plane = held([P, S], U8, "b_plane")
+        a_rounded = [placed([P, HALF * PACK], BF16, "a_rounded%d" % h, AT_A) for h in range(HALVES)]
+        a_codes = [placed([P, HALF], U32, "a_codes%d" % h, AT_A_CODES[h]) for h in range(HALVES)]
+        a_plane = [held([P, HALF], U8, "a_plane%d" % h) for h in range(HALVES)]
         sigmoid_values = [
-            placed([P, PACK, HALF], F32, "sigmoid_values0", AT_SIGMOID_VALUES),
+            placed([P, PACK, HALF], F32, "sigmoid_values0", AT_SIGMOID_FIRST),
             held([P, PACK, HALF], F32, "sigmoid_values1"),
         ]
+        tanh_values = [
+            placed([P, width], F32, "tanh_values1", AT_TANH_1) if d == 1 else held([P, width], F32, "tanh_values%d" % d)
+            for d in range(QUARTERS)
+        ]
 
-        def activate_sigmoid(h, lo, hi):
+        def activate_sigmoid(h):
             for t in range(PACK):
-                nc.scalar.activation(
-                    out=sigmoid_values[h][:, t, lo:hi], in_=banks["sigmoid", h, t][:, lo:hi], func=ACT.Sigmoid
-                )
+                nc.scalar.activation(out=sigmoid_values[h][:, t, :], in_=banks["sigmoid", h, t][:], func=ACT.Sigmoid)
 
         def activate_tanh(d):
             for side in range(2):
@@ -273,45 +257,37 @@ def tile_list_campaign_branch_bids_kernel(
                     func=ACT.Tanh,
                 )
 
-        def gain_sigmoid(d, first):
-            h, lo = divmod(d * QUARTER, HALF)
-            nc.vector.tensor_tensor(
-                out=hidden["sigmoid", d][:, PACK * first :].rearrange("p (c i t) -> p c t i", i=2, t=PACK),
-                in0=sigmoid_values[h][:, :, lo + first : lo + QUARTER].rearrange("p t (c i) -> p c t i", i=2),
-                in1=gain_bank[:, 0:PACK].unsqueeze(1).unsqueeze(3).to_broadcast([P, (QUARTER - first) // 2, PACK, 2]),
+        def gain_sigmoid(i, lo, hi, engine, gain):
+            h, first = divmod(b_spans[i][0], HALF)
+            engine.tensor_tensor(
+                out=b_rounded[i][:, PACK * lo : PACK * hi].rearrange("p (c i t) -> p c t i", i=2, t=PACK),
+                in0=sigmoid_values[h][:, :, first + lo : first + hi].rearrange("p t (c i) -> p c t i", i=2),
+                in1=gain.unsqueeze(1).unsqueeze(3).to_broadcast([P, (hi - lo) // 2, PACK, 2]),
                 op=MULT,
             )
-
-        def gain_sigmoid_shared(d):
-            h, lo = divmod(d * QUARTER, HALF)
-            nc.gpsimd.tensor_tensor(
-                out=hidden["sigmoid", d][:, 0 : PACK * GPSIMD_SHARE].rearrange("p (c i t) -> p c t i", i=2, t=PACK),
-                in0=sigmoid_values[h][:, :, lo : lo + GPSIMD_SHARE].rearrange("p t (c i) -> p c t i", i=2),
-                in1=gs_sb.unsqueeze(1).unsqueeze(3).to_broadcast([P, GPSIMD_SHARE // 2, PACK, 2]),
-                op=MULT,
-            )
-            gain_sigmoid(d, GPSIMD_SHARE)
 
         def gain_tanh(d):
+            h, part = divmod(d, 2)
             order = "e s" if d == CROSSED else "s e"
+            rounded = a_rounded[h][:, part * width : (part + 1) * width].rearrange("p (c %s) -> p c s e" % order, s=2, e=2)
+            values_d = tanh_values[d][:].rearrange("p (s c e) -> p c s e", s=2, e=2)
             share = TANH_SHARES[d]
             for engine, gain, lo, hi in ((nc.gpsimd, gt_sb, 0, share), (nc.vector, gt_psum, share, QUARTER)):
                 if lo < hi:
+                    by_side = gain.rearrange("p (%s) -> p s e" % order, s=2, e=2)
                     engine.tensor_tensor(
-                        out=hidden["tanh", d].rearrange("p (c %s) -> p c s e" % order, s=2, e=2)[:, lo:hi, :, :],
-                        in0=tanh_values[d][:].rearrange("p (s c e) -> p c s e", s=2, e=2)[:, lo:hi, :, :],
-                        in1=gain.rearrange("p (%s) -> p s e" % order, s=2, e=2).unsqueeze(1).to_broadcast([P, hi - lo, 2, 2]),
+                        out=rounded[:, lo:hi, :, :],
+                        in0=values_d[:, lo:hi, :, :],
+                        in1=by_side.unsqueeze(1).to_broadcast([P, hi - lo, 2, 2]),
                         op=MULT,
                     )
 
-        def quantise_hidden(branch, d):
-            h, lo = divmod(d * QUARTER, HALF)
-            codes = b_codes[d - 2] if (branch, h) == ("sigmoid", 1) else hidden_codes[branch, h][:, lo : lo + QUARTER]
-            nc.vector.quantize_mx(
-                out=codes.bitcast(FP8X4),
-                scales=hidden_plane[branch, h][:, lo : lo + QUARTER],
-                in_=hidden[branch, d],
-            )
+        def quantise_b(i):
+            lo, hi = b_spans[i]
+            nc.vector.quantize_mx(out=b_codes[i][:].bitcast(FP8X4), scales=b_plane[:, lo:hi], in_=b_rounded[i][:])
+
+        def quantise_a(h):
+            nc.vector.quantize_mx(out=a_codes[h][:].bitcast(FP8X4), scales=a_plane[h][:], in_=a_rounded[h][:])
 
         wt_grouped = {}
         wt_codes = {}
@@ -319,11 +295,11 @@ def tile_list_campaign_branch_bids_kernel(
         for a in range(PASSES):
             for side in range(2):
                 if (a, side) == (1, 1):
-                    wt_grouped[a, side] = placed([P, 2 * P * PACK], BF16, "wt_grouped_held", AT_ROUNDED_1)
+                    wt_grouped[a, side] = placed([P, 2 * P * PACK], BF16, "wt_grouped_held", AT_WT_ROUNDED_1)
                 else:
                     wt_grouped[a, side] = held([P, 2 * P * PACK], BF16, "wt_grouped%d_%d" % (a, side))
                 if a == LAST:
-                    wt_codes[a, side] = placed([P, 2 * P], U32, "wt_codes_last%d" % side, AT_LAST_WT_CODES[side])
+                    wt_codes[a, side] = placed([P, 2 * P], U32, "wt_codes_last%d" % side, AT_WT_CODES_LAST[side])
                 else:
                     wt_codes[a, side] = held([P, 2 * P], U32, "wt_codes%d_%d" % (a, side))
                 wt_plane[a, side] = held([P, 2 * P], U8, "wt_plane%d_%d" % (a, side))
@@ -346,7 +322,7 @@ def tile_list_campaign_branch_bids_kernel(
         for h in range(HALVES):
             for n in range(SLOT_TILES):
                 if (h, n) == (0, 1):
-                    response[h, n] = placed([P, HALF], F32, "response_held", AT_RESPONSE)
+                    response[h, n] = placed([P, HALF], F32, "response_held", AT_RESPONSE_1)
                 else:
                     response[h, n] = held([P, HALF], F32, "response%d_%d" % (h, n))
 
@@ -354,18 +330,17 @@ def tile_list_campaign_branch_bids_kernel(
             for n in tiles:
                 cols = slice(P * n, P * (n + 1))
                 bank = in_bank(RESPONSE_BANKS[h][n], [P, HALF])
-                pieces = [hidden_codes["sigmoid", 0][:]] if h == 0 else b_codes
-                step = HALF // len(pieces)
-                for i, codes in enumerate(pieces):
-                    nc.tensor.matmul_mx(
-                        out=bank[:, i * step : (i + 1) * step],
-                        lhsT=wq_codes[:, cols].bitcast(FP8X4),
-                        lhsT_scale=wq_plane[:, cols],
-                        rhs=codes.bitcast(FP8X4),
-                        rhs_scale=hidden_plane["sigmoid", h][:, i * step : (i + 1) * step],
-                        start=True,
-                        stop=True,
-                    )
+                for i, (lo, hi) in enumerate(b_spans):
+                    if lo // HALF == h:
+                        nc.tensor.matmul_mx(
+                            out=bank[:, lo - h * HALF : hi - h * HALF],
+                            lhsT=wq_codes[:, cols].bitcast(FP8X4),
+                            lhsT_scale=wq_plane[:, cols],
+                            rhs=b_codes[i][:].bitcast(FP8X4),
+                            rhs_scale=b_plane[:, lo:hi],
+                            start=True,
+                            stop=True,
+                        )
                 nc.scalar.copy(out=response[h, n][:], in_=bank[:])
 
         values = {}
@@ -377,8 +352,8 @@ def tile_list_campaign_branch_bids_kernel(
                 out=values[h, n][:],
                 lhsT=wp_codes[:, cols].bitcast(FP8X4),
                 lhsT_scale=wp_plane[:].bitcast(U8)[:, cols],
-                rhs=hidden_codes["tanh", h][:].bitcast(FP8X4),
-                rhs_scale=hidden_plane["tanh", h][:],
+                rhs=a_codes[h][:].bitcast(FP8X4),
+                rhs_scale=a_plane[h][:],
                 start=True,
                 stop=True,
             )
@@ -394,9 +369,10 @@ def tile_list_campaign_branch_bids_kernel(
             gather_half(LAST, h)
             sigmoid_pass(h, LAST)
         for h in range(HALVES):
-            activate_sigmoid(h, 0, HALF)
+            activate_sigmoid(h)
         gain_bank = in_bank(GAIN_BANK, [P, P])
-        nc.tensor.transpose(gain_bank[:], gains_turned[:], identity)
+        nc.tensor.transpose(gain_bank[:], gains_transposed[:], identity)
+        gs_psum = gain_bank[:, 0:PACK]
         gt_psum = gain_bank[:, PACK : 2 * PACK]
         for a in range(PASSES):
             for side in range(2):
@@ -404,9 +380,9 @@ def tile_list_campaign_branch_bids_kernel(
             if a < LAST:
                 for side in range(2):
                     quantise_wt(a, side)
-        gain_sigmoid_shared(1)
-        gain_sigmoid(0, 0)
-        gain_sigmoid(2, 0)
+        gain_sigmoid(0, 0, SIGMOID_SHARE, nc.gpsimd, gs_sb)
+        gain_sigmoid(0, SIGMOID_SHARE, HALF, nc.vector, gs_psum)
+        gain_sigmoid(1, 0, QUARTER, nc.vector, gs_psum)
         for side in range(2):
             quantise_wt(LAST, side)
         for a in range(PASSES):
@@ -416,9 +392,8 @@ def tile_list_campaign_branch_bids_kernel(
         for a in range(PASSES):
             for side in range(2):
                 tanh_pass(2, side, a)
-        quantise_hidden("sigmoid", 0)
-        quantise_hidden("sigmoid", 1)
-        quantise_hidden("sigmoid", 2)
+        quantise_b(0)
+        quantise_b(1)
         wq_grouped = placed([P, N * PACK], BF16, "wq_grouped", AT_WQ_ROUNDED)
         nc.gpsimd.tensor_scalar(
             out=wq_grouped[:].rearrange("p (c j) -> p c j", j=PACK),
@@ -428,7 +403,7 @@ def tile_list_campaign_branch_bids_kernel(
             op0=MULT,
             op1=ADD,
         )
-        gain_sigmoid(3, 0)
+        gain_sigmoid(2, 0, QUARTER, nc.vector, gs_psum)
         activate_tanh(0)
         activate_tanh(1)
         for side in range(2):
@@ -444,9 +419,8 @@ def tile_list_campaign_branch_bids_kernel(
                 scales=wq_plane[:, lo:hi],
                 in_=wq_grouped[:, PACK * lo : PACK * hi],
             )
-        quantise_hidden("sigmoid", 3)
-        quantise_hidden("tanh", 0)
-        quantise_hidden("tanh", 1)
+        quantise_b(2)
+        quantise_a(0)
         respond(0, range(SLOT_TILES))
         project(0, 0)
         project(0, 1)
@@ -457,9 +431,7 @@ def tile_list_campaign_branch_bids_kernel(
         respond(1, (2,))
         project(0, 2)
         bid(0, 1, 0, HALF)
-        nc.vector.quantize_mx(
-            out=hidden_codes["tanh", 1][:].bitcast(FP8X4), scales=hidden_plane["tanh", 1][:], in_=hidden_late[:]
-        )
+        quantise_a(1)
         for n in range(SLOT_TILES):
             project(1, n)
         bid(0, 2, 0, HALF)

@@ -39,24 +39,24 @@ AT_WP_PLANE = 2
 AT_WT_ROUNDED_1 = 84
 AT_B_FIRST = 84
 AT_SIGMOID_FIRST = 90
-AT_WT_CODES_LAST = (90, 91)
+AT_WT_CODES_HELD = {(2, 0): 90, (2, 1): 91, (1, 1): 96}
 AT_B_CODES = (92, 94, 100.5)
-AT_B_LATE = (105, 104)
-AT_WQ_ROUNDED = 106
+AT_B_LATE = (105, 82.5)
+AT_WQ_ROUNDED = 84.5
 AT_TANH_1 = 100
 AT_WQ_CODES = 99
 AT_A_CODES = (101.5, 114)
 AT_A = 110
 AT_RESPONSE_1 = 114
-SIGMOID_SHARE = 176
-TANH_SHARES = (0, 80, 0, QUARTER)
+SIGMOID_SHARE = 192
+TANH_SHARES = (128, 0, 0, QUARTER)
 
 GAINS_TRANSPOSED_BANK = 7
 GAIN_BANK = 0
-TANH_BANKS = ((1, 3), (2, 4), (5, 6), (2, 4))
-RESPONSE_BANKS = ((5, 6, 1), (2, 4, 3))
-VALUE_BANKS = ((3, 7, 4), (5, 6, 1))
-CROSSED = 2
+TANH_BANKS = ((1, 5), (2, 6), (3, 7), (4, 6))
+RESPONSE_BANKS = ((5, 2, 1), (4, 6, 3))
+VALUE_BANKS = ((3, 7, 6), (5, 2, 1))
+CROSSED = (2, 3)
 
 SCALE_ROW_LOADS = ((0, 16, 48), (16, 32, 96))
 SCALE_WINDOW_GAPS = ((0, 48), (64, 96))
@@ -210,12 +210,12 @@ def tile_list_campaign_branch_bids_kernel(
                     stop=(a == LAST),
                 )
 
-        def tanh_pass(d, side, a):
+        def tanh_pass(d, side, a, tiles=(0, 1)):
             h, lo = divmod(d * QUARTER, HALF)
             if a == 0:
                 banks["tanh", d, side] = in_bank(TANH_BANKS[d][side], [P, 2, QUARTER])
-            for e in range(2):
-                piece, tile = (e, side) if d == CROSSED else (side, e)
+            for e in tiles:
+                piece, tile = (e, side) if d in CROSSED else (side, e)
                 nc.tensor.matmul_mx(
                     out=banks["tanh", d, side][:, e, :],
                     lhsT=wt_codes[a, piece][:, P * tile : P * (tile + 1)].bitcast(FP8X4),
@@ -240,7 +240,7 @@ def tile_list_campaign_branch_bids_kernel(
             held([P, PACK, HALF], F32, "sigmoid_values1"),
         ]
         tanh_values = [
-            placed([P, width], F32, "tanh_values1", AT_TANH_1) if d == 1 else held([P, width], F32, "tanh_values%d" % d)
+            placed([P, width], F32, "tanh_values0", AT_TANH_1) if d == 0 else held([P, width], F32, "tanh_values%d" % d)
             for d in range(QUARTERS)
         ]
 
@@ -257,18 +257,18 @@ def tile_list_campaign_branch_bids_kernel(
                     func=ACT.Tanh,
                 )
 
-        def gain_sigmoid(i, lo, hi, engine, gain):
+        def gain_sigmoid(i, lo, hi, engine, gain, run=2):
             h, first = divmod(b_spans[i][0], HALF)
             engine.tensor_tensor(
-                out=b_rounded[i][:, PACK * lo : PACK * hi].rearrange("p (c i t) -> p c t i", i=2, t=PACK),
-                in0=sigmoid_values[h][:, :, first + lo : first + hi].rearrange("p t (c i) -> p c t i", i=2),
-                in1=gain.unsqueeze(1).unsqueeze(3).to_broadcast([P, (hi - lo) // 2, PACK, 2]),
+                out=b_rounded[i][:, PACK * lo : PACK * hi].rearrange("p (c i t) -> p c t i", i=run, t=PACK),
+                in0=sigmoid_values[h][:, :, first + lo : first + hi].rearrange("p t (c i) -> p c t i", i=run),
+                in1=gain.unsqueeze(1).unsqueeze(3).to_broadcast([P, (hi - lo) // run, PACK, run]),
                 op=MULT,
             )
 
         def gain_tanh(d):
             h, part = divmod(d, 2)
-            order = "e s" if d == CROSSED else "s e"
+            order = "e s" if d in CROSSED else "s e"
             rounded = a_rounded[h][:, part * width : (part + 1) * width].rearrange("p (c %s) -> p c s e" % order, s=2, e=2)
             values_d = tanh_values[d][:].rearrange("p (s c e) -> p c s e", s=2, e=2)
             share = TANH_SHARES[d]
@@ -294,20 +294,22 @@ def tile_list_campaign_branch_bids_kernel(
         wt_plane = {}
         for a in range(PASSES):
             for side in range(2):
-                if (a, side) == (1, 1):
+                if (a, side) == (1, 0):
                     wt_grouped[a, side] = placed([P, 2 * P * PACK], BF16, "wt_grouped_held", AT_WT_ROUNDED_1)
                 else:
                     wt_grouped[a, side] = held([P, 2 * P * PACK], BF16, "wt_grouped%d_%d" % (a, side))
-                if a == LAST:
-                    wt_codes[a, side] = placed([P, 2 * P], U32, "wt_codes_last%d" % side, AT_WT_CODES_LAST[side])
+                if (a, side) in AT_WT_CODES_HELD:
+                    wt_codes[a, side] = placed(
+                        [P, 2 * P], U32, "wt_codes%d_%d" % (a, side), AT_WT_CODES_HELD[a, side]
+                    )
                 else:
                     wt_codes[a, side] = held([P, 2 * P], U32, "wt_codes%d_%d" % (a, side))
                 wt_plane[a, side] = held([P, 2 * P], U8, "wt_plane%d_%d" % (a, side))
 
-        def round_wt(a, side, copy):
+        def round_wt(a, side, copy, lo=0, hi=P):
             dst = wt_grouped[a, side][:].rearrange("p (e m j) -> p m j e", e=2, j=PACK)
             src = wt_raw[a][:].rearrange("p j (m t) -> p m j t", t=PACK)
-            copy(out=dst, in_=src[:, :, :, 2 * side : 2 * side + 2])
+            copy(out=dst[:, lo:hi, :, :], in_=src[:, lo:hi, :, 2 * side : 2 * side + 2])
 
         def quantise_wt(a, side):
             nc.vector.quantize_mx(
@@ -374,26 +376,40 @@ def tile_list_campaign_branch_bids_kernel(
         nc.tensor.transpose(gain_bank[:], gains_transposed[:], identity)
         gs_psum = gain_bank[:, 0:PACK]
         gt_psum = gain_bank[:, PACK : 2 * PACK]
-        for a in range(PASSES):
-            for side in range(2):
-                round_wt(a, side, nc.scalar.copy if a == LAST else nc.vector.tensor_copy)
-            if a < LAST:
-                for side in range(2):
-                    quantise_wt(a, side)
-        gain_sigmoid(0, 0, SIGMOID_SHARE, nc.gpsimd, gs_sb)
+        for side in range(2):
+            round_wt(0, side, nc.vector.tensor_copy)
+        for side in range(2):
+            quantise_wt(0, side)
+        round_wt(1, 0, nc.vector.tensor_copy)
+        round_wt(1, 1, nc.vector.tensor_copy, 0, P // 2)
+        quantise_wt(1, 0)
+        round_wt(1, 1, nc.scalar.copy, P // 2, P)
+        round_wt(2, 0, nc.scalar.copy)
+        round_wt(2, 1, nc.scalar.copy)
+        gain_sigmoid(0, 0, SIGMOID_SHARE, nc.gpsimd, gs_sb, 1)
         gain_sigmoid(0, SIGMOID_SHARE, HALF, nc.vector, gs_psum)
         gain_sigmoid(1, 0, QUARTER, nc.vector, gs_psum)
-        for side in range(2):
-            quantise_wt(LAST, side)
-        for a in range(PASSES):
-            for side in range(2):
-                for d in (0, 1):
-                    tanh_pass(d, side, a)
-        for a in range(PASSES):
-            for side in range(2):
-                tanh_pass(2, side, a)
-        quantise_b(0)
+        quantise_wt(1, 1)
+        quantise_wt(2, 0)
         quantise_b(1)
+        quantise_b(0)
+        quantise_wt(2, 1)
+        for side in range(2):
+            for d in (0, 1):
+                tanh_pass(d, side, 0)
+        for side in range(2):
+            tanh_pass(2, side, 0)
+        tanh_pass(3, 0, 0)
+        for a in (1, 2):
+            for d in (0, 1):
+                tanh_pass(d, 0, a)
+        for d in (0, 1):
+            for a in (1, 2):
+                tanh_pass(d, 1, a)
+        for d, side in ((2, 0), (2, 1), (3, 0)):
+            for e in range(2):
+                for a in (1, 2):
+                    tanh_pass(d, side, a, (e,))
         wq_grouped = placed([P, N * PACK], BF16, "wq_grouped", AT_WQ_ROUNDED)
         nc.gpsimd.tensor_scalar(
             out=wq_grouped[:].rearrange("p (c j) -> p c j", j=PACK),
@@ -406,9 +422,8 @@ def tile_list_campaign_branch_bids_kernel(
         gain_sigmoid(2, 0, QUARTER, nc.vector, gs_psum)
         activate_tanh(0)
         activate_tanh(1)
-        for side in range(2):
-            for a in range(PASSES):
-                tanh_pass(3, side, a)
+        for a in range(PASSES):
+            tanh_pass(3, 1, a)
         activate_tanh(2)
         activate_tanh(3)
         gain_tanh(0)

@@ -45,17 +45,17 @@ AT_B_LATE = (105, 82.5)
 AT_WQ_ROUNDED = 84.5
 AT_TANH_1 = 100
 AT_WQ_CODES = 99
-AT_A_CODES = (101.5, 114)
+AT_A_CODES = (101.5, 116, 114)
 AT_A = 110
 AT_RESPONSE_1 = 114
 SIGMOID_SHARE = 192
-TANH_SHARES = (128, 0, 0, QUARTER)
+TANH_SHARES = (128, 0, 112, 176)
 
 GAINS_TRANSPOSED_BANK = 7
 GAIN_BANK = 0
 TANH_BANKS = ((1, 5), (2, 6), (3, 7), (4, 6))
-RESPONSE_BANKS = ((5, 2, 1), (4, 6, 3))
-VALUE_BANKS = ((3, 7, 6), (5, 2, 1))
+RESPONSE_BANKS = ((1, 2, 5), (6, 1, 2))
+VALUE_BANKS = ((3, 7, 4), (3, 5, 7), (4, 6, 1))
 CROSSED = (2, 3)
 
 SCALE_ROW_LOADS = ((0, 16, 48), (16, 32, 96))
@@ -232,9 +232,11 @@ def tile_list_campaign_branch_bids_kernel(
         b_rounded = b_rounded + [placed([P, width], BF16, "b_rounded%d" % (i + 1), AT_B_LATE[i]) for i in range(2)]
         b_codes = [placed([P, hi - lo], U32, "b_codes%d" % i, AT_B_CODES[i]) for i, (lo, hi) in enumerate(b_spans)]
         b_plane = held([P, S], U8, "b_plane")
-        a_rounded = [placed([P, HALF * PACK], BF16, "a_rounded%d" % h, AT_A) for h in range(HALVES)]
-        a_codes = [placed([P, HALF], U32, "a_codes%d" % h, AT_A_CODES[h]) for h in range(HALVES)]
-        a_plane = [held([P, HALF], U8, "a_plane%d" % h) for h in range(HALVES)]
+        a_rounded = [
+            placed([P, (hi - lo) * PACK], BF16, "a_rounded%d" % i, AT_A) for i, (lo, hi) in enumerate(b_spans)
+        ]
+        a_codes = [placed([P, hi - lo], U32, "a_codes%d" % i, AT_A_CODES[i]) for i, (lo, hi) in enumerate(b_spans)]
+        a_plane = [held([P, hi - lo], U8, "a_plane%d" % i) for i, (lo, hi) in enumerate(b_spans)]
         sigmoid_values = [
             placed([P, PACK, HALF], F32, "sigmoid_values0", AT_SIGMOID_FIRST),
             held([P, PACK, HALF], F32, "sigmoid_values1"),
@@ -266,13 +268,14 @@ def tile_list_campaign_branch_bids_kernel(
                 op=MULT,
             )
 
-        def gain_tanh(d):
-            h, part = divmod(d, 2)
+        def gain_tanh(d, engines=(0, 1)):
+            h, part = (0, d) if d < 2 else (d - 1, 0)
             order = "e s" if d in CROSSED else "s e"
             rounded = a_rounded[h][:, part * width : (part + 1) * width].rearrange("p (c %s) -> p c s e" % order, s=2, e=2)
             values_d = tanh_values[d][:].rearrange("p (s c e) -> p c s e", s=2, e=2)
             share = TANH_SHARES[d]
-            for engine, gain, lo, hi in ((nc.gpsimd, gt_sb, 0, share), (nc.vector, gt_psum, share, QUARTER)):
+            parts = ((nc.gpsimd, gt_sb, 0, share), (nc.vector, gt_psum, share, QUARTER))
+            for engine, gain, lo, hi in [parts[i] for i in engines]:
                 if lo < hi:
                     by_side = gain.rearrange("p (%s) -> p s e" % order, s=2, e=2)
                     engine.tensor_tensor(
@@ -321,49 +324,56 @@ def tile_list_campaign_branch_bids_kernel(
 
         response = {}
 
-        for h in range(HALVES):
+        for i, (lo, hi) in enumerate(b_spans):
             for n in range(SLOT_TILES):
-                if (h, n) == (0, 1):
-                    response[h, n] = placed([P, HALF], F32, "response_held", AT_RESPONSE_1)
+                if (i, n) == (0, 2):
+                    response[i, n] = placed([P, hi - lo], F32, "response_held", AT_RESPONSE_1)
                 else:
-                    response[h, n] = held([P, HALF], F32, "response%d_%d" % (h, n))
+                    response[i, n] = held([P, hi - lo], F32, "response%d_%d" % (i, n))
 
-        def respond(h, tiles):
-            for n in tiles:
-                cols = slice(P * n, P * (n + 1))
-                bank = in_bank(RESPONSE_BANKS[h][n], [P, HALF])
-                for i, (lo, hi) in enumerate(b_spans):
-                    if lo // HALF == h:
-                        nc.tensor.matmul_mx(
-                            out=bank[:, lo - h * HALF : hi - h * HALF],
-                            lhsT=wq_codes[:, cols].bitcast(FP8X4),
-                            lhsT_scale=wq_plane[:, cols],
-                            rhs=b_codes[i][:].bitcast(FP8X4),
-                            rhs_scale=b_plane[:, lo:hi],
-                            start=True,
-                            stop=True,
-                        )
-                nc.scalar.copy(out=response[h, n][:], in_=bank[:])
+        response_banks = {}
+
+        def respond(h, n):
+            cols = slice(P * n, P * (n + 1))
+            response_banks[h, n] = in_bank(RESPONSE_BANKS[h][n], [P, HALF])
+            for i, (lo, hi) in enumerate(b_spans):
+                if lo // HALF == h:
+                    nc.tensor.matmul_mx(
+                        out=response_banks[h, n][:, lo - h * HALF : hi - h * HALF],
+                        lhsT=wq_codes[:, cols].bitcast(FP8X4),
+                        lhsT_scale=wq_plane[:, cols],
+                        rhs=b_codes[i][:].bitcast(FP8X4),
+                        rhs_scale=b_plane[:, lo:hi],
+                        start=True,
+                        stop=True,
+                    )
+
+        def copy_response(i, n):
+            lo, hi = b_spans[i]
+            h = lo // HALF
+            nc.scalar.copy(out=response[i, n][:], in_=response_banks[h, n][:, lo - h * HALF : hi - h * HALF])
 
         values = {}
 
-        def project(h, n):
+        def project(i, n):
+            lo, hi = b_spans[i]
             cols = slice(P * n, P * (n + 1))
-            values[h, n] = in_bank(VALUE_BANKS[h][n], [P, HALF])
+            values[i, n] = in_bank(VALUE_BANKS[i][n], [P, hi - lo])
             nc.tensor.matmul_mx(
-                out=values[h, n][:],
+                out=values[i, n][:],
                 lhsT=wp_codes[:, cols].bitcast(FP8X4),
                 lhsT_scale=wp_plane[:].bitcast(U8)[:, cols],
-                rhs=a_codes[h][:].bitcast(FP8X4),
-                rhs_scale=a_plane[h][:],
+                rhs=a_codes[i][:].bitcast(FP8X4),
+                rhs_scale=a_plane[i][:],
                 start=True,
                 stop=True,
             )
 
-        def bid(h, n, lo, hi):
-            bids = held([P, hi - lo], F32, "bids%d_%d_%d" % (h, n, lo))
-            nc.vector.tensor_tensor(out=bids[:], in0=values[h, n][:, lo:hi], in1=response[h, n][:, lo:hi], op=MULT)
-            nc.sync.dma_start(out=out[P * n : P * (n + 1), h * HALF + lo : h * HALF + hi], in_=bids[:])
+        def bid(i, n):
+            lo, hi = b_spans[i]
+            bids = held([P, hi - lo], F32, "bids%d_%d" % (i, n))
+            nc.vector.tensor_tensor(out=bids[:], in0=values[i, n][:], in1=response[i, n][:], op=MULT)
+            nc.sync.dma_start(out=out[P * n : P * (n + 1), lo:hi], in_=bids[:])
 
         for h in range(HALVES):
             for a in range(LAST):
@@ -436,21 +446,30 @@ def tile_list_campaign_branch_bids_kernel(
             )
         quantise_b(2)
         quantise_a(0)
-        respond(0, range(SLOT_TILES))
-        project(0, 0)
-        project(0, 1)
-        respond(1, (0, 1))
+        for n in range(SLOT_TILES):
+            respond(0, n)
+            copy_response(0, n)
+        for n in range(SLOT_TILES):
+            project(0, n)
+        for n in range(SLOT_TILES):
+            respond(1, n)
+        for i in (1, 2):
+            for n in range(SLOT_TILES):
+                copy_response(i, n)
         gain_tanh(2)
-        gain_tanh(3)
-        bid(0, 0, 0, HALF)
-        respond(1, (2,))
-        project(0, 2)
-        bid(0, 1, 0, HALF)
+        bid(0, 0)
         quantise_a(1)
+        gain_tanh(3, (0,))
+        bid(0, 1)
+        gain_tanh(3, (1,))
+        bid(0, 2)
         for n in range(SLOT_TILES):
             project(1, n)
-        bid(0, 2, 0, HALF)
-        bid(1, 0, 0, HALF)
-        bid(1, 1, 0, HALF)
-        bid(1, 2, 0, QUARTER)
-        bid(1, 2, QUARTER, HALF)
+        bid(1, 0)
+        quantise_a(2)
+        for n in range(SLOT_TILES):
+            project(2, n)
+        bid(1, 1)
+        bid(1, 2)
+        for n in range(SLOT_TILES):
+            bid(2, n)

@@ -27,6 +27,7 @@ HALVES = S // HALF
 QUARTER = HALF // 2
 QUARTERS = S // QUARTER
 SLOT_TILES = N // P
+SPANS = ((0, HALF), (HALF, HALF + QUARTER), (HALF + QUARTER, S))
 
 AT_SCALE_WINDOW = 15
 AT_TABLE = (58, 0, 18)
@@ -36,27 +37,27 @@ AT_WT = (51, 59, 73)
 AT_WQ = 67
 AT_WP_CODES = 0
 AT_WP_PLANE = 2
-AT_WT_ROUNDED_1 = 84
-AT_B_FIRST = 84
+AT_WT_ROUNDED_OPENS = 84
 AT_SIGMOID_FIRST = 90
-AT_WT_CODES_HELD = {(2, 0): 90, (2, 1): 91, (1, 1): 96}
+AT_WT_CODES_LATE = {(1, 1): 96, (2, 0): 90, (2, 1): 91}
+AT_B_ROUNDED = (84, 105, 82.5)
 AT_B_CODES = (92, 94, 100.5)
-AT_B_LATE = (105, 82.5)
 AT_WQ_ROUNDED = 84.5
-AT_TANH_1 = 100
+AT_TANH_FIRST = 100
 AT_WQ_CODES = 99
+AT_A_ROUNDED = 110
 AT_A_CODES = (101.5, 116, 114)
-AT_A = 110
-AT_RESPONSE_1 = 114
+AT_RESPONSE_LAST = 114
 SIGMOID_SHARE = 192
-TANH_SHARES = (128, 0, 112, 176)
+TANH_SHARES = (104, 0, 112, 176)
+WT_SPLIT = P // 2
 
 GAINS_TRANSPOSED_BANK = 7
 GAIN_BANK = 0
-TANH_BANKS = ((1, 5), (2, 6), (3, 7), (4, 6))
-RESPONSE_BANKS = ((1, 2, 5), (6, 1, 2))
-VALUE_BANKS = ((3, 7, 4), (3, 5, 7), (4, 6, 1))
-CROSSED = (2, 3)
+TANH_BANKS = ((1, 5), (2, 6), (3, 7), (1, 6))
+RESPONSE_BANKS = ((4, 2, 5), (6, 4, 2))
+VALUE_BANKS = ((3, 7, 1), (3, 5, 7), (1, 6, 4))
+CROSSED = 2
 
 SCALE_ROW_LOADS = ((0, 16, 48), (16, 32, 96))
 SCALE_WINDOW_GAPS = ((0, 48), (64, 96))
@@ -215,7 +216,7 @@ def tile_list_campaign_branch_bids_kernel(
             if a == 0:
                 banks["tanh", d, side] = in_bank(TANH_BANKS[d][side], [P, 2, QUARTER])
             for e in tiles:
-                piece, tile = (e, side) if d in CROSSED else (side, e)
+                piece, tile = (e, side) if d == CROSSED else (side, e)
                 nc.tensor.matmul_mx(
                     out=banks["tanh", d, side][:, e, :],
                     lhsT=wt_codes[a, piece][:, P * tile : P * (tile + 1)].bitcast(FP8X4),
@@ -227,24 +228,22 @@ def tile_list_campaign_branch_bids_kernel(
                 )
 
         width = QUARTER * PACK
-        b_spans = ((0, HALF), (HALF, HALF + QUARTER), (HALF + QUARTER, S))
-        b_rounded = [placed([P, HALF * PACK], BF16, "b_rounded0", AT_B_FIRST)]
-        b_rounded = b_rounded + [placed([P, width], BF16, "b_rounded%d" % (i + 1), AT_B_LATE[i]) for i in range(2)]
-        b_codes = [placed([P, hi - lo], U32, "b_codes%d" % i, AT_B_CODES[i]) for i, (lo, hi) in enumerate(b_spans)]
+        b_rounded = [
+            placed([P, (hi - lo) * PACK], BF16, "b_rounded%d" % i, AT_B_ROUNDED[i]) for i, (lo, hi) in enumerate(SPANS)
+        ]
+        b_codes = [placed([P, hi - lo], U32, "b_codes%d" % i, AT_B_CODES[i]) for i, (lo, hi) in enumerate(SPANS)]
         b_plane = held([P, S], U8, "b_plane")
         a_rounded = [
-            placed([P, (hi - lo) * PACK], BF16, "a_rounded%d" % i, AT_A) for i, (lo, hi) in enumerate(b_spans)
+            placed([P, (hi - lo) * PACK], BF16, "a_rounded%d" % i, AT_A_ROUNDED) for i, (lo, hi) in enumerate(SPANS)
         ]
-        a_codes = [placed([P, hi - lo], U32, "a_codes%d" % i, AT_A_CODES[i]) for i, (lo, hi) in enumerate(b_spans)]
-        a_plane = [held([P, hi - lo], U8, "a_plane%d" % i) for i, (lo, hi) in enumerate(b_spans)]
+        a_codes = [placed([P, hi - lo], U32, "a_codes%d" % i, AT_A_CODES[i]) for i, (lo, hi) in enumerate(SPANS)]
+        a_plane = [held([P, hi - lo], U8, "a_plane%d" % i) for i, (lo, hi) in enumerate(SPANS)]
         sigmoid_values = [
             placed([P, PACK, HALF], F32, "sigmoid_values0", AT_SIGMOID_FIRST),
             held([P, PACK, HALF], F32, "sigmoid_values1"),
         ]
-        tanh_values = [
-            placed([P, width], F32, "tanh_values0", AT_TANH_1) if d == 0 else held([P, width], F32, "tanh_values%d" % d)
-            for d in range(QUARTERS)
-        ]
+        tanh_values = [placed([P, width], F32, "tanh_values0", AT_TANH_FIRST)]
+        tanh_values.extend(held([P, width], F32, "tanh_values%d" % d) for d in range(1, QUARTERS))
 
         def activate_sigmoid(h):
             for t in range(PACK):
@@ -259,8 +258,8 @@ def tile_list_campaign_branch_bids_kernel(
                     func=ACT.Tanh,
                 )
 
-        def gain_sigmoid(i, lo, hi, engine, gain, run=2):
-            h, first = divmod(b_spans[i][0], HALF)
+        def gain_sigmoid(i, lo, hi, engine, gain, run):
+            h, first = divmod(SPANS[i][0], HALF)
             engine.tensor_tensor(
                 out=b_rounded[i][:, PACK * lo : PACK * hi].rearrange("p (c i t) -> p c t i", i=run, t=PACK),
                 in0=sigmoid_values[h][:, :, first + lo : first + hi].rearrange("p t (c i) -> p c t i", i=run),
@@ -268,29 +267,31 @@ def tile_list_campaign_branch_bids_kernel(
                 op=MULT,
             )
 
-        def gain_tanh(d, engines=(0, 1)):
-            h, part = (0, d) if d < 2 else (d - 1, 0)
-            order = "e s" if d in CROSSED else "s e"
-            rounded = a_rounded[h][:, part * width : (part + 1) * width].rearrange("p (c %s) -> p c s e" % order, s=2, e=2)
-            values_d = tanh_values[d][:].rearrange("p (s c e) -> p c s e", s=2, e=2)
-            share = TANH_SHARES[d]
-            parts = ((nc.gpsimd, gt_sb, 0, share), (nc.vector, gt_psum, share, QUARTER))
-            for engine, gain, lo, hi in [parts[i] for i in engines]:
-                if lo < hi:
-                    by_side = gain.rearrange("p (%s) -> p s e" % order, s=2, e=2)
-                    engine.tensor_tensor(
-                        out=rounded[:, lo:hi, :, :],
-                        in0=values_d[:, lo:hi, :, :],
-                        in1=by_side.unsqueeze(1).to_broadcast([P, hi - lo, 2, 2]),
-                        op=MULT,
-                    )
+        def gain_tanh(d, lo, hi, engine, gain):
+            i = max(d - 1, 0)
+            first = d * QUARTER - SPANS[i][0]
+            order = "e s" if d == CROSSED else "s e"
+            rounded = a_rounded[i][:, PACK * first : PACK * (first + QUARTER)]
+            by_side = gain.rearrange("p (%s) -> p s e" % order, s=2, e=2)
+            engine.tensor_tensor(
+                out=rounded.rearrange("p (c %s) -> p c s e" % order, s=2, e=2)[:, lo:hi, :, :],
+                in0=tanh_values[d][:].rearrange("p (s c e) -> p c s e", s=2, e=2)[:, lo:hi, :, :],
+                in1=by_side.unsqueeze(1).to_broadcast([P, hi - lo, 2, 2]),
+                op=MULT,
+            )
+
+        def gain_tanh_gpsimd(d):
+            gain_tanh(d, 0, TANH_SHARES[d], nc.gpsimd, gt_sb)
+
+        def gain_tanh_vector(d):
+            gain_tanh(d, TANH_SHARES[d], QUARTER, nc.vector, gt_psum)
 
         def quantise_b(i):
-            lo, hi = b_spans[i]
+            lo, hi = SPANS[i]
             nc.vector.quantize_mx(out=b_codes[i][:].bitcast(FP8X4), scales=b_plane[:, lo:hi], in_=b_rounded[i][:])
 
-        def quantise_a(h):
-            nc.vector.quantize_mx(out=a_codes[h][:].bitcast(FP8X4), scales=a_plane[h][:], in_=a_rounded[h][:])
+        def quantise_a(i):
+            nc.vector.quantize_mx(out=a_codes[i][:].bitcast(FP8X4), scales=a_plane[i][:], in_=a_rounded[i][:])
 
         wt_grouped = {}
         wt_codes = {}
@@ -298,12 +299,12 @@ def tile_list_campaign_branch_bids_kernel(
         for a in range(PASSES):
             for side in range(2):
                 if (a, side) == (1, 0):
-                    wt_grouped[a, side] = placed([P, 2 * P * PACK], BF16, "wt_grouped_held", AT_WT_ROUNDED_1)
+                    wt_grouped[a, side] = placed([P, 2 * P * PACK], BF16, "wt_grouped_opens", AT_WT_ROUNDED_OPENS)
                 else:
                     wt_grouped[a, side] = held([P, 2 * P * PACK], BF16, "wt_grouped%d_%d" % (a, side))
-                if (a, side) in AT_WT_CODES_HELD:
+                if (a, side) in AT_WT_CODES_LATE:
                     wt_codes[a, side] = placed(
-                        [P, 2 * P], U32, "wt_codes%d_%d" % (a, side), AT_WT_CODES_HELD[a, side]
+                        [P, 2 * P], U32, "wt_codes%d_%d" % (a, side), AT_WT_CODES_LATE[a, side]
                     )
                 else:
                     wt_codes[a, side] = held([P, 2 * P], U32, "wt_codes%d_%d" % (a, side))
@@ -324,10 +325,10 @@ def tile_list_campaign_branch_bids_kernel(
 
         response = {}
 
-        for i, (lo, hi) in enumerate(b_spans):
+        for i, (lo, hi) in enumerate(SPANS):
             for n in range(SLOT_TILES):
-                if (i, n) == (0, 2):
-                    response[i, n] = placed([P, hi - lo], F32, "response_held", AT_RESPONSE_1)
+                if (i, n) == (0, SLOT_TILES - 1):
+                    response[i, n] = placed([P, hi - lo], F32, "response_last", AT_RESPONSE_LAST)
                 else:
                     response[i, n] = held([P, hi - lo], F32, "response%d_%d" % (i, n))
 
@@ -336,7 +337,7 @@ def tile_list_campaign_branch_bids_kernel(
         def respond(h, n):
             cols = slice(P * n, P * (n + 1))
             response_banks[h, n] = in_bank(RESPONSE_BANKS[h][n], [P, HALF])
-            for i, (lo, hi) in enumerate(b_spans):
+            for i, (lo, hi) in enumerate(SPANS):
                 if lo // HALF == h:
                     nc.tensor.matmul_mx(
                         out=response_banks[h, n][:, lo - h * HALF : hi - h * HALF],
@@ -349,14 +350,14 @@ def tile_list_campaign_branch_bids_kernel(
                     )
 
         def copy_response(i, n):
-            lo, hi = b_spans[i]
+            lo, hi = SPANS[i]
             h = lo // HALF
             nc.scalar.copy(out=response[i, n][:], in_=response_banks[h, n][:, lo - h * HALF : hi - h * HALF])
 
         values = {}
 
         def project(i, n):
-            lo, hi = b_spans[i]
+            lo, hi = SPANS[i]
             cols = slice(P * n, P * (n + 1))
             values[i, n] = in_bank(VALUE_BANKS[i][n], [P, hi - lo])
             nc.tensor.matmul_mx(
@@ -370,7 +371,7 @@ def tile_list_campaign_branch_bids_kernel(
             )
 
         def bid(i, n):
-            lo, hi = b_spans[i]
+            lo, hi = SPANS[i]
             bids = held([P, hi - lo], F32, "bids%d_%d" % (i, n))
             nc.vector.tensor_tensor(out=bids[:], in0=values[i, n][:], in1=response[i, n][:], op=MULT)
             nc.sync.dma_start(out=out[P * n : P * (n + 1), lo:hi], in_=bids[:])
@@ -391,35 +392,34 @@ def tile_list_campaign_branch_bids_kernel(
         for side in range(2):
             quantise_wt(0, side)
         round_wt(1, 0, nc.vector.tensor_copy)
-        round_wt(1, 1, nc.vector.tensor_copy, 0, P // 2)
+        round_wt(1, 1, nc.vector.tensor_copy, 0, WT_SPLIT)
         quantise_wt(1, 0)
-        round_wt(1, 1, nc.scalar.copy, P // 2, P)
-        round_wt(2, 0, nc.scalar.copy)
-        round_wt(2, 1, nc.scalar.copy)
+        round_wt(1, 1, nc.scalar.copy, WT_SPLIT, P)
+        for side in range(2):
+            round_wt(LAST, side, nc.scalar.copy)
         gain_sigmoid(0, 0, SIGMOID_SHARE, nc.gpsimd, gs_sb, 1)
-        gain_sigmoid(0, SIGMOID_SHARE, HALF, nc.vector, gs_psum)
-        gain_sigmoid(1, 0, QUARTER, nc.vector, gs_psum)
+        gain_sigmoid(0, SIGMOID_SHARE, HALF, nc.vector, gs_psum, 2)
+        gain_sigmoid(1, 0, QUARTER, nc.vector, gs_psum, 2)
         quantise_wt(1, 1)
-        quantise_wt(2, 0)
+        quantise_wt(LAST, 0)
         quantise_b(1)
         quantise_b(0)
-        quantise_wt(2, 1)
+        quantise_wt(LAST, 1)
         for side in range(2):
             for d in (0, 1):
                 tanh_pass(d, side, 0)
         for side in range(2):
-            tanh_pass(2, side, 0)
-        tanh_pass(3, 0, 0)
-        for a in (1, 2):
+            tanh_pass(CROSSED, side, 0)
+        for a in range(1, PASSES):
             for d in (0, 1):
                 tanh_pass(d, 0, a)
         for d in (0, 1):
-            for a in (1, 2):
+            for a in range(1, PASSES):
                 tanh_pass(d, 1, a)
-        for d, side in ((2, 0), (2, 1), (3, 0)):
+        for side in range(2):
             for e in range(2):
-                for a in (1, 2):
-                    tanh_pass(d, side, a, (e,))
+                for a in range(1, PASSES):
+                    tanh_pass(CROSSED, side, a, (e,))
         wq_grouped = placed([P, N * PACK], BF16, "wq_grouped", AT_WQ_ROUNDED)
         nc.gpsimd.tensor_scalar(
             out=wq_grouped[:].rearrange("p (c j) -> p c j", j=PACK),
@@ -429,23 +429,25 @@ def tile_list_campaign_branch_bids_kernel(
             op0=MULT,
             op1=ADD,
         )
-        gain_sigmoid(2, 0, QUARTER, nc.vector, gs_psum)
+        gain_sigmoid(2, 0, QUARTER, nc.vector, gs_psum, 2)
         activate_tanh(0)
         activate_tanh(1)
-        for a in range(PASSES):
-            tanh_pass(3, 1, a)
+        for side in range(2):
+            for a in range(PASSES):
+                tanh_pass(3, side, a)
         activate_tanh(2)
         activate_tanh(3)
-        gain_tanh(0)
-        gain_tanh(1)
+        gain_tanh_gpsimd(0)
+        gain_tanh_vector(0)
+        gain_tanh_vector(1)
         for lo, hi in ((0, 2 * P), (2 * P, N)):
             nc.vector.quantize_mx(
                 out=wq_codes[:, lo:hi].bitcast(FP8X4),
                 scales=wq_plane[:, lo:hi],
                 in_=wq_grouped[:, PACK * lo : PACK * hi],
             )
-        quantise_b(2)
         quantise_a(0)
+        quantise_b(2)
         for n in range(SLOT_TILES):
             respond(0, n)
             copy_response(0, n)
@@ -456,12 +458,13 @@ def tile_list_campaign_branch_bids_kernel(
         for i in (1, 2):
             for n in range(SLOT_TILES):
                 copy_response(i, n)
-        gain_tanh(2)
+        gain_tanh_gpsimd(2)
+        gain_tanh_vector(2)
         bid(0, 0)
         quantise_a(1)
-        gain_tanh(3, (0,))
+        gain_tanh_gpsimd(3)
         bid(0, 1)
-        gain_tanh(3, (1,))
+        gain_tanh_vector(3)
         bid(0, 2)
         for n in range(SLOT_TILES):
             project(1, n)

@@ -54,9 +54,9 @@ WT_SPLIT = P // 2
 
 GAINS_TRANSPOSED_BANK = 7
 GAIN_BANK = 0
-TANH_BANKS = ((1, 5), (2, 6), (3, 7), (1, 6))
-RESPONSE_BANKS = ((4, 2, 5), (6, 4, 2))
-VALUE_BANKS = ((3, 7, 1), (3, 5, 7), (1, 6, 4))
+TANH_BANKS = ((1, 5), (2, 6), (3, 7), (1, 3))
+RESPONSE_BANKS = ((4, 2, 5), (3, 4, 2))
+VALUE_BANKS = ((6, 7, 1), (6, 5, 7), (1, 3, 4))
 CROSSED = 2
 
 SCALE_ROW_LOADS = ((0, 16, 48), (16, 32, 96))
@@ -249,8 +249,8 @@ def tile_list_campaign_branch_bids_kernel(
             for t in range(PACK):
                 nc.scalar.activation(out=sigmoid_values[h][:, t, :], in_=banks["sigmoid", h, t][:], func=ACT.Sigmoid)
 
-        def activate_tanh(d):
-            for side in range(2):
+        def activate_tanh(d, sides=(0, 1)):
+            for side in sides:
                 run = tanh_values[d][:, side * 2 * QUARTER : (side + 1) * 2 * QUARTER]
                 nc.scalar.activation(
                     out=run.rearrange("p (c e) -> p c e", e=2),
@@ -432,24 +432,24 @@ def tile_list_campaign_branch_bids_kernel(
         gain_sigmoid(2, 0, QUARTER, nc.vector, gs_psum, 2)
         activate_tanh(0)
         activate_tanh(1)
-        for side in range(2):
-            for a in range(PASSES):
-                tanh_pass(3, side, a)
+        for a in range(PASSES):
+            tanh_pass(3, 0, a)
         activate_tanh(2)
-        activate_tanh(3)
+        activate_tanh(3, (0,))
         gain_tanh_gpsimd(0)
         gain_tanh_vector(0)
         gain_tanh_vector(1)
-        for lo, hi in ((0, 2 * P), (2 * P, N)):
-            nc.vector.quantize_mx(
-                out=wq_codes[:, lo:hi].bitcast(FP8X4),
-                scales=wq_plane[:, lo:hi],
-                in_=wq_grouped[:, PACK * lo : PACK * hi],
-            )
+        nc.vector.quantize_mx(out=wq_codes[:].bitcast(FP8X4), scales=wq_plane[:], in_=wq_grouped[:])
         quantise_a(0)
         quantise_b(2)
-        for n in range(SLOT_TILES):
+        respond(0, 0)
+        for a in range(PASSES):
+            tanh_pass(3, 1, a)
+        for n in range(1, SLOT_TILES):
             respond(0, n)
+        copy_response(0, 0)
+        activate_tanh(3, (1,))
+        for n in range(1, SLOT_TILES):
             copy_response(0, n)
         for n in range(SLOT_TILES):
             project(0, n)

@@ -37,27 +37,28 @@ AT_WT = (51, 59, 73)
 AT_WQ = 67
 AT_WP_CODES = 0
 AT_WP_PLANE = 2
-AT_WT_ROUNDED_OPENS = 84
+AT_WT_ROUNDED = {(0, 0): 84, (1, 1): 36, (2, 0): 90, (2, 1): 42}
 AT_SIGMOID_FIRST = 90
-AT_WT_CODES_LATE = {(1, 1): 96, (2, 0): 90, (2, 1): 91}
-AT_B_ROUNDED = (84, 105, 82.5)
-AT_B_CODES = (92, 94, 100.5)
-AT_WQ_ROUNDED = 84.5
+AT_SIGMOID_LAST = 37.5
+AT_WT_CODES_LATE = {(1, 0): 96, (1, 1): 97}
+AT_B_ROUNDED_FIRST = 84
+AT_B_CODES = (34.5, 36.5, 100.5)
+AT_WQ_ROUNDED = 42
 AT_TANH_FIRST = 100
 AT_WQ_CODES = 99
 AT_A_ROUNDED = 110
 AT_A_CODES = (101.5, 116, 114)
 AT_RESPONSE_LAST = 114
 SIGMOID_SHARE = 192
-TANH_SHARES = (104, 0, 112, 176)
-WT_SPLIT = P // 2
+TANH_SHARES = (0, 80, 112, 176)
+WT_SPLIT = P // 4
 
 GAINS_TRANSPOSED_BANK = 7
 GAIN_BANK = 0
-TANH_BANKS = ((1, 5), (2, 6), (3, 7), (1, 3))
-RESPONSE_BANKS = ((4, 2, 5), (3, 4, 2))
-VALUE_BANKS = ((6, 7, 1), (6, 5, 7), (1, 3, 4))
-CROSSED = 2
+SIGMOID_BANKS = {2: (4, 5), 3: (6, 5)}
+TANH_BANKS = ((7, 1), (2, 3), (4, 6), (2, 4))
+RESPONSE_BANKS = ((5, 7, 1), (4, 5, 7))
+VALUE_BANKS = ((3, 6, 2), (1, 3, 6), (2, 4, 5))
 
 SCALE_ROW_LOADS = ((0, 16, 48), (16, 32, 96))
 SCALE_WINDOW_GAPS = ((0, 48), (64, 96))
@@ -78,10 +79,10 @@ def tile_list_campaign_branch_bids_kernel(
         psum = ctx.enter_context(tc.psum_pool(name="psum", bufs=1))
 
         def held(shape, dtype, name):
-            return keep.tile(shape, dtype, name=name, tag=name, align_bytes=64)
+            return keep.tile(shape, dtype, name=name, tag=name, align_bytes=256)
 
         def placed(shape, dtype, name, kib):
-            return rooms.tile(shape, dtype, name=name, align_bytes=64, offset=int(kib * 1024))
+            return rooms.tile(shape, dtype, name=name, align_bytes=256, offset=int(kib * 1024))
 
         def in_bank(number, shape):
             return psum.tile(shape, F32, name="bank%d" % number, tag="bank%d" % number)
@@ -197,30 +198,37 @@ def tile_list_campaign_branch_bids_kernel(
 
         banks = {}
 
-        def sigmoid_pass(h, a):
+        def sigmoid_pass(a):
             for t in range(PACK):
                 if a == 0:
-                    banks["sigmoid", h, t] = in_bank(PACK * h + t, [P, HALF])
+                    banks["sigmoid", t] = in_bank(t, [P, HALF])
                 nc.tensor.matmul_mx(
-                    out=banks["sigmoid", h, t][:],
+                    out=banks["sigmoid", t][:],
                     lhsT=wg_codes[:, a, 2 * P * t : 2 * P * (t + 1)].bitcast(FP4X4),
                     lhsT_scale=wg_plane[:, a, P * t : P * (t + 1)],
-                    rhs=v_codes[a, h].bitcast(FP8X4),
-                    rhs_scale=v_planes[a][:, h * HALF : (h + 1) * HALF],
+                    rhs=v_codes[a, 0].bitcast(FP8X4),
+                    rhs_scale=v_planes[a][:, 0:HALF],
                     start=(a == 0),
                     stop=(a == LAST),
                 )
 
-        def tanh_pass(d, side, a, tiles=(0, 1)):
+        def quarter_pass(branch, d, side, a):
             h, lo = divmod(d * QUARTER, HALF)
             if a == 0:
-                banks["tanh", d, side] = in_bank(TANH_BANKS[d][side], [P, 2, QUARTER])
-            for e in tiles:
-                piece, tile = (e, side) if d == CROSSED else (side, e)
+                numbers = TANH_BANKS if branch == "tanh" else SIGMOID_BANKS
+                banks[branch, d, side] = in_bank(numbers[d][side], [P, 2, QUARTER])
+            for e in range(2):
+                t = 2 * side + e
+                if branch == "tanh":
+                    codes = wt_codes[a, side][:, P * e : P * (e + 1)].bitcast(FP8X4)
+                    plane = wt_plane[a, side][:, P * e : P * (e + 1)]
+                else:
+                    codes = wg_codes[:, a, 2 * P * t : 2 * P * (t + 1)].bitcast(FP4X4)
+                    plane = wg_plane[:, a, P * t : P * (t + 1)]
                 nc.tensor.matmul_mx(
-                    out=banks["tanh", d, side][:, e, :],
-                    lhsT=wt_codes[a, piece][:, P * tile : P * (tile + 1)].bitcast(FP8X4),
-                    lhsT_scale=wt_plane[a, piece][:, P * tile : P * (tile + 1)],
+                    out=banks[branch, d, side][:, e, :],
+                    lhsT=codes,
+                    lhsT_scale=plane,
                     rhs=v_codes[a, h][:, lo : lo + QUARTER].bitcast(FP8X4),
                     rhs_scale=v_planes[a][:, d * QUARTER : (d + 1) * QUARTER],
                     start=(a == 0 and e == 0),
@@ -228,9 +236,8 @@ def tile_list_campaign_branch_bids_kernel(
                 )
 
         width = QUARTER * PACK
-        b_rounded = [
-            placed([P, (hi - lo) * PACK], BF16, "b_rounded%d" % i, AT_B_ROUNDED[i]) for i, (lo, hi) in enumerate(SPANS)
-        ]
+        b_rounded = [placed([P, HALF * PACK], BF16, "b_rounded0", AT_B_ROUNDED_FIRST)]
+        b_rounded.extend(held([P, width], BF16, "b_rounded%d" % i) for i in (1, 2))
         b_codes = [placed([P, hi - lo], U32, "b_codes%d" % i, AT_B_CODES[i]) for i, (lo, hi) in enumerate(SPANS)]
         b_plane = held([P, S], U8, "b_plane")
         a_rounded = [
@@ -238,53 +245,53 @@ def tile_list_campaign_branch_bids_kernel(
         ]
         a_codes = [placed([P, hi - lo], U32, "a_codes%d" % i, AT_A_CODES[i]) for i, (lo, hi) in enumerate(SPANS)]
         a_plane = [held([P, hi - lo], U8, "a_plane%d" % i) for i, (lo, hi) in enumerate(SPANS)]
-        sigmoid_values = [
-            placed([P, PACK, HALF], F32, "sigmoid_values0", AT_SIGMOID_FIRST),
-            held([P, PACK, HALF], F32, "sigmoid_values1"),
-        ]
-        tanh_values = [placed([P, width], F32, "tanh_values0", AT_TANH_FIRST)]
-        tanh_values.extend(held([P, width], F32, "tanh_values%d" % d) for d in range(1, QUARTERS))
+        sigmoid_first = placed([P, PACK, HALF], F32, "sigmoid_first", AT_SIGMOID_FIRST)
+        values_of = {
+            ("sigmoid", 2): held([P, width], F32, "sigmoid_values2"),
+            ("sigmoid", 3): placed([P, width], F32, "sigmoid_values3", AT_SIGMOID_LAST),
+            ("tanh", 0): placed([P, width], F32, "tanh_values0", AT_TANH_FIRST),
+        }
+        for d in range(1, QUARTERS):
+            values_of["tanh", d] = held([P, width], F32, "tanh_values%d" % d)
 
-        def activate_sigmoid(h):
+        def activate_first():
             for t in range(PACK):
-                nc.scalar.activation(out=sigmoid_values[h][:, t, :], in_=banks["sigmoid", h, t][:], func=ACT.Sigmoid)
+                nc.scalar.activation(out=sigmoid_first[:, t, :], in_=banks["sigmoid", t][:], func=ACT.Sigmoid)
 
-        def activate_tanh(d, sides=(0, 1)):
-            for side in sides:
-                run = tanh_values[d][:, side * 2 * QUARTER : (side + 1) * 2 * QUARTER]
+        def activate(branch, d):
+            for side in range(2):
+                run = values_of[branch, d][:, side * 2 * QUARTER : (side + 1) * 2 * QUARTER]
                 nc.scalar.activation(
                     out=run.rearrange("p (c e) -> p c e", e=2),
-                    in_=banks["tanh", d, side][:].rearrange("p e c -> p c e"),
-                    func=ACT.Tanh,
+                    in_=banks[branch, d, side][:].rearrange("p e c -> p c e"),
+                    func=ACT.Tanh if branch == "tanh" else ACT.Sigmoid,
                 )
 
-        def gain_sigmoid(i, lo, hi, engine, gain, run):
-            h, first = divmod(SPANS[i][0], HALF)
+        def gain_first(lo, hi, engine, gain, run):
             engine.tensor_tensor(
-                out=b_rounded[i][:, PACK * lo : PACK * hi].rearrange("p (c i t) -> p c t i", i=run, t=PACK),
-                in0=sigmoid_values[h][:, :, first + lo : first + hi].rearrange("p t (c i) -> p c t i", i=run),
+                out=b_rounded[0][:, PACK * lo : PACK * hi].rearrange("p (c i t) -> p c t i", i=run, t=PACK),
+                in0=sigmoid_first[:, :, lo:hi].rearrange("p t (c i) -> p c t i", i=run),
                 in1=gain.unsqueeze(1).unsqueeze(3).to_broadcast([P, (hi - lo) // run, PACK, run]),
                 op=MULT,
             )
 
-        def gain_tanh(d, lo, hi, engine, gain):
+        def gain_quarter(branch, d, lo, hi, engine, gain):
             i = max(d - 1, 0)
             first = d * QUARTER - SPANS[i][0]
-            order = "e s" if d == CROSSED else "s e"
-            rounded = a_rounded[i][:, PACK * first : PACK * (first + QUARTER)]
-            by_side = gain.rearrange("p (%s) -> p s e" % order, s=2, e=2)
+            rounded = (a_rounded if branch == "tanh" else b_rounded)[i][:, PACK * first : PACK * (first + QUARTER)]
+            by_side = gain.rearrange("p (s e) -> p s e", s=2, e=2)
             engine.tensor_tensor(
-                out=rounded.rearrange("p (c %s) -> p c s e" % order, s=2, e=2)[:, lo:hi, :, :],
-                in0=tanh_values[d][:].rearrange("p (s c e) -> p c s e", s=2, e=2)[:, lo:hi, :, :],
+                out=rounded.rearrange("p (c s e) -> p c s e", s=2, e=2)[:, lo:hi, :, :],
+                in0=values_of[branch, d][:].rearrange("p (s c e) -> p c s e", s=2, e=2)[:, lo:hi, :, :],
                 in1=by_side.unsqueeze(1).to_broadcast([P, hi - lo, 2, 2]),
                 op=MULT,
             )
 
         def gain_tanh_gpsimd(d):
-            gain_tanh(d, 0, TANH_SHARES[d], nc.gpsimd, gt_sb)
+            gain_quarter("tanh", d, 0, TANH_SHARES[d], nc.gpsimd, gt_sb)
 
         def gain_tanh_vector(d):
-            gain_tanh(d, TANH_SHARES[d], QUARTER, nc.vector, gt_psum)
+            gain_quarter("tanh", d, TANH_SHARES[d], QUARTER, nc.vector, gt_psum)
 
         def quantise_b(i):
             lo, hi = SPANS[i]
@@ -298,8 +305,10 @@ def tile_list_campaign_branch_bids_kernel(
         wt_plane = {}
         for a in range(PASSES):
             for side in range(2):
-                if (a, side) == (1, 0):
-                    wt_grouped[a, side] = placed([P, 2 * P * PACK], BF16, "wt_grouped_opens", AT_WT_ROUNDED_OPENS)
+                if (a, side) in AT_WT_ROUNDED:
+                    wt_grouped[a, side] = placed(
+                        [P, 2 * P * PACK], BF16, "wt_grouped%d_%d" % (a, side), AT_WT_ROUNDED[a, side]
+                    )
                 else:
                     wt_grouped[a, side] = held([P, 2 * P * PACK], BF16, "wt_grouped%d_%d" % (a, side))
                 if (a, side) in AT_WT_CODES_LATE:
@@ -376,13 +385,19 @@ def tile_list_campaign_branch_bids_kernel(
             nc.vector.tensor_tensor(out=bids[:], in0=values[i, n][:], in1=response[i, n][:], op=MULT)
             nc.sync.dma_start(out=out[P * n : P * (n + 1), lo:hi], in_=bids[:])
 
-        for h in range(HALVES):
-            for a in range(LAST):
-                sigmoid_pass(h, a)
-            gather_half(LAST, h)
-            sigmoid_pass(h, LAST)
-        for h in range(HALVES):
-            activate_sigmoid(h)
+        for a in range(LAST):
+            sigmoid_pass(a)
+        gather_half(LAST, 0)
+        sigmoid_pass(LAST)
+        ahead = ((2, 0), (2, 1), (3, 0))
+        for a in range(LAST):
+            for d, side in ahead:
+                quarter_pass("sigmoid", d, side, a)
+        gather_half(LAST, 1)
+        for d, side in ahead:
+            quarter_pass("sigmoid", d, side, LAST)
+        activate_first()
+        activate("sigmoid", 2)
         gain_bank = in_bank(GAIN_BANK, [P, P])
         nc.tensor.transpose(gain_bank[:], gains_transposed[:], identity)
         gs_psum = gain_bank[:, 0:PACK]
@@ -391,35 +406,30 @@ def tile_list_campaign_branch_bids_kernel(
             round_wt(0, side, nc.vector.tensor_copy)
         for side in range(2):
             quantise_wt(0, side)
-        round_wt(1, 0, nc.vector.tensor_copy)
-        round_wt(1, 1, nc.vector.tensor_copy, 0, WT_SPLIT)
-        quantise_wt(1, 0)
-        round_wt(1, 1, nc.scalar.copy, WT_SPLIT, P)
+        early = [(d, side) for d in range(QUARTERS) for side in range(2)][:5]
+        for d, side in early:
+            quarter_pass("tanh", d, side, 0)
+        for a in range(PASSES):
+            quarter_pass("sigmoid", 3, 1, a)
         for side in range(2):
-            round_wt(LAST, side, nc.scalar.copy)
-        gain_sigmoid(0, 0, SIGMOID_SHARE, nc.gpsimd, gs_sb, 1)
-        gain_sigmoid(0, SIGMOID_SHARE, HALF, nc.vector, gs_psum, 2)
-        gain_sigmoid(1, 0, QUARTER, nc.vector, gs_psum, 2)
+            round_wt(1, side, nc.scalar.copy)
+        round_wt(LAST, 1, nc.scalar.copy, WT_SPLIT, P)
+        gain_first(0, SIGMOID_SHARE, nc.gpsimd, gs_sb, 1)
+        gain_first(SIGMOID_SHARE, HALF, nc.vector, gs_psum, 2)
+        gain_quarter("sigmoid", 2, 0, QUARTER, nc.vector, gs_psum)
+        quantise_wt(1, 0)
+        round_wt(LAST, 0, nc.vector.tensor_copy)
+        round_wt(LAST, 1, nc.vector.tensor_copy, 0, WT_SPLIT)
         quantise_wt(1, 1)
+        activate("sigmoid", 3)
         quantise_wt(LAST, 0)
-        quantise_b(1)
         quantise_b(0)
         quantise_wt(LAST, 1)
-        for side in range(2):
-            for d in (0, 1):
-                tanh_pass(d, side, 0)
-        for side in range(2):
-            tanh_pass(CROSSED, side, 0)
-        for a in range(1, PASSES):
-            for d in (0, 1):
-                tanh_pass(d, 0, a)
-        for d in (0, 1):
-            for a in range(1, PASSES):
-                tanh_pass(d, 1, a)
-        for side in range(2):
-            for e in range(2):
-                for a in range(1, PASSES):
-                    tanh_pass(CROSSED, side, a, (e,))
+        quantise_b(1)
+        for d in range(QUARTERS):
+            for side in range(2):
+                for a in range(1 if (d, side) in early else 0, PASSES):
+                    quarter_pass("tanh", d, side, a)
         wq_grouped = placed([P, N * PACK], BF16, "wq_grouped", AT_WQ_ROUNDED)
         nc.gpsimd.tensor_scalar(
             out=wq_grouped[:].rearrange("p (c j) -> p c j", j=PACK),
@@ -429,30 +439,20 @@ def tile_list_campaign_branch_bids_kernel(
             op0=MULT,
             op1=ADD,
         )
-        gain_sigmoid(2, 0, QUARTER, nc.vector, gs_psum, 2)
-        activate_tanh(0)
-        activate_tanh(1)
-        for a in range(PASSES):
-            tanh_pass(3, 0, a)
-        activate_tanh(2)
-        activate_tanh(3, (0,))
-        gain_tanh_gpsimd(0)
+        gain_quarter("sigmoid", 3, 0, QUARTER, nc.vector, gs_psum)
+        for d in range(QUARTERS):
+            activate("tanh", d)
+        gain_tanh_gpsimd(1)
         gain_tanh_vector(0)
         gain_tanh_vector(1)
         nc.vector.quantize_mx(out=wq_codes[:].bitcast(FP8X4), scales=wq_plane[:], in_=wq_grouped[:])
         quantise_a(0)
         quantise_b(2)
-        respond(0, 0)
-        for a in range(PASSES):
-            tanh_pass(3, 1, a)
-        for n in range(1, SLOT_TILES):
-            respond(0, n)
-        copy_response(0, 0)
-        activate_tanh(3, (1,))
-        for n in range(1, SLOT_TILES):
-            copy_response(0, n)
         for n in range(SLOT_TILES):
+            respond(0, n)
             project(0, n)
+        for n in range(SLOT_TILES):
+            copy_response(0, n)
         for n in range(SLOT_TILES):
             respond(1, n)
         for i in (1, 2):

@@ -49,13 +49,12 @@ AT_WQ_CODES = 99
 AT_A_ROUNDED = 110
 AT_A_CODES = (101.5, 116, 114)
 AT_RESPONSE_LAST = 114
-SIGMOID_SHARE = 192
+SIGMOID_SHARE = 216
 TANH_SHARES = (0, 80, 112, 176)
-WT_SPLIT = P // 4
 
 GAINS_TRANSPOSED_BANK = 7
 GAIN_BANK = 0
-SIGMOID_BANKS = {2: (4, 5), 3: (6, 5)}
+SIGMOID_BANKS = ((0, 1), (2, 3), (4, 5), (6, 5))
 TANH_BANKS = ((7, 1), (2, 3), (4, 6), (2, 4))
 RESPONSE_BANKS = ((5, 7, 1), (4, 5, 7))
 VALUE_BANKS = ((3, 6, 2), (1, 3, 6), (2, 4, 5))
@@ -166,26 +165,20 @@ def tile_list_campaign_branch_bids_kernel(
 
         v_codes = {}
 
-        def gather_whole(a):
-            picked = held([P, S], U32, "picked%d" % a)
-            nc.vector.tensor_copy(picked[:], table[a][:].bitcast(U32).indirect(offsets[:]))
-            for h in range(HALVES):
-                v_codes[a, h] = picked[:, h * HALF : (h + 1) * HALF]
+        def gather(a, lo, hi):
+            picked = held([P, hi - lo], U32, "picked%d_%d" % (a, lo))
+            nc.vector.tensor_copy(picked[:], table[a][:].bitcast(U32).indirect(offsets[:, lo // 16 : hi // 16]))
+            for first in range(lo, hi, QUARTER):
+                v_codes[a, first // QUARTER] = picked[:, first - lo : first - lo + QUARTER]
 
-        def gather_half(a, h):
-            picked = held([P, HALF], U32, "picked%d_%d" % (a, h))
-            cols = HALF // 16
-            nc.vector.tensor_copy(picked[:], table[a][:].bitcast(U32).indirect(offsets[:, h * cols : (h + 1) * cols]))
-            v_codes[a, h] = picked[:]
-
-        gather_whole(0)
+        gather(0, 0, S)
         wt_raw = [placed([P, PACK, H], F32, "wt_raw%d" % a, AT_WT[a]) for a in range(PASSES)]
         for a in range(PASSES):
             rows = wt[a * P * PACK : (a + 1) * P * PACK, :]
             nc.sync.dma_start(out=wt_raw[a][:], in_=rows.rearrange("(p j) c -> p j c", j=PACK))
         wq_raw = placed([P, PACK, N], F32, "wq_raw", AT_WQ)
         nc.sync.dma_start(out=wq_raw[:], in_=wq.rearrange("(p j) c -> p j c", j=PACK))
-        gather_whole(1)
+        gather(1, 0, S)
         wp_codes = placed([P, N], I32, "wp_codes", AT_WP_CODES)
         nc.sync.dma_start(out=wp_codes[:], in_=wp_words[0].rearrange("p c i -> p (c i)").bitcast(I32))
         wp_plane = placed([P, N // 4], I32, "wp_plane", AT_WP_PLANE)
@@ -198,22 +191,7 @@ def tile_list_campaign_branch_bids_kernel(
 
         banks = {}
 
-        def sigmoid_pass(a):
-            for t in range(PACK):
-                if a == 0:
-                    banks["sigmoid", t] = in_bank(t, [P, HALF])
-                nc.tensor.matmul_mx(
-                    out=banks["sigmoid", t][:],
-                    lhsT=wg_codes[:, a, 2 * P * t : 2 * P * (t + 1)].bitcast(FP4X4),
-                    lhsT_scale=wg_plane[:, a, P * t : P * (t + 1)],
-                    rhs=v_codes[a, 0].bitcast(FP8X4),
-                    rhs_scale=v_planes[a][:, 0:HALF],
-                    start=(a == 0),
-                    stop=(a == LAST),
-                )
-
         def quarter_pass(branch, d, side, a):
-            h, lo = divmod(d * QUARTER, HALF)
             if a == 0:
                 numbers = TANH_BANKS if branch == "tanh" else SIGMOID_BANKS
                 banks[branch, d, side] = in_bank(numbers[d][side], [P, 2, QUARTER])
@@ -229,7 +207,7 @@ def tile_list_campaign_branch_bids_kernel(
                     out=banks[branch, d, side][:, e, :],
                     lhsT=codes,
                     lhsT_scale=plane,
-                    rhs=v_codes[a, h][:, lo : lo + QUARTER].bitcast(FP8X4),
+                    rhs=v_codes[a, d].bitcast(FP8X4),
                     rhs_scale=v_planes[a][:, d * QUARTER : (d + 1) * QUARTER],
                     start=(a == 0 and e == 0),
                     stop=(a == LAST and e == 1),
@@ -245,44 +223,33 @@ def tile_list_campaign_branch_bids_kernel(
         ]
         a_codes = [placed([P, hi - lo], U32, "a_codes%d" % i, AT_A_CODES[i]) for i, (lo, hi) in enumerate(SPANS)]
         a_plane = [held([P, hi - lo], U8, "a_plane%d" % i) for i, (lo, hi) in enumerate(SPANS)]
-        sigmoid_first = placed([P, PACK, HALF], F32, "sigmoid_first", AT_SIGMOID_FIRST)
         values_of = {
-            ("sigmoid", 2): held([P, width], F32, "sigmoid_values2"),
-            ("sigmoid", 3): placed([P, width], F32, "sigmoid_values3", AT_SIGMOID_LAST),
-            ("tanh", 0): placed([P, width], F32, "tanh_values0", AT_TANH_FIRST),
+            ("sigmoid", 0): placed([P, 2, HALF, 2], F32, "sigmoid_values0", AT_SIGMOID_FIRST),
+            ("sigmoid", 2): held([P, 2, QUARTER, 2], F32, "sigmoid_values2"),
+            ("sigmoid", 3): placed([P, 2, QUARTER, 2], F32, "sigmoid_values3", AT_SIGMOID_LAST),
+            ("tanh", 0): placed([P, 2, QUARTER, 2], F32, "tanh_values0", AT_TANH_FIRST),
         }
         for d in range(1, QUARTERS):
-            values_of["tanh", d] = held([P, width], F32, "tanh_values%d" % d)
-
-        def activate_first():
-            for t in range(PACK):
-                nc.scalar.activation(out=sigmoid_first[:, t, :], in_=banks["sigmoid", t][:], func=ACT.Sigmoid)
+            values_of["tanh", d] = held([P, 2, QUARTER, 2], F32, "tanh_values%d" % d)
 
         def activate(branch, d):
+            first = d if (branch, d) in values_of else d - 1
+            lo = (d - first) * QUARTER
             for side in range(2):
-                run = values_of[branch, d][:, side * 2 * QUARTER : (side + 1) * 2 * QUARTER]
                 nc.scalar.activation(
-                    out=run.rearrange("p (c e) -> p c e", e=2),
+                    out=values_of[branch, first][:, side, lo : lo + QUARTER, :],
                     in_=banks[branch, d, side][:].rearrange("p e c -> p c e"),
                     func=ACT.Tanh if branch == "tanh" else ACT.Sigmoid,
                 )
 
-        def gain_first(lo, hi, engine, gain, run):
-            engine.tensor_tensor(
-                out=b_rounded[0][:, PACK * lo : PACK * hi].rearrange("p (c i t) -> p c t i", i=run, t=PACK),
-                in0=sigmoid_first[:, :, lo:hi].rearrange("p t (c i) -> p c t i", i=run),
-                in1=gain.unsqueeze(1).unsqueeze(3).to_broadcast([P, (hi - lo) // run, PACK, run]),
-                op=MULT,
-            )
-
         def gain_quarter(branch, d, lo, hi, engine, gain):
             i = max(d - 1, 0)
             first = d * QUARTER - SPANS[i][0]
-            rounded = (a_rounded if branch == "tanh" else b_rounded)[i][:, PACK * first : PACK * (first + QUARTER)]
+            rounded = (a_rounded if branch == "tanh" else b_rounded)[i][:, PACK * (first + lo) : PACK * (first + hi)]
             by_side = gain.rearrange("p (s e) -> p s e", s=2, e=2)
             engine.tensor_tensor(
-                out=rounded.rearrange("p (c s e) -> p c s e", s=2, e=2)[:, lo:hi, :, :],
-                in0=values_of[branch, d][:].rearrange("p (s c e) -> p c s e", s=2, e=2)[:, lo:hi, :, :],
+                out=rounded.rearrange("p (c s e) -> p c s e", s=2, e=2),
+                in0=values_of[branch, d][:, :, lo:hi, :].rearrange("p s c e -> p c s e"),
                 in1=by_side.unsqueeze(1).to_broadcast([P, hi - lo, 2, 2]),
                 op=MULT,
             )
@@ -319,10 +286,10 @@ def tile_list_campaign_branch_bids_kernel(
                     wt_codes[a, side] = held([P, 2 * P], U32, "wt_codes%d_%d" % (a, side))
                 wt_plane[a, side] = held([P, 2 * P], U8, "wt_plane%d_%d" % (a, side))
 
-        def round_wt(a, side, copy, lo=0, hi=P):
+        def round_wt(a, side, copy):
             dst = wt_grouped[a, side][:].rearrange("p (e m j) -> p m j e", e=2, j=PACK)
             src = wt_raw[a][:].rearrange("p j (m t) -> p m j t", t=PACK)
-            copy(out=dst[:, lo:hi, :, :], in_=src[:, lo:hi, :, 2 * side : 2 * side + 2])
+            copy(out=dst, in_=src[:, :, :, 2 * side : 2 * side + 2])
 
         def quantise_wt(a, side):
             nc.vector.quantize_mx(
@@ -385,19 +352,22 @@ def tile_list_campaign_branch_bids_kernel(
             nc.vector.tensor_tensor(out=bids[:], in0=values[i, n][:], in1=response[i, n][:], op=MULT)
             nc.sync.dma_start(out=out[P * n : P * (n + 1), lo:hi], in_=bids[:])
 
-        for a in range(LAST):
-            sigmoid_pass(a)
-        gather_half(LAST, 0)
-        sigmoid_pass(LAST)
+        for d in (0, 1):
+            for a in range(LAST):
+                for side in range(2):
+                    quarter_pass("sigmoid", d, side, a)
+            gather(LAST, d * QUARTER, (d + 1) * QUARTER)
+            for side in range(2):
+                quarter_pass("sigmoid", d, side, LAST)
         ahead = ((2, 0), (2, 1), (3, 0))
         for a in range(LAST):
             for d, side in ahead:
                 quarter_pass("sigmoid", d, side, a)
-        gather_half(LAST, 1)
+        gather(LAST, HALF, S)
         for d, side in ahead:
             quarter_pass("sigmoid", d, side, LAST)
-        activate_first()
-        activate("sigmoid", 2)
+        for d in range(QUARTERS - 1):
+            activate("sigmoid", d)
         gain_bank = in_bank(GAIN_BANK, [P, P])
         nc.tensor.transpose(gain_bank[:], gains_transposed[:], identity)
         gs_psum = gain_bank[:, 0:PACK]
@@ -413,13 +383,12 @@ def tile_list_campaign_branch_bids_kernel(
             quarter_pass("sigmoid", 3, 1, a)
         for side in range(2):
             round_wt(1, side, nc.scalar.copy)
-        round_wt(LAST, 1, nc.scalar.copy, WT_SPLIT, P)
-        gain_first(0, SIGMOID_SHARE, nc.gpsimd, gs_sb, 1)
-        gain_first(SIGMOID_SHARE, HALF, nc.vector, gs_psum, 2)
+        round_wt(LAST, 1, nc.scalar.copy)
+        gain_quarter("sigmoid", 0, 0, SIGMOID_SHARE, nc.gpsimd, gs_sb)
+        gain_quarter("sigmoid", 0, SIGMOID_SHARE, HALF, nc.vector, gs_psum)
         gain_quarter("sigmoid", 2, 0, QUARTER, nc.vector, gs_psum)
         quantise_wt(1, 0)
         round_wt(LAST, 0, nc.vector.tensor_copy)
-        round_wt(LAST, 1, nc.vector.tensor_copy, 0, WT_SPLIT)
         quantise_wt(1, 1)
         activate("sigmoid", 3)
         quantise_wt(LAST, 0)

from contextlib import ExitStack

import concourse.mybir as mybir
from concourse.masks import make_identity

K, T, S, H, N = 1536, 4096, 1024, 512, 384
FLOPS = 2 * 2 * K * H * S + 2 * 2 * H * N * S

F32 = mybir.dt.float32
BF16 = mybir.dt.bfloat16
I32 = mybir.dt.int32
U32 = mybir.dt.uint32
U16 = mybir.dt.uint16
U8 = mybir.dt.uint8
FP8X4 = mybir.dt.float8_e4m3fn_x4
FP4X4 = mybir.dt.float4_e2m1fn_x4
ACT = mybir.ActivationFunctionType
MULT = mybir.AluOpType.mult
ADD = mybir.AluOpType.add

P = 128
PACK = 4
PASSES = K // (P * PACK)
LAST = PASSES - 1
HALF = 512
HALVES = S // HALF
QUARTER = HALF // 2
QUARTERS = S // QUARTER
SLOT_TILES = N // P
SPANS = ((0, HALF), (HALF, HALF + QUARTER), (HALF + QUARTER, S))

AT_SCALE_WINDOW = 15
AT_TABLE = (58, 0, 18)
AT_IDENTITY = 17
AT_GAINS_PADDED = 17.5
AT_WT = (51, 59, 73)
AT_WQ = 67
AT_WP_CODES = 0
AT_WP_PLANE = 2
AT_WT_ROUNDED = {(0, 0): 84, (1, 1): 36, (2, 0): 90, (2, 1): 42}
AT_SIGMOID_FIRST = 90
AT_SIGMOID_LAST = 37.5
AT_WT_CODES_LATE = {(1, 0): 96, (1, 1): 97}
AT_B_ROUNDED_FIRST = 84
AT_B_CODES = (34.5, 36.5, 100.5)
AT_WQ_ROUNDED = 42
AT_TANH_FIRST = 100
AT_WQ_CODES = 99
AT_A_ROUNDED = 110
AT_A_CODES = (101.5, 116, 114)
AT_RESPONSE_LAST = 114
SIGMOID_SHARE = 216
TANH_SHARES = (0, 80, 112, 176)

GAINS_TRANSPOSED_BANK = 7
GAIN_BANK = 0
SIGMOID_BANKS = ((0, 1), (2, 3), (4, 5), (6, 5))
TANH_BANKS = ((7, 1), (2, 3), (4, 6), (2, 4))
RESPONSE_BANKS = ((5, 7, 1), (4, 5, 7))
VALUE_BANKS = ((3, 6, 2), (1, 3, 6), (2, 4, 5))

SCALE_ROW_LOADS = ((0, 16, 48), (16, 32, 96))
SCALE_WINDOW_GAPS = ((0, 48), (64, 96))
QUADRANT_ORDER = (0, 2, 1, 3)


def scale_row_partition(row):
    return [at + row - first for first, count, at in SCALE_ROW_LOADS if first <= row < first + count][0]


def tile_list_campaign_branch_bids_kernel(
    tc, tab_words, tab_scales, offs, wt, wg_words, wg_scales, gt, gs, wp_words, wp_scales, wq, out
):
    nc = tc.nc
    with ExitStack() as ctx:
        keep = ctx.enter_context(tc.tile_pool(name="keep", bufs=1))
        rooms = ctx.enter_context(tc.tile_pool(name="rooms", bufs=1))
        psum = ctx.enter_context(tc.psum_pool(name="psum", bufs=1))

        def held(shape, dtype, name):
            return keep.tile(shape, dtype, name=name, tag=name, align_bytes=256)

        def placed(shape, dtype, name, kib):
            return rooms.tile(shape, dtype, name=name, align_bytes=256, offset=int(kib * 1024))

        def in_bank(number, shape):
            return psum.tile(shape, F32, name="bank%d" % number, tag="bank%d" % number)

        offsets = keep.tile([P, S // 16], U16, name="offsets")
        table = {}
        table_scales = placed([P, T // 4], I32, "table_scales", AT_SCALE_WINDOW)
        wg_raw = held([P, PASSES, H // 2], I32, "wg_raw")
        wg_scales_raw = held([P, PASSES, H // 4], I32, "wg_scales_raw")
        v_plane_words = held([P, PASSES, S // 4], I32, "v_plane_words")

        nc.vector.memset(wg_scales_raw[:], 0)
        for lo, hi in SCALE_WINDOW_GAPS:
            nc.vector.memset(table_scales[lo:hi, :], 0)
        nc.vector.memset(v_plane_words[:], 0)

        def load_table(a):
            table[a] = placed([P, T], I32, "table%d" % a, AT_TABLE[a])
            nc.sync.dma_start(out=table[a][:], in_=tab_words[a].rearrange("p t i -> p (t i)").bitcast(I32))

        nc.sync.dma_start(offsets[:], offs)
        scale_rows = tab_scales.rearrange("a q t -> (a q) t").bitcast(I32)
        for first, count, at in SCALE_ROW_LOADS:
            nc.sync.dma_start(out=table_scales[at : at + count, :], in_=scale_rows[first : first + count, :])
        nc.sync.dma_start(out=wg_raw[:], in_=wg_words.rearrange("a p c -> p a c").bitcast(I32))
        gains = held([P, 2, 2 * PACK], F32, "gains")
        gs_sb = gains[:, 0, 0:PACK]
        gt_sb = gains[:, 1, 0:PACK]
        nc.sync.dma_start(out=gs_sb, in_=gs.rearrange("(p t) -> p t", t=PACK))
        nc.sync.dma_start(out=gt_sb, in_=gt.rearrange("(p t) -> p t", t=PACK))
        load_table(0)
        for q in QUADRANT_ORDER:
            nc.sync.dma_start(
                out=wg_scales_raw[32 * q : 32 * q + 4, :, :],
                in_=wg_scales[:, 4 * q : 4 * q + 4, :].rearrange("a r c -> r a c").bitcast(I32),
            )

        picked_scales = held([P, S], U8, "picked_scales")
        nc.vector.tensor_copy(picked_scales[:], table_scales[:].bitcast(U8).indirect(offsets[:]))

        def move_scale_rows(a, q):
            at = scale_row_partition(16 * a + 4 * q)
            nc.sync.dma_start(
                out=v_plane_words[32 * q : 32 * q + 4, a, :],
                in_=picked_scales[at : at + 4, :].bitcast(I32),
            )

        moves = [(a, q) for a in range(PASSES) for q in QUADRANT_ORDER]
        for a, q in moves[:2]:
            move_scale_rows(a, q)
        load_table(1)
        for a, q in moves[2:8]:
            move_scale_rows(a, q)
        load_table(2)
        for a, q in moves[8:]:
            move_scale_rows(a, q)

        identity = placed([P, P], F32, "identity", AT_IDENTITY)[:]
        gains_padded = placed([P, P], F32, "gains_padded", AT_GAINS_PADDED)[:]
        make_identity(nc, identity)
        nc.vector.memset(gains_padded, 0.0)
        nc.vector.tensor_copy(
            out=gains_padded[:, 0 : 2 * PACK].rearrange("p (b t) -> p b t", t=PACK), in_=gains[:, :, 0:PACK]
        )
        gains_transposed = held([P, P], F32, "gains_transposed")
        transposed_bank = in_bank(GAINS_TRANSPOSED_BANK, [P, P])
        nc.tensor.transpose(transposed_bank[:], gains_padded, identity)
        nc.vector.tensor_copy(out=gains_transposed[:], in_=transposed_bank[:])
        v_planes = [v_plane_words[:, a, :].bitcast(U8) for a in range(PASSES)]

        wg_codes = held([P, PASSES, 2 * H], U8, "wg_codes")
        wg_plane = held([P, PASSES, H], U8, "wg_plane")
        nc.vector.tensor_copy(
            out=wg_codes[:].bitcast(U16).rearrange("p a (t m) -> p a t m", t=PACK),
            in_=wg_raw[:].bitcast(U16).rearrange("p a (m t) -> p a t m", t=PACK),
        )
        nc.vector.tensor_copy(
            out=wg_plane[:].rearrange("p a (t m) -> p a t m", t=PACK),
            in_=wg_scales_raw[:].bitcast(U8).rearrange("p a (m t) -> p a t m", t=PACK),
        )

        v_codes = {}

        def gather(a, lo, hi):
            picked = held([P, hi - lo], U32, "picked%d_%d" % (a, lo))
            nc.vector.tensor_copy(picked[:], table[a][:].bitcast(U32).indirect(offsets[:, lo // 16 : hi // 16]))
            for first in range(lo, hi, QUARTER):
                v_codes[a, first // QUARTER] = picked[:, first - lo : first - lo + QUARTER]

        gather(0, 0, S)
        wt_raw = [placed([P, PACK, H], F32, "wt_raw%d" % a, AT_WT[a]) for a in range(PASSES)]
        for a in range(PASSES):
            rows = wt[a * P * PACK : (a + 1) * P * PACK, :]
            nc.sync.dma_start(out=wt_raw[a][:], in_=rows.rearrange("(p j) c -> p j c", j=PACK))
        wq_raw = placed([P, PACK, N], F32, "wq_raw", AT_WQ)
        nc.sync.dma_start(out=wq_raw[:], in_=wq.rearrange("(p j) c -> p j c", j=PACK))
        gather(1, 0, S)
        wp_codes = placed([P, N], I32, "wp_codes", AT_WP_CODES)
        nc.sync.dma_start(out=wp_codes[:], in_=wp_words[0].rearrange("p c i -> p (c i)").bitcast(I32))
        wp_plane = placed([P, N // 4], I32, "wp_plane", AT_WP_PLANE)
        nc.vector.memset(wp_plane[:], 0)
        for q in QUADRANT_ORDER:
            nc.sync.dma_start(
                out=wp_plane[32 * q : 32 * q + 4, :],
                in_=wp_scales[0, 4 * q : 4 * q + 4, :].bitcast(I32),
            )

        banks = {}

        def quarter_pass(branch, d, side, a):
            if a == 0:
                numbers = TANH_BANKS if branch == "tanh" else SIGMOID_BANKS
                banks[branch, d, side] = in_bank(numbers[d][side], [P, 2, QUARTER])
            for e in range(2):
                t = 2 * side + e
                if branch == "tanh":
                    codes = wt_codes[a, side][:, P * e : P * (e + 1)].bitcast(FP8X4)
                    plane = wt_plane[a, side][:, P * e : P * (e + 1)]
                else:
                    codes = wg_codes[:, a, 2 * P * t : 2 * P * (t + 1)].bitcast(FP4X4)
                    plane = wg_plane[:, a, P * t : P * (t + 1)]
                nc.tensor.matmul_mx(
                    out=banks[branch, d, side][:, e, :],
                    lhsT=codes,
                    lhsT_scale=plane,
                    rhs=v_codes[a, d].bitcast(FP8X4),
                    rhs_scale=v_planes[a][:, d * QUARTER : (d + 1) * QUARTER],
                    start=(a == 0 and e == 0),
                    stop=(a == LAST and e == 1),
                )

        width = QUARTER * PACK
        b_rounded = [placed([P, HALF * PACK], BF16, "b_rounded0", AT_B_ROUNDED_FIRST)]
        b_rounded.extend(held([P, width], BF16, "b_rounded%d" % i) for i in (1, 2))
        b_codes = [placed([P, hi - lo], U32, "b_codes%d" % i, AT_B_CODES[i]) for i, (lo, hi) in enumerate(SPANS)]
        b_plane = held([P, S], U8, "b_plane")
        a_rounded = [
            placed([P, (hi - lo) * PACK], BF16, "a_rounded%d" % i, AT_A_ROUNDED) for i, (lo, hi) in enumerate(SPANS)
        ]
        a_codes = [placed([P, hi - lo], U32, "a_codes%d" % i, AT_A_CODES[i]) for i, (lo, hi) in enumerate(SPANS)]
        a_plane = [held([P, hi - lo], U8, "a_plane%d" % i) for i, (lo, hi) in enumerate(SPANS)]
        values_of = {
            ("sigmoid", 0): placed([P, 2, HALF, 2], F32, "sigmoid_values0", AT_SIGMOID_FIRST),
            ("sigmoid", 2): held([P, 2, QUARTER, 2], F32, "sigmoid_values2"),
            ("sigmoid", 3): placed([P, 2, QUARTER, 2], F32, "sigmoid_values3", AT_SIGMOID_LAST),
            ("tanh", 0): placed([P, 2, QUARTER, 2], F32, "tanh_values0", AT_TANH_FIRST),
        }
        for d in range(1, QUARTERS):
            values_of["tanh", d] = held([P, 2, QUARTER, 2], F32, "tanh_values%d" % d)

        def activate(branch, d):
            first = d if (branch, d) in values_of else d - 1
            lo = (d - first) * QUARTER
            for side in range(2):
                nc.scalar.activation(
                    out=values_of[branch, first][:, side, lo : lo + QUARTER, :],
                    in_=banks[branch, d, side][:].rearrange("p e c -> p c e"),
                    func=ACT.Tanh if branch == "tanh" else ACT.Sigmoid,
                )

        def gain_quarter(branch, d, lo, hi, engine, gain):
            i = max(d - 1, 0)
            first = d * QUARTER - SPANS[i][0]
            rounded = (a_rounded if branch == "tanh" else b_rounded)[i][:, PACK * (first + lo) : PACK * (first + hi)]
            by_side = gain.rearrange("p (s e) -> p s e", s=2, e=2)
            engine.tensor_tensor(
                out=rounded.rearrange("p (c s e) -> p c s e", s=2, e=2),
                in0=values_of[branch, d][:, :, lo:hi, :].rearrange("p s c e -> p c s e"),
                in1=by_side.unsqueeze(1).to_broadcast([P, hi - lo, 2, 2]),
                op=MULT,
            )

        def gain_tanh_gpsimd(d):
            gain_quarter("tanh", d, 0, TANH_SHARES[d], nc.gpsimd, gt_sb)

        def gain_tanh_vector(d):
            gain_quarter("tanh", d, TANH_SHARES[d], QUARTER, nc.vector, gt_psum)

        def quantise_b(i):
            lo, hi = SPANS[i]
            nc.vector.quantize_mx(out=b_codes[i][:].bitcast(FP8X4), scales=b_plane[:, lo:hi], in_=b_rounded[i][:])

        def quantise_a(i):
            nc.vector.quantize_mx(out=a_codes[i][:].bitcast(FP8X4), scales=a_plane[i][:], in_=a_rounded[i][:])

        wt_grouped = {}
        wt_codes = {}
        wt_plane = {}
        for a in range(PASSES):
            for side in range(2):
                if (a, side) in AT_WT_ROUNDED:
                    wt_grouped[a, side] = placed(
                        [P, 2 * P * PACK], BF16, "wt_grouped%d_%d" % (a, side), AT_WT_ROUNDED[a, side]
                    )
                else:
                    wt_grouped[a, side] = held([P, 2 * P * PACK], BF16, "wt_grouped%d_%d" % (a, side))
                if (a, side) in AT_WT_CODES_LATE:
                    wt_codes[a, side] = placed(
                        [P, 2 * P], U32, "wt_codes%d_%d" % (a, side), AT_WT_CODES_LATE[a, side]
                    )
                else:
                    wt_codes[a, side] = held([P, 2 * P], U32, "wt_codes%d_%d" % (a, side))
                wt_plane[a, side] = held([P, 2 * P], U8, "wt_plane%d_%d" % (a, side))

        def round_wt(a, side, copy):
            dst = wt_grouped[a, side][:].rearrange("p (e m j) -> p m j e", e=2, j=PACK)
            src = wt_raw[a][:].rearrange("p j (m t) -> p m j t", t=PACK)
            copy(out=dst, in_=src[:, :, :, 2 * side : 2 * side + 2])

        def quantise_wt(a, side):
            nc.vector.quantize_mx(
                out=wt_codes[a, side][:].bitcast(FP8X4), scales=wt_plane[a, side][:], in_=wt_grouped[a, side][:]
            )

        wq_codes = placed([P, N], U32, "wq_codes", AT_WQ_CODES)
        wq_plane = held([P, N], U8, "wq_plane")

        response = {}

        for i, (lo, hi) in enumerate(SPANS):
            for n in range(SLOT_TILES):
                if (i, n) == (0, SLOT_TILES - 1):
                    response[i, n] = placed([P, hi - lo], F32, "response_last", AT_RESPONSE_LAST)
                else:
                    response[i, n] = held([P, hi - lo], F32, "response%d_%d" % (i, n))

        response_banks = {}

        def respond(h, n):
            cols = slice(P * n, P * (n + 1))
            response_banks[h, n] = in_bank(RESPONSE_BANKS[h][n], [P, HALF])
            for i, (lo, hi) in enumerate(SPANS):
                if lo // HALF == h:
                    nc.tensor.matmul_mx(
                        out=response_banks[h, n][:, lo - h * HALF : hi - h * HALF],
                        lhsT=wq_codes[:, cols].bitcast(FP8X4),
                        lhsT_scale=wq_plane[:, cols],
                        rhs=b_codes[i][:].bitcast(FP8X4),
                        rhs_scale=b_plane[:, lo:hi],
                        start=True,
                        stop=True,
                    )

        def copy_response(i, n):
            lo, hi = SPANS[i]
            h = lo // HALF
            nc.scalar.copy(out=response[i, n][:], in_=response_banks[h, n][:, lo - h * HALF : hi - h * HALF])

        values = {}

        def project(i, n):
            lo, hi = SPANS[i]
            cols = slice(P * n, P * (n + 1))
            values[i, n] = in_bank(VALUE_BANKS[i][n], [P, hi - lo])
            nc.tensor.matmul_mx(
                out=values[i, n][:],
                lhsT=wp_codes[:, cols].bitcast(FP8X4),
                lhsT_scale=wp_plane[:].bitcast(U8)[:, cols],
                rhs=a_codes[i][:].bitcast(FP8X4),
                rhs_scale=a_plane[i][:],
                start=True,
                stop=True,
            )

        def bid(i, n):
            lo, hi = SPANS[i]
            bids = held([P, hi - lo], F32, "bids%d_%d" % (i, n))
            nc.vector.tensor_tensor(out=bids[:], in0=values[i, n][:], in1=response[i, n][:], op=MULT)
            nc.sync.dma_start(out=out[P * n : P * (n + 1), lo:hi], in_=bids[:])

        for d in (0, 1):
            for a in range(LAST):
                for side in range(2):
                    quarter_pass("sigmoid", d, side, a)
            gather(LAST, d * QUARTER, (d + 1) * QUARTER)
            for side in range(2):
                quarter_pass("sigmoid", d, side, LAST)
        ahead = ((2, 0), (2, 1), (3, 0))
        for a in range(LAST):
            for d, side in ahead:
                quarter_pass("sigmoid", d, side, a)
        gather(LAST, HALF, S)
        for d, side in ahead:
            quarter_pass("sigmoid", d, side, LAST)
        for d in range(QUARTERS - 1):
            activate("sigmoid", d)
        gain_bank = in_bank(GAIN_BANK, [P, P])
        nc.tensor.transpose(gain_bank[:], gains_transposed[:], identity)
        gs_psum = gain_bank[:, 0:PACK]
        gt_psum = gain_bank[:, PACK : 2 * PACK]
        for side in range(2):
            round_wt(0, side, nc.vector.tensor_copy)
        for side in range(2):
            quantise_wt(0, side)
        early = [(d, side) for d in range(QUARTERS) for side in range(2)][:5]
        for d, side in early:
            quarter_pass("tanh", d, side, 0)
        for a in range(PASSES):
            quarter_pass("sigmoid", 3, 1, a)
        for side in range(2):
            round_wt(1, side, nc.scalar.copy)
        round_wt(LAST, 1, nc.scalar.copy)
        gain_quarter("sigmoid", 0, 0, SIGMOID_SHARE, nc.gpsimd, gs_sb)
        gain_quarter("sigmoid", 0, SIGMOID_SHARE, HALF, nc.vector, gs_psum)
        gain_quarter("sigmoid", 2, 0, QUARTER, nc.vector, gs_psum)
        quantise_wt(1, 0)
        round_wt(LAST, 0, nc.vector.tensor_copy)
        quantise_wt(1, 1)
        activate("sigmoid", 3)
        quantise_wt(LAST, 0)
        quantise_b(0)
        quantise_wt(LAST, 1)
        quantise_b(1)
        for d in range(QUARTERS):
            for side in range(2):
                for a in range(1 if (d, side) in early else 0, PASSES):
                    quarter_pass("tanh", d, side, a)
        wq_grouped = placed([P, N * PACK], BF16, "wq_grouped", AT_WQ_ROUNDED)
        nc.gpsimd.tensor_scalar(
            out=wq_grouped[:].rearrange("p (c j) -> p c j", j=PACK),
            in0=wq_raw[:].rearrange("p j c -> p c j"),
            scalar1=1.0,
            scalar2=0.0,
            op0=MULT,
            op1=ADD,
        )
        gain_quarter("sigmoid", 3, 0, QUARTER, nc.vector, gs_psum)
        for d in range(QUARTERS):
            activate("tanh", d)
        gain_tanh_gpsimd(1)
        gain_tanh_vector(0)
        gain_tanh_vector(1)
        nc.vector.quantize_mx(out=wq_codes[:].bitcast(FP8X4), scales=wq_plane[:], in_=wq_grouped[:])
        quantise_a(0)
        quantise_b(2)
        for n in range(SLOT_TILES):
            respond(0, n)
            project(0, n)
        for n in range(SLOT_TILES):
            copy_response(0, n)
        for n in range(SLOT_TILES):
            respond(1, n)
        for i in (1, 2):
            for n in range(SLOT_TILES):
                copy_response(i, n)
        gain_tanh_gpsimd(2)
        gain_tanh_vector(2)
        bid(0, 0)
        quantise_a(1)
        gain_tanh_gpsimd(3)
        bid(0, 1)
        gain_tanh_vector(3)
        bid(0, 2)
        for n in range(SLOT_TILES):
            project(1, n)
        bid(1, 0)
        quantise_a(2)
        for n in range(SLOT_TILES):
            project(2, n)
        bid(1, 1)
        bid(1, 2)
        for n in range(SLOT_TILES):
            bid(2, n)
